import numpy as np, ml_dtypes
CORES = [10,34,74,98]
N = 4
BF = ml_dtypes.bfloat16
def gentries(a):
    return np.ascontiguousarray(a.reshape(8, 16, -1).transpose(0, 2, 1)).reshape(8, -1)
def gtable(e):
    e = np.asarray(e); return np.ascontiguousarray(e.reshape(8, -1, 16).transpose(0, 2, 1)).reshape(128, -1).astype(np.int32)
W, B, E, SH, L, H = 4096, 64, 64, 6, 6, 1
R = L * B
def parts(rng):
    Y = rng.integers(0, 256, (N, 8, 16, W)); X = rng.integers(0, 256, (N, 8, 16, R)); m = rng.integers(0, W, (N, 8, R))
    lev = np.arange(B, R) // B; h = []
    for k in range(2):
        at = np.where(rng.random((N, 8, R - B)) < 0.5, 0, (lev * rng.random((N, 8, R - B))).astype(np.int64))
        h.append(rng.integers(0, H + 1, (N, 8, R - B)) * R + at * B + rng.integers(0, B, (N, 8, R - B)))
    a, b = rng.integers(0, W, (N, 8, B)), rng.integers(0, W, (N, 8, B)); far = rng.random((N, 8, B)) < 0.7
    lo = np.where(far, rng.integers(0, W // 4, (N, 8, B)), np.minimum(a, b)); hi = np.where(far, rng.integers(3 * W // 4, W, (N, 8, B)), np.maximum(a, b))
    return Y, X, h[0], h[1], m, lo, hi
def pack(Y, X, a, b, m, lo, hi):
    return {"ytab": np.ascontiguousarray(Y.reshape(N, 128, W)).astype(np.float32).astype(BF), "xrow": np.ascontiguousarray(X.reshape(N, 128, R)).astype(np.float32).astype(BF),
            "ha": np.stack([gtable(v) for v in a]), "hb": np.stack([gtable(v) for v in b]), "home": np.stack([gtable(v) for v in m]), "lo0": np.stack([gtable(v) for v in lo]), "hi0": np.stack([gtable(v) for v in hi])}
def setup_inputs(rng):
    return pack(*parts(rng))
def setup_inputs_ties(rng):
    Y, X, a, b, m, lo, hi = parts(rng)
    Y = np.take_along_axis(rng.integers(0, 256, (N, 8, 16, 4)), rng.integers(0, 4, (N, 8, 1, W)), 3)
    Y[:, 0] = Y[:, 0, :, :1]
    hi = np.where(rng.random(hi.shape) < 0.2, np.minimum(lo + rng.integers(0, E, hi.shape), W - 1), hi)
    m[:, :, :B] = (lo + hi) >> 1
    return pack(Y, X, a, b, m, lo, hi)
def setup_inputs_narrow(rng):
    Y, X, a, b, m, lo, hi = parts(rng)
    lo = rng.integers(0, W - 1, lo.shape); lo[:, :4] = rng.integers(0, W - 1024, (1, 4, 1)) + rng.integers(0, 40, (N, 4, B))
    hi = np.minimum(lo + rng.choice(np.array([0, 1, 2, E - 1, E, E + 1, 2 * E + 1, 300]), lo.shape), W - 1)
    for k, (p, q) in enumerate(((0, 0), (W - 1, W - 1), (0, W - 1), (W - 2, W - 1), (0, 1))): lo[:, 3:, k] = p; hi[:, 3:, k] = q
    t = rng.random((N, 5, R - B)) < 0.2
    a[:, 3:] = np.where(t, 1, a[:, 3:]); b[:, 3:] = np.where(t, H * R, b[:, 3:])
    lo[:, 7] = (E * np.arange(B)) % W; hi[:, 7] = np.minimum(lo[:, 7] + E, W - 1)
    o = np.arange(R - B); a[:, 7] = o; b[:, 7] = o + (o % B < B - 1)
    return pack(Y, X, a, b, m, lo, hi)
def setup_inputs_alike(rng):
    Y, X, a, b, m, lo, hi = parts(rng); lev = np.arange(B, R) // B
    v = a.reshape(N, 8, L - 1, B); a = np.where((np.arange(8) % 2 == 0)[None, :, None, None], v[..., :1], v).reshape(N, 8, R - B)
    a[:, 4] = rng.integers(0, H + 1, (N, 1)) * R + rng.integers(0, B, (N, 1))
    b[:, 1] = np.where(rng.random((N, R - B)) < 0.5, a[:, 1], b[:, 1]); b[:, 2] = a[:, 2]
    a[:, 3] = a[:, 3] % R; b[:, 3] = b[:, 3] % R
    a[:, 5] = a[:, 5] % R + H * R; b[:, 5] = b[:, 5] % R + H * R
    for w in (a, b): w[:, 7] = rng.integers(0, H + 1, (N, R - B)) * R + np.where(rng.random((N, R - B)) < 0.5, 0, B * lev - 1)
    return pack(Y, X, a, b, m, lo, hi)
def setup_inputs_far(rng):
    Y, X, a, b, m, lo, hi = parts(rng)
    Y = 255 * rng.integers(0, 2, Y.shape); X = 255 * rng.integers(0, 2, (N, 8, 1, R)) + np.zeros((1, 1, 16, 1), np.int64); m = (W - 1) * rng.integers(0, 2, m.shape)
    Y[:, 0] = 255; X[:, 0] = 0; Y[:, 1] = 0; X[:, 1] = 255; lo[:, :, :8] = 0; m[:, :, :4] = W - 1; m[:, :, 4:8] = 0
    for i, p, q, c in ((8, W - 1, W - 1, 0), (12, W - 16, W - 1, 0), (16, 0, 31, W - 1), (20, 1, 15, W - 1)): lo[:, :2, i:i + 4] = p; hi[:, :2, i:i + 4] = q; m[:, :2, i:i + 4] = c
    a[:, 1, ::B] = 8; b[:, 1, ::B] = H * R + 9
    Y[:, 2] = rng.integers(0, 2, (N, 16, W)); X[:, 2] = 255; hi[:, 2] = np.minimum(lo[:, 2] + 2 * E, W - 1)
    return pack(Y, X, a, b, m, lo, hi)
def setup_inputs_spread(rng):
    Y, X, a, b, m, lo, hi = parts(rng); lev = np.arange(B, R) // B
    Y = (np.exp2(rng.integers(1, 9, (N, 8, 1, W))) * rng.random(Y.shape)).astype(np.int64); X = (np.exp2(rng.integers(1, 9, (N, 8, 1, R))) * rng.random(X.shape)).astype(np.int64)
    a = (a // R) * R + (B * lev * rng.random(a.shape) ** 3).astype(np.int64); m = (W * rng.random(m.shape) ** 2).astype(np.int64)
    return pack(Y, X, a, b, m, lo, hi)
def check_inputs(d):
    bad = []
    for k in ("ytab", "xrow"):
        v = np.asarray(d[k]).astype(np.float32)
        if not np.all((v >= 0) & (v <= 255) & (v == np.floor(v))): bad.append("whole numbers of " + k)
    for k in ("home", "lo0", "hi0"):
        if np.min(d[k]) < 0 or np.max(d[k]) >= W: bad.append("range of " + k)
    if np.any(d["lo0"] > d["hi0"]): bad.append("lo0 over hi0")
    lev = np.arange(B, R) // B
    for k in ("ha", "hb"):
        h = np.stack([gentries(v) for v in d[k]]).astype(np.int64)
        if np.min(h) < 0 or np.max(h) >= (H + 1) * R or np.any(h % R >= B * lev): bad.append("rows that " + k + " names")
    return bad
def reference(ytab, xrow, ha, hb, home, lo0, hi0):
    Y = ytab.astype(np.float32).astype(np.int32).reshape(N, 8, 16, W); X = xrow.astype(np.float32).astype(np.int32).reshape(N, 8, 16, R)
    a, b, m, first, last = [np.stack([gentries(v) for v in t]).astype(np.int64) for t in (ha, hb, home, lo0, hi0)]
    e = np.arange(E); wins = []
    for ps in range(2):
        arg = np.zeros((N, 8, R), np.int64)
        for l in range(L):
            s = l * B
            if l == 0: lo, hi = first, last
            else:
                known = np.concatenate([np.roll(arg, -k, axis=0) for k in range(H + 1)], axis=2)
                u = np.take_along_axis(known, a[:, :, s - B:s], 2); v = np.take_along_axis(known, b[:, :, s - B:s], 2)
                lo, hi = np.minimum(u, v), np.maximum(u, v)
            j = lo[..., None] + (((hi - lo)[..., None] * e) >> SH)
            y = np.take_along_axis(Y, j.reshape(N, 8, 1, B * E), 3).reshape(N, 8, 16, B, E)
            cost = np.add.reduce(np.abs(X[..., s:s + B, None] - y), axis=2) + (np.abs(j - m[:, :, s:s + B, None]) >> 4)
            k = np.argmin(cost, axis=3)
            arg[:, :, s:s + B] = np.take_along_axis(j, k[..., None], 3)[..., 0]
        X = np.abs(X - np.take_along_axis(Y, arg[:, :, None, :], 3))
        wins.append(arg)
    both = np.concatenate(wins, axis=2)
    return {"argm": np.stack([gtable(v) for v in both]).astype(np.float32), "xo": X.reshape(N, 128, R).astype(np.float32)}

@@ -1,0 +1,426 @@
+import numpy as np
+from concourse.mybir import AluOpType, AxisListType, ActivationFunctionType
+
+A = AluOpType
+F = ActivationFunctionType
+L, R, NI = 6, 384, 4096
+BIG = float(2 ** 22)
+CJ = 2048.0 - 63.0 / 128.0
+SBL = [0, 2]
+SPLIT = [([0], [1]), ([2], [3])]
+CFG = {(p, l): (SPLIT, [[0], [1]]) for p in range(2) for l in range(L)}
+CH = 256
+COST = dict(GE=1.5e-3, CY=0.83e-3, WAKE=0.12, REMOTE=4.0, PE=0.5e-3, FIX=0.01, YT=7.0)
+PRI = dict(chain=1.0, relu=2.0, p1=1.5, xup=3.0)
+
+SCRATCH = {
+    "yt": ("sbuf", [128, NI], "bfloat16"),
+    "x0": ("sbuf", [128, R], "bfloat16"), "x1": ("sbuf", [128, R], "bfloat16"), "xf": ("sbuf", [128, R], "float32"),
+    "rep0": ("sbuf", [128, L * 2 * CH], "bfloat16"), "rep1": ("sbuf", [128, L * 2 * CH], "bfloat16"),
+    "am": ("sbuf", [128, 48], "float32"), "wall": ("sbuf", [128, 48], "int32"),
+    "hm": ("sbuf", [128, 24], "int32"), "hf": ("sbuf", [128, 24], "float32"),
+    "lh": ("sbuf", [128, 8], "int32"), "lob": ("sbuf", [128, 8], "float32"),
+    "hi40": ("sbuf", [128, 40], "int32"), "h1": ("sbuf", [128, 40], "int32"), "h2": ("sbuf", [128, 40], "int32"),
+    "h3": ("sbuf", [128, 40], "int32"), "h4": ("sbuf", [128, 40], "int32"), "h5": ("sbuf", [128, 40], "int32"),
+    "h6": ("sbuf", [128, 40], "int32"), "hl": ("sbuf", [128, 40], "uint16"), "hs": ("sbuf", [128, 20], "uint16"),
+    "ones": ("sbuf", [128, 128], "float32"), "bo1": ("sbuf", [128, 128], "float32"), "bo": ("sbuf", [128, 128], "float32"),
+    "idm": ("sbuf", [128, 128], "float32"), "etab": ("sbuf", [128, 64], "float32"), "e0": ("sbuf", [128, 128], "float32"),
+    "idb": ("sbuf", [128, 128], "bfloat16"), "i64": ("sbuf", [128, 128], "float16"),
+    "m1": ("sbuf", [128, 64], "float32"), "m2": ("sbuf", [128, 32], "float32"),
+    "mk": ("sbuf", [128, 64], "float32"), "mks": ("sbuf", [128, 128], "float32"),
+    "col": ("sbuf", [128, 8], "float32"), "qt": ("sbuf", [128, 512], "float32"), "qw": ("sbuf", [128, 512], "float16"),
+    "zs": ("sbuf", [128, 160], "bfloat16"), "zr": ("sbuf", [128, 160], "bfloat16"), "zd": ("sbuf", [128, 160], "bfloat16"),
+    "bos": ("sbuf", [128, 128], "float16"), "seg": ("sbuf", [128, 64], "float32"), "nst": ("sbuf", [128, 128], "float32"),
+    "cli": ("sbuf", [128, 4], "int32"), "clist": ("sbuf", [128, 4], "uint16"),
+    "dg0": ("sbuf", [128, 128], "float16"),
+}
+for _p in range(2):
+    SCRATCH["win%d" % _p] = ("sbuf", [128, 2 * R], "float32")
+    SCRATCH["as%d" % _p] = ("sbuf", [128, 32 * 64], "bfloat16")
+    SCRATCH["dv%d" % _p] = ("sbuf", [128, 32 * 64], "bfloat16")
+    SCRATCH["rv%d" % _p] = ("sbuf", [128, 32 * 64], "bfloat16")
+    SCRATCH["ks%d" % _p] = ("sbuf", [128, 256], "float32")
+    SCRATCH["ki%d" % _p] = ("sbuf", [128, 4], "int32")
+    SCRATCH["ei%d" % _p] = ("sbuf", [128, 4], "int32")
+    SCRATCH["tf%d" % _p] = ("sbuf", [128, 4], "float32")
+    SCRATCH["wf%d" % _p] = ("sbuf", [128, 8], "float32")
+    SCRATCH["wo%d" % _p] = ("sbuf", [128, 8], "uint16")
+    SCRATCH["dg%d" % (_p + 1)] = ("sbuf", [128, 64], "float16")
+    SCRATCH["dx%d" % _p] = ("sbuf", [128, 64], "bfloat16")
+    SCRATCH["um%d" % _p] = ("sbuf", [128, 128], "float32")
+    SCRATCH["us%d" % _p] = ("sbuf", [128, 128], "float32")
+    SCRATCH["vz%d" % _p] = ("sbuf", [128, 32], "float32")
+    SCRATCH["z%d" % _p] = ("sbuf", [128, 32], "float16")
+    for _u in range(2): SCRATCH["K%d%d" % (_p, _u)] = ("psum", [128, 512], "float32")
+    SCRATCH["Q%d" % _p] = ("psum", [128, 512], "float32")
+    SCRATCH["KN%d" % _p] = ("psum", [128, 512], "float32")
+for _s in range(3):
+    SCRATCH["sc%d" % _s] = ("sbuf", [128, 24], "float32")
+    SCRATCH["ofv%d" % _s] = ("sbuf", [128, 128], "uint16")
+    SCRATCH["ofs%d" % _s] = ("sbuf", [128, 128], "uint16")
+    SCRATCH["pa%d" % _s] = ("sbuf", [128, 256], "float32")
+    SCRATCH["pn%d" % _s] = ("sbuf", [128, 256], "float16")
+
+LOADS = ["lo", "hi", "x", "home", "y", "h"]
+SEMAPHORES = (["cV", "cS", "cT", "cG", "snt", "st"] + ["ld_" + k for k in LOADS]
+              + ["arr%d_%d" % (p, l) for p in range(2) for l in range(L - 1)])
+
+
+def build(g, core, T, topo, rank):
+    ops = []; ctx = [("setup", 0, 0, 0)]
+    last_w, readers = {}, {}
+    GE, CY, PE = COST["GE"], COST["CY"], COST["PE"]
+
+    def add(q, dur, fn, r=(), w=(), n=1, sem=None, val=0, lat=0.0, grp=None):
+        i = len(ops); deps = {}
+        for t in r:
+            if t in last_w: deps[last_w[t]] = "raw"
+        for t in w:
+            if t in last_w: deps.setdefault(last_w[t], "waw")
+            for k in readers.get(t, ()):
+                if k != i: deps.setdefault(k, "war")
+        for t in r: readers.setdefault(t, []).append(i)
+        for t in w: last_w[t] = i; readers[t] = []
+        ops.append(dict(q=q, dur=dur, fn=fn, deps=deps, n=n, sem=sem, val=val, lat=lat, grp=grp, tag=ctx[0]))
+        return i
+
+    V, S, G, TE, SY = g.vector, g.scalar, g, g.tensor, g.sync
+    sv = lambda n, c=1.0: COST["FIX"] + max(64, n * c) * CY
+
+    def ts(out, in0, s1, s2, o0, o1, r, w, n, c=1.0):
+        if o1 is None: add("V", sv(n, c), lambda: V.tensor_scalar(out, in0, s1, None, o0), r, w)
+        else: add("V", sv(n, c), lambda: V.tensor_scalar(out, in0, s1, s2, o0, o1), r, w)
+    def tt(out, a, b, op, r, w, n, c=2.0, gather=False):
+        add("V", 0.05 + n * GE if gather else sv(n, c), lambda: V.tensor_tensor(out, a, b, op), r, w)
+    def cp(out, in_, r, w, n, c=1.0, gather=False):
+        add("V", 0.05 + n * GE if gather else sv(n, c), lambda: V.tensor_copy(out, in_), r, w)
+    def ms(ap, v, w, n, r=()):
+        add("V", sv(n), lambda: V.memset(ap, v), r, w)
+    def scan(out, d0, d1, init, o0, o1, r, w, n):
+        add("V", sv(n), lambda: V.tensor_tensor_scan(out, d0, d1, init, o0, o1), r, w)
+    def act(out, in_, r, w, n, bias=0.0, scale=1.0, f=F.Abs):
+        add("S", 0.065 + n * CY, lambda: S.activation(out, in_, f, bias=bias, scale=scale), r, w)
+
+    def load(q, key, out, in_, tok, lat):
+        eng = SY if q == "SY" else S
+        add(q, 0.1, lambda: eng.dma_start(out, in_), (), (tok,), sem="ld_" + key, val=16, lat=lat)
+    load("S", "lo", T.lh[:, 0:4], T.lo0[:], "lo", 1.8)
+    load("SY", "hi", T.lh[:, 4:8], T.hi0[:], "hi", 1.8)
+    load("S", "x", T.x0[:], T.xrow[:], "x0", 2.2)
+    load("SY", "home", T.hm[:], T.home[:], "hm", 2.2)
+    load("SY", "y", T.yt[:], T.ytab[:], "yt", COST["YT"])
+    for l in range(L - 1):
+        for k, (nm, q) in enumerate((("ha", "S"), ("hb", "SY"))):
+            eng = SY if q == "SY" else S
+            add(q, 0.1, lambda eng=eng, o=8 * l + 4 * k, t=T[nm][:, 4 * l:4 * l + 4]: eng.dma_start(T.hi40[:, o:o + 4], t), (), ("%s%d" % (nm, l),), sem="ld_h", val=32 * (L - 1), lat=7.5)
+    HT = ["%s%d" % (nm, l) for l in range(L - 1) for nm in ("ha", "hb")]
+
+    ms(T.ones[:], 1.0, ["ones"], 128)
+    def aff(out, in_, pat, op, base, cm, r, w): add("G", 0.4, lambda: G.affine_select(out, in_, pat, op, 0.0, base, cm), r, w)
+    add("G", 0.25, lambda: G.iota(T.etab[:], [[1, 64]], 0, 0, allow_small_or_imprecise_dtypes=True), (), ["etab"])
+    aff(T.idm[:], T.ones[:], [[-1, 128]], A.is_equal, 0, 1, ["ones"], ["idm"])
+    aff(T.bo1[:], T.ones[:], [[-16, 8], [0, 16]], A.is_ge, 0, 1, ["ones"], ["bo1"])
+    aff(T.bo[:], T.bo1[:], [[16, 8], [0, 16]], A.is_ge, 15, -1, ["bo1"], ["bo"])
+    add("G", 0.35, lambda: G.iota(T.e0[:], [[0, 8], [1, 16]], 0, 0, allow_small_or_imprecise_dtypes=True), (), ["e0"])
+    add("G", 0.15, lambda: G.iota(T.cli[:], [[1, 4]], 0, 0), (), ["cli"])
+    cp(T.clist[:], T.cli[:], ["cli"], ["clist"], 4)
+    ms(T.seg[:], -1.0, ["seg0"], 64)
+    ms(T.seg[:, 0:1], BIG, ["seg"], 1, ["seg0"])
+    tt(T.m1[:], T.idm[:, 0:64], T.idm[:, 64:128], A.add, ["idm"], ["m1"], 64)
+    tt(T.m2[:], T.m1[:, 0:32], T.m1[:, 32:64], A.add, ["m1"], ["m2"], 32)
+    tt(T.mk[:, 0:16], T.m2[:, 0:16], T.m2[:, 16:32], A.add, ["m2"], ["mk16"], 16)
+    cp(T.mk[:, 16:32], T.mk[:, 0:16], ["mk16"], ["mk32"], 16)
+    cp(T.mk[:, 32:64], T.mk[:, 0:32], ["mk16", "mk32"], ["mk"], 32)
+    add("V", sv(8), lambda: V.tensor_reduce(T.col[:, 0:1], T.mk[:, 1:16:2], AxisListType.X, A.add), ["mk16"], ["odd"])
+    ts(T.col[:, 1:2], T.col[:, 0:1], 2.0, -1.0, A.mult, A.add, ["odd"], ["sgn"], 1)
+    tt(T.col[:, 2:3], T.mk[:, 0:1], T.mk[:, 1:2], A.add, ["mk16"], ["ab"], 1)
+    ts(T.col[:, 3:4], T.mk[:, 0:1], -64.0, None, A.mult, None, ["mk16"], ["a64_0"], 1)
+    for c in range(1, 4):
+        ts(T.col[:, 3 + c:4 + c], T.col[:, 2:3], 16.0 * c, T.col[:, 3:4], A.mult, A.add, ["ab", "a64_0"], ["a64_%d" % c], 1)
+    for c in range(4):
+        q = T.qt[:, 128 * c:128 * c + 128]
+        act(q, T.e0[:], ["e0", "ab", "a64_%d" % c], ["qt%d" % c], 128, bias=T.col[:, 3 + c:4 + c], scale=T.col[:, 2:3], f=F.Identity)
+        tt(T.qw[:, 128 * c:128 * c + 128], q, T.bo[:], A.mult, ["qt%d" % c, "bo"], ["qw%d" % c], 128)
+    QWT = ["qw%d" % c for c in range(4)]
+    ts(T.bos[:, 0:128:2], T.bo[:, 0:128:2], -1.0, None, A.mult, None, ["bo"], ["bosA"], 64)
+    cp(T.bos[:, 1:128:2], T.bo[:, 1:128:2], ["bo"], ["bosB"], 64)
+    act(T.idb[:], T.idm[:], ["idm"], ["idb"], 128, f=F.Identity)
+    for nm, c in (("zs", 64.0), ("zr", 128.0), ("zd", -64.0)):
+        ms(T[nm][:], 0.0, [nm + "0"], 160)
+        act(T[nm][:, 15:143:16], T.bo[:, 0:128:16], ["bo", nm + "0"], [nm], 8, scale=c, f=F.Identity)
+    ts(T.i64[:], T.idm[:], 64.0, None, A.mult, None, ["idm"], ["i64"], 128)
+    ts(T.nst[:], T.e0[:], 0.0, None, A.is_gt, None, ["e0"], ["nst"], 128)
+    for k in range(2):
+        act(T.mks[:, 64 * k:64 * k + 64], T.mk[:], ["mk16", "mk32", "mk", "sgn"], ["mks%d" % k], 64, scale=T.col[:, 1:2], f=F.Identity)
+
+    for k, nm in ((0, "lo"), (4, "hi")):
+        ts(T.lob[:, k:k + 4], T.lh[:, k:k + 4], -2048.0, 1.0 / 64, A.add, A.mult, [nm], [nm + "b"], 4)
+    cp(T.hf[:], T.hm[:], ["hm"], ["hf"], 24)
+    ts(T.h1[:], T.hi40[:], 384.0, -384.0, A.is_ge, A.mult, HT, ["h1"], 40)
+    tt(T.h2[:], T.hi40[:], T.h1[:], A.add, HT + ["h1"], ["h2"], 40)
+    ts(T.h3[:], T.h2[:], 960, None, A.bitwise_and, None, ["h2"], ["h3"], 40)
+    tt(T.h4[:], T.h2[:], T.h3[:], A.add, ["h2", "h3"], ["h4"], 40)
+    ts(T.h5[:], T.h1[:], -1.0 / 6, None, A.mult, None, ["h1"], ["h5"], 40)
+    tt(T.h6[:], T.h4[:], T.h5[:], A.add, ["h4", "h5"], ["h6"], 40)
+    cp(T.hl[:], T.h6[:], ["h6"], ["hl"], 40)
+    cp(T.hs[:], T.h6[:, 0:40:2], ["h6"], ["hs"], 20)
+
+    def xtok(p, l, a): return "x0" if p == 0 else "x1.%d.%d" % (l, a)
+    reptok = {}
+    def reps(p, l, u):
+        vb = CFG[p, l][0][u][1]; ctx[0] = ("reps", p, l, u)
+        o = 2 * CH * l + CH * u; t = "rep%d.%d.%d" % (p, l, u)
+        x = T["x%d" % p]; q = 1 - p; nb = len(vb); n = 16
+        def mm():
+            return [TE.matmul(T["Q%d" % q][:, k:k + n], T.idb[:], x[:, 64 * l + 16 * vb[k // n % nb]:64 * l + 16 * vb[k // n % nb] + n], True, True) for k in range(0, CH, n)]
+        add("T", CH // n * 64 * PE, mm, ["idb"] + [xtok(p, l, a) for a in vb], ["Q%d" % q], n=CH // n)
+        act(T["rep%d" % p][:, o:o + CH], T["Q%d" % q][:, 0:CH], ["Q%d" % q], [t], CH, f=F.Identity)
+        reptok[p, l, u] = [t]
+
+    def lists(p, s, l, lotok):
+        sc = T["sc%d" % s]; t = "sc%d." % s
+        lo, hi = (T.lob[:, 0:4], T.lob[:, 4:8]) if s == 2 else (sc[:, 0:4], sc[:, 4:8])
+        tt(sc[:, 8:12], hi, lo, A.subtract, lotok, [t + "D"], 4)
+        ts(sc[:, 12:16], lo, 64.0, CJ, A.mult, A.add, lotok, [t + "B1"], 4)
+        tt(sc[:, 16:20], sc[:, 12:16], T.hf[:, 4 * l:4 * l + 4], A.subtract, [t + "B1", "hf"], [t + "B2"], 4)
+        pa = T["pa%d" % s]; po = 0; vo = 0; pt = []
+        for sb, vb in CFG[p, l][0]:
+            nb = len(vb); o = po + 64 * len(sb)
+            for k, a in enumerate(vb):
+                ts(T["ofv%d" % s][:, vo + k:vo + 64 * nb:nb], T.etab[:], sc[:, 8 + a:9 + a], sc[:, 12 + a:13 + a], A.mult, A.add, ["etab", t + "D", t + "B1"], ["ofv%d.%d" % (s, a)], 64)
+            for k, a in enumerate(sb + vb):
+                out = pa[:, po + 64 * k:po + 64 * k + 64] if a in sb else pa[:, o + k - len(sb):o + 64 * nb:nb]
+                act(out, T.etab[:], ["etab", t + "D", t + "B2"], ["pa%d.%d" % (s, a)], 64, bias=sc[:, 16 + a:17 + a], scale=sc[:, 8 + a:9 + a])
+                pt.append("pa%d.%d" % (s, a))
+            po = o + 64 * nb; vo += 64 * nb
+        ts(T["pn%d" % s][:], pa[:], 1.0 / 16, 1280.0 - 15.0 / 32, A.mult, A.add, pt, ["pn%d" % s], 256)
+
+    def slist(s, p):
+        def mm():
+            return [TE.matmul(T["Q%d" % p][:, c:128:4], T.qw[:, 128 * c:128 * c + 128], T["z%d" % p][:], True, True) for c in range(4)]
+        add("T", 4 * 64 * PE, mm, QWT + ["z%d" % p], ["Q%d" % p], n=4)
+        ts(T["ofs%d" % s][:], T["Q%d" % p][:, 0:128], CJ, None, A.add, None, ["Q%d" % p], ["ofs%d" % s], 128)
+
+    def prep0():
+        ctx[0] = ("prep", 0, 0, 0); r = []
+        for k, nm in ((0, "lob"), (1, "hib")):
+            for j, a in enumerate(SBL):
+                ts(T.dg0[:, 32 * k + 16 * j:32 * k + 16 * j + 16], T.mk[:, 0:16], T.lob[:, 4 * k + a:4 * k + a + 1], None, A.mult, None, ["mk16", nm], ["dg0.%d%d" % (k, a)], 16)
+                r.append("dg0.%d%d" % (k, a))
+        add("T", 0.05, lambda: TE.matmul(T.KN1[:, 0:64], T.bos[:], T.dg0[:, 0:64], True, True), ["bosA", "bosB"] + r, ["KN1"])
+        cp(T.vz0[:], T.KN1[:, 32:64], ["KN1"], ["vz0"], 32)
+        tt(T.z0[:], T.KN1[:, 0:32], T.vz0[:], A.max, ["KN1", "vz0"], ["z0"], 32, 1.0)
+        slist(2, 0)
+        lists(0, 2, 0, ["lob", "hib"])
+
+    def prep(p, l):
+        ctx[0] = ("prep", p, l, 0); w = T["win%d" % p]; win = w[:, 0:128 * l]; sc = T["sc%d" % p]
+        wt = ["w%d.%d.%s" % (p, k, x) for k in range(l) for x in ("own", "rem")]
+        h = 8 * (l - 1); hh = 4 * (l - 1)
+        um, us, vz, z = T["um%d" % p], T["us%d" % p], T["vz%d" % p], T["z%d" % p]
+        tt(um[:], win.indirect(T.hl[:, h:h + 8]), T.mks[:], A.mult, wt + ["hl", "mks0", "mks1"], ["um%d" % p], 128, gather=True)
+        scan(us[:], T.nst[:], um[:], 0.0, A.mult, A.add, ["nst", "um%d" % p], ["us%d" % p], 128)
+        cp(vz[:], win.indirect(T.hs[:, hh + 2:hh + 4]), wt + ["hs"], ["vz%d" % p], 32, gather=True)
+        tt(z[:], win.indirect(T.hs[:, hh:hh + 2]), vz[:], A.max, wt + ["hs", "vz%d" % p], ["z%d" % p], 32, gather=True)
+        u, v = us[:, 15:64:16], us[:, 79:128:16]
+        tt(sc[:, 0:4], u, v, A.min, ["us%d" % p], ["sc%d.lo" % p], 4)
+        tt(sc[:, 4:8], u, v, A.max, ["us%d" % p], ["sc%d.hi" % p], 4)
+        slist(p, p)
+        lists(p, p, l, ["sc%d.lo" % p, "sc%d.hi" % p])
+
+    def sets(p, l): return 2 if l == 0 else p
+
+    def keys(p, l, u):
+        sb, vb = CFG[p, l][0][u]
+        return ["s%d.%d" % (a, i) for a in sb for i in range(16)] + ["v%s%d" % (k, h) for k in "dr" for h in range(len(vb))]
+
+    def search(p, l, u):
+        ctx[0] = ("search", p, l, u); s = sets(p, l); units = CFG[p, l][0]
+        sb, vb = units[u]; nb = len(vb)
+        po = sum(64 * len(a + b) for a, b in units[:u]); vo = sum(64 * len(b) for a, b in units[:u])
+        K = T["K%d%d" % (p, u)]; kt = lambda x: "K%d%d.%s" % (p, u, x)
+        x = T["x%d" % p]; w = 64 * (len(sb) + nb); ko = 64 * len(sb)
+        grp = (p, l, u)
+        kx = [kt(q) for q in keys(p, l, u)]
+        add("T", w * PE, lambda: TE.matmul(K[:, 0:w], T.i64[:], T["pn%d" % s][:, po:po + w], True, False), ["i64", "pn%d" % s], kx + [kt("0")])
+        for j, a in enumerate(sb):
+            for i in range(16):
+                r = 16 * SBL.index(a) + i
+                o = T["as%d" % p][:, 64 * r:64 * r + 64]
+                add("S", 0.065 + 64 * GE, lambda o=o, r=r, a=a, i=i: S.activation(o, T.yt[:].indirect(T["ofs%d" % s][:, 4 * r:4 * r + 4]), F.Abs, bias=x[:, 64 * l + 16 * a + i:64 * l + 16 * a + i + 1], scale=-1.0),
+                    ["yt", "ofs%d" % s, xtok(p, l, a)], ["as%d.%d" % (p, r)])
+                add("T", 64 * PE, lambda stop, o=o, j=j, i=i: TE.matmul(K[:, 64 * j:64 * j + 64], T.zs[:, 15 - i:143 - i], o, False, stop), ["zs", "as%d.%d" % (p, r), kt("0")], [kt("s%d.%d" % (a, i))], grp=grp)
+        nc = 64 * 16 * nb // CH
+        dv, rv = T["dv%d" % p], T["rv%d" % p]
+        for h in range(nb):
+            cs = range(h * nc // nb, (h + 1) * nc // nb)
+            for c in cs:
+                d = 16 * vo + CH * c
+                tt(dv[:, d:d + CH], T.yt[:].indirect(T["ofv%d" % s][:, vo + CH // 16 * c:vo + CH // 16 * (c + 1)]), T["rep%d" % p][:, 2 * CH * l + CH * u:2 * CH * l + CH * u + CH], A.subtract,
+                   ["yt"] + ["ofv%d.%d" % (s, a) for a in vb] + reptok[p, l, u], ["dv%d.%d" % (p, d)], CH, gather=True)
+                if c % 2 == 1:
+                    d -= CH; ctx[0] = ("relu", p, l, u)
+                    ts(rv[:, d:d + 2 * CH], dv[:, d:d + 2 * CH], 0.0, None, A.max, None, ["dv%d.%d" % (p, d), "dv%d.%d" % (p, d + CH)], ["rv%d.%d" % (p, d)], 2 * CH, 0.5)
+                    ctx[0] = ("search", p, l, u)
+            d0 = 16 * vo + CH * cs[0]; d1 = 16 * vo + CH * (cs[-1] + 1)
+            for kind, buf, z in (("d", dv, "zd"), ("r", rv, "zr")):
+                toks = ["%sv%d.%d" % (kind, p, q) for q in range(d0, d1, CH if kind == "d" else 2 * CH)]
+                def mm(stop, h=h, buf=buf, z=z, d0=d0, d1=d1):
+                    return [TE.matmul(K[:, ko + 64 * h:ko + 64 * h + 64], T[z][:, 15 - i:143 - i], buf[:, d0 + i:d1:16], False, stop and i == 15) for i in range(16)]
+                add("T", 16 * 64 * PE, mm, [z, kt("0")] + toks, [kt("v%s%d" % (kind, h))], n=16, grp=grp)
+
+    def post(p, l, us):
+        ctx[0] = ("post", p, l, us[0]); s = sets(p, l); units = CFG[p, l][0]
+        ks, sc = T["ks%d" % p], T["sc%d" % s]; P = "%d" % p
+        bl = []; kst = []
+        for u in us:
+            sb, vb = units[u]; K = T["K%d%d" % (p, u)]; ko = 64 * len(sb); nb = len(vb)
+            kt = ["K%d%d.%s" % (p, u, q) for q in keys(p, l, u)]
+            for j, a in enumerate(sb + vb):
+                src = K[:, 64 * j:64 * j + 64] if a in sb else K[:, ko + j - len(sb):ko + 64 * nb:nb]
+                scan(ks[:, 64 * a:64 * a + 64], T.seg[:], src, BIG, A.add, A.min, kt + ["seg"], ["ks%d.%d" % (p, a)], 64)
+                kst.append("ks%d.%d" % (p, a)); bl.append(a)
+        bl.sort(); c0, c1 = bl[0], bl[-1] + 1; n = c1 - c0; q = P + ".%d" % c0
+        c = slice(c0, c1); wall = T.wall[:, 24 * p + 4 * l + c0:24 * p + 4 * l + c1]
+        ts(T["ki" + P][:, c], ks[:, 64 * c0 + 63:64 * c1:64], 63.0, None, A.add, None, kst, ["ki" + q], 4)
+        ts(T["ei" + P][:, c], T["ki" + P][:, c], 63, None, A.bitwise_and, None, ["ki" + q], ["ei" + q], 4)
+        tt(T["tf" + P][:, c], T["ei" + P][:, c], sc[:, 8 + c0:8 + c1], A.mult, ["ei" + q, "sc%d.D" % s], ["tf" + q], 4)
+        ctx[0] = ("win", p, l, us[0]); wt = "wall%d.%d.%d" % (p, l, c0)
+        tt(wall, T["tf" + P][:, c], sc[:, 12 + c0:12 + c1], A.add, ["tf" + q, "sc%d.B1" % s], [wt], 4)
+        ctx[0] = ("xup", p, l, us[0])
+        cp(T["wo" + P][:, 2 * c0:2 * c0 + n], wall, [wt], ["wo" + q], 4)
+        r0, r1 = 64 * l + 16 * c0, 64 * l + 16 * c1
+        tt(T["dx" + P][:, 16 * c0:16 * c1], T.yt[:].indirect(T["wo" + P][:, 2 * c0:2 * c0 + n]), T["x" + P][:, r0:r1], A.subtract, ["yt", "wo" + q] + [xtok(p, l, a) for a in bl], ["dx" + q], 16 * n, gather=True)
+        if p == 0:
+            act(T.x1[:, r0:r1], T.dx0[:, 16 * c0:16 * c1], ["dx" + q], [xtok(1, l, a) for a in bl], 16 * n)
+        else:
+            act(T.xf[:, r0:r1], T.dx1[:, 16 * c0:16 * c1], ["dx" + q], ["xf.%d.%d" % (l, a) for a in bl], 16 * n)
+        return wt
+
+    def known(p, l, wts):
+        ctx[0] = ("known", p, l, 0); P = "%d" % p; dg = T["dg%d" % (p + 1)]; w = T["win" + P]
+        ts(T["wf" + P][:, 0:4], T.wall[:, 24 * p + 4 * l:24 * p + 4 * l + 4], -2048.0, 1.0 / 64, A.add, A.mult, wts, ["wf" + P], 4)
+        tt(dg[:], T["wf" + P][:, 0:4].indirect(T.clist[:]), T.mk[:], A.mult, ["wf" + P, "clist", "mk16", "mk32", "mk"], ["dg%d" % (p + 1)], 64, gather=True)
+        add("T", 64 * PE, lambda: TE.matmul(T["KN" + P][:, 0:64], T.bos[:], dg[:], True, True), ["bosA", "bosB", "dg%d" % (p + 1)], ["KN" + P])
+        own = w[:, 128 * l:128 * l + 64]; ot = "w%d.%d.own" % (p, l)
+        cp(own, T["KN" + P][:, 0:64], ["KN" + P], [ot], 64)
+        dst = T.cores[(rank - 1) % len(T.cores)]
+        rid, pid, _ = topo.addr(dst)
+        m = topo.mask(core, dst)
+        def send():
+            G.remote_dma(w[:, 128 * l + 64:128 * l + 128], own, T.sem["arr%d_%d" % (p, l)], T.sem.snt, pid, rid, m)
+        add("G", 1.0, send, [ot], ["w%d.%d.rem" % (p, l)], n=0, sem="arr%d_%d" % (p, l), val=len(topo.engines(core, dst)), lat=COST["REMOTE"])
+
+    stores = [0]
+    def store(out, in_, r):
+        stores[0] += 1
+        add("SY", 0.1, lambda: SY.dma_start(out, in_), r, [], sem="st", val=None, lat=2.0)
+
+    prep0()
+    allw = {0: [], 1: []}
+    for k in range(2 * L):
+        p, l = k % 2, k // 2
+        units, posts = CFG[p, l]
+        if p == 0:
+            for u in range(len(units)): reps(0, l, u)
+        if l: prep(p, l)
+        for u in range(len(units)):
+            if p == 1: reps(1, l, u)
+            search(p, l, u)
+        wts = [post(p, l, us) for us in posts]
+        allw[p] += wts
+        if l < L - 1: known(p, l, wts)
+        else:
+            cp(T.am[:, 24 * p:24 * p + 24], T.wall[:, 24 * p:24 * p + 24], allw[p], ["am%d" % p], 24)
+            store(T.argm[:, 24 * p:24 * p + 24], T.am[:, 24 * p:24 * p + 24], ["am%d" % p])
+        if p == 1 and l in (2, 4, 5):
+            f = {2: 0, 4: 3, 5: 5}[l]
+            store(T.xo[:, 64 * f:64 * l + 64], T.xf[:, 64 * f:64 * l + 64], ["xf.%d.%d" % (q, a) for q in range(f, l + 1) for a in range(4)])
+    return ops, stores
+
+
+def early(tag):
+    k, p = tag[0], tag[1]; v = 0.0
+    if k in ("prep", "post", "win", "known"): v += PRI["chain"]
+    if k in ("xup", "reps"): v += PRI["xup"]
+    if k == "relu": v += PRI["relu"]
+    if k != "setup": v += PRI["p1"] * p
+    return v
+
+
+def plan(ops):
+    n = len(ops); WAKE = COST["WAKE"]
+    succ = [[] for _ in range(n)]
+    for i, o in enumerate(ops):
+        for d in o["deps"]: succ[d].append(i)
+    way = [0.0] * n
+    for i in range(n - 1, -1, -1):
+        o = ops[i]
+        way[i] = o["dur"] + max([o["lat"] + WAKE + way[j] for j in succ[i]] + [0.0])
+    pri = [way[i] + early(ops[i]["tag"]) for i in range(n)]
+    left = [len(o["deps"]) for o in ops]
+    ready = [0.0] * n
+    free = {"V": 0.0, "S": 0.0, "G": 0.0, "T": 0.0, "SY": 0.0}
+    cand = {q: [] for q in free}
+    for i in range(n):
+        if left[i] == 0: cand[ops[i]["q"]].append(i)
+    order, start = [], [0.0] * n
+    while len(order) < n:
+        best = None
+        for q in cand:
+            for i in cand[q]:
+                key = (max(free[q], ready[i]), -pri[i], i)
+                if best is None or key < best: best = key
+        t, i = best[0], best[2]
+        o = ops[i]; q = o["q"]
+        cand[q].remove(i)
+        start[i] = t; fin = t + o["dur"]; free[q] = fin
+        order.append(i)
+        for j in succ[i]:
+            same = ops[j]["q"] == q and q == "T"
+            ready[j] = max(ready[j], t if same else fin + o["lat"] + WAKE)
+            left[j] -= 1
+            if left[j] == 0: cand[ops[j]["q"]].append(j)
+    pos = {i: k for k, i in enumerate(order)}
+    order.sort(key=lambda i: (start[i], pos[i]))
+    return order
+
+
+CACHE = {}
+
+
+def rank_program(g, core, T, topo):
+    rank = T.rank_of(core)
+    if rank is None:
+        return
+    ops, stores = build(g, core, T, topo, rank)
+    if "order" not in CACHE: CACHE["order"] = plan(ops)
+    order = CACHE["order"]
+    eng = {"V": g.vector, "S": g.scalar, "G": g, "T": g.tensor, "SY": g.sync}
+    csem = {"V": T.sem.cV, "S": T.sem.cS, "T": T.sem.cT, "G": T.sem.cG}
+    count = {q: 0 for q in csem}
+    done = {}
+    seen = {q: {} for q in eng}
+    last = {ops[i]["grp"]: i for i in order if ops[i]["grp"]}
+    for i in order:
+        o = ops[i]; q = o["q"]; need = {}
+        for d in o["deps"]:
+            if ops[d]["q"] == q and q == "T": continue
+            nm, v = done[d]
+            need[nm] = max(need.get(nm, 0), v)
+        for nm in sorted(need):
+            if seen[q].get(nm, 0) < need[nm]:
+                eng[q].wait_ge(T.sem[nm], need[nm]); seen[q][nm] = need[nm]
+        res = o["fn"](last[o["grp"]] == i) if o["grp"] else o["fn"]()
+        if o["sem"] is not None:
+            if q != "G": res.then_inc(T.sem[o["sem"]], 16)
+            done[i] = (o["sem"], o["val"])
+        else:
+            for x in (res if o["n"] > 1 else [res]): x.then_inc(csem[q], 1)
+            count[q] += o["n"]
+            done[i] = ("c" + q, count[q])
+    g.sync.wait_ge(T.sem.st, 16 * stores[0])
+    dst = T.cores[(rank - 1) % len(T.cores)]
+    g.wait_ge(T.sem.snt, 2 * (L - 1) * len(topo.engines(core, dst)))
+    for q in ("V", "S", "T", "G"):
+        g.sync.wait_ge(csem[q], count[q])

@@ -5,63 +5,57 @@ A = AluOpType
 F = ActivationFunctionType
 L, R, NI = 6, 384, 4096
 BIG = float(2 ** 22)
-CJ = 2048.0 - 63.0 / 128.0
-SBL = [0, 2]
-SPLIT = [([0], [1]), ([2], [3])]
-CFG = {(p, l): (SPLIT, [[0], [1]]) for p in range(2) for l in range(L)}
+OFF = 16384.0
+DL = 63.0 / 128.0
+BLK = [0, 2, 1, 3]
 CH = 256
-COST = dict(GE=1.5e-3, CY=0.83e-3, WAKE=0.12, REMOTE=4.0, PE=0.5e-3, FIX=0.01, YT=7.0)
-PRI = dict(chain=1.0, relu=2.0, p1=1.5, xup=3.0)
+XW = 16 + CH
+COST = dict(GE=1.3e-3, CY=0.95e-3, WAKE=0.15, REMOTE=2.5, PE=0.5e-3, FIX=0.01, YT=5.5, SF=0.05, LOOK=0.03, TOL=0.0, GAP=0.3)
+PRI = dict(setup=-9.0, hints=-3.0, reps=-5.0, const=-3.0, z=-5.0, prep=-5.0, pen=0.5, search=0.0, post=-3.0, xup=-2.0, late=3.0, v=0.0, relu=2.0, mv=0.0)
+OPT = dict(joint=1, nrelu=2, share=1)
 
 SCRATCH = {
-    "yt": ("sbuf", [128, NI], "bfloat16"),
-    "x0": ("sbuf", [128, R], "bfloat16"), "x1": ("sbuf", [128, R], "bfloat16"), "xf": ("sbuf", [128, R], "float32"),
-    "rep0": ("sbuf", [128, L * 2 * CH], "bfloat16"), "rep1": ("sbuf", [128, L * 2 * CH], "bfloat16"),
-    "am": ("sbuf", [128, 48], "float32"), "wall": ("sbuf", [128, 48], "int32"),
-    "hm": ("sbuf", [128, 24], "int32"), "hf": ("sbuf", [128, 24], "float32"),
-    "lh": ("sbuf", [128, 8], "int32"), "lob": ("sbuf", [128, 8], "float32"),
-    "hi40": ("sbuf", [128, 40], "int32"), "h1": ("sbuf", [128, 40], "int32"), "h2": ("sbuf", [128, 40], "int32"),
-    "h3": ("sbuf", [128, 40], "int32"), "h4": ("sbuf", [128, 40], "int32"), "h5": ("sbuf", [128, 40], "int32"),
-    "h6": ("sbuf", [128, 40], "int32"), "hl": ("sbuf", [128, 40], "uint16"), "hs": ("sbuf", [128, 20], "uint16"),
-    "ones": ("sbuf", [128, 128], "float32"), "bo1": ("sbuf", [128, 128], "float32"), "bo": ("sbuf", [128, 128], "float32"),
-    "idm": ("sbuf", [128, 128], "float32"), "etab": ("sbuf", [128, 64], "float32"), "e0": ("sbuf", [128, 128], "float32"),
-    "idb": ("sbuf", [128, 128], "bfloat16"), "i64": ("sbuf", [128, 128], "float16"),
-    "m1": ("sbuf", [128, 64], "float32"), "m2": ("sbuf", [128, 32], "float32"),
-    "mk": ("sbuf", [128, 64], "float32"), "mks": ("sbuf", [128, 128], "float32"),
-    "col": ("sbuf", [128, 8], "float32"), "qt": ("sbuf", [128, 512], "float32"), "qw": ("sbuf", [128, 512], "float16"),
+    "yt": ("sbuf", [128, NI], "bfloat16"), "x0": ("sbuf", [128, 2 * L, 32], "bfloat16"), "xf": ("sbuf", [128, R], "float32"),
+    "rep0": ("sbuf", [128, 2 * L, XW], "bfloat16"), "xr": ("sbuf", [128, 2 * L, XW], "bfloat16"), "m16": ("sbuf", [128, 16], "bfloat16"),
+    "am": ("sbuf", [128, 48], "float32"), "hm": ("sbuf", [128, 24], "int32"), "hf": ("sbuf", [128, 24], "float32"),
+    "lh": ("sbuf", [128, 8], "int32"), "lob": ("sbuf", [128, 8], "float32"), "hab": ("sbuf", [128, 40], "int32"),
+    "hl": ("sbuf", [128, 48], "uint16"), "hr": ("sbuf", [128, 48], "uint16"), "mk": ("sbuf", [128, L * 128], "bfloat16"),
+    "pi": ("sbuf", [128, 8], "int32"), "pj": ("sbuf", [128, 24], "int32"), "col": ("sbuf", [128, 16], "float32"),
+    "ctab": ("sbuf", [128, 160], "float32"), "gtab": ("sbuf", [128, 128], "float32"), "t2": ("sbuf", [128, 128], "float32"),
+    "e0": ("sbuf", [128, 128], "float32"), "qt": ("sbuf", [128, 512], "bfloat16"), "qw": ("sbuf", [128, 512], "float16"),
+    "bo": ("sbuf", [128, 128], "float16"), "bos": ("sbuf", [128, 128], "float16"), "bop": ("sbuf", [128, 128], "float16"),
+    "bon": ("sbuf", [128, 128], "float16"), "idh": ("sbuf", [128, 128], "float16"), "i64": ("sbuf", [128, 128], "float16"),
+    "idb": ("sbuf", [128, 128], "bfloat16"), "idn": ("sbuf", [128, 128], "bfloat16"),
+    "c1": ("sbuf", [128, 256], "float16"), "c2": ("sbuf", [128, 128], "float16"), "zero": ("sbuf", [128, 128], "bfloat16"),
     "zs": ("sbuf", [128, 160], "bfloat16"), "zr": ("sbuf", [128, 160], "bfloat16"), "zd": ("sbuf", [128, 160], "bfloat16"),
-    "bos": ("sbuf", [128, 128], "float16"), "seg": ("sbuf", [128, 64], "float32"), "nst": ("sbuf", [128, 128], "float32"),
-    "cli": ("sbuf", [128, 4], "int32"), "clist": ("sbuf", [128, 4], "uint16"),
-    "dg0": ("sbuf", [128, 128], "float16"),
+    "seg": ("sbuf", [128, 128], "float32"), "sgp": ("sbuf", [128, 64], "float32"), "sgn": ("sbuf", [128, 64], "float32"),
+    "sgz": ("sbuf", [128, 64], "float32"),
+    "Z": ("psum", [128, 512], "float32"), "X": ("psum", [128, 512], "float32"),
 }
+for _k in range(1, 8): SCRATCH["h%d" % _k] = ("sbuf", [128, 40], "int32")
 for _p in range(2):
-    SCRATCH["win%d" % _p] = ("sbuf", [128, 2 * R], "float32")
+    SCRATCH["win%d" % _p] = ("sbuf", [128, 8 * L], "int32")
     SCRATCH["as%d" % _p] = ("sbuf", [128, 32 * 64], "bfloat16")
     SCRATCH["dv%d" % _p] = ("sbuf", [128, 32 * 64], "bfloat16")
     SCRATCH["rv%d" % _p] = ("sbuf", [128, 32 * 64], "bfloat16")
     SCRATCH["ks%d" % _p] = ("sbuf", [128, 256], "float32")
     SCRATCH["ki%d" % _p] = ("sbuf", [128, 4], "int32")
     SCRATCH["ei%d" % _p] = ("sbuf", [128, 4], "int32")
-    SCRATCH["tf%d" % _p] = ("sbuf", [128, 4], "float32")
-    SCRATCH["wf%d" % _p] = ("sbuf", [128, 8], "float32")
-    SCRATCH["wo%d" % _p] = ("sbuf", [128, 8], "uint16")
-    SCRATCH["dg%d" % (_p + 1)] = ("sbuf", [128, 64], "float16")
-    SCRATCH["dx%d" % _p] = ("sbuf", [128, 64], "bfloat16")
-    SCRATCH["um%d" % _p] = ("sbuf", [128, 128], "float32")
-    SCRATCH["us%d" % _p] = ("sbuf", [128, 128], "float32")
-    SCRATCH["vz%d" % _p] = ("sbuf", [128, 32], "float32")
-    SCRATCH["z%d" % _p] = ("sbuf", [128, 32], "float16")
+    SCRATCH["wo%d" % _p] = ("sbuf", [128, 4], "uint16")
+    SCRATCH["dx%d" % _p] = ("sbuf", [128, 128], "bfloat16")
+    SCRATCH["rh%d" % _p] = ("sbuf", [128, 128], "float16")
+    SCRATCH["z%d" % _p] = ("sbuf", [128, 64], "float16")
     for _u in range(2): SCRATCH["K%d%d" % (_p, _u)] = ("psum", [128, 512], "float32")
-    SCRATCH["Q%d" % _p] = ("psum", [128, 512], "float32")
-    SCRATCH["KN%d" % _p] = ("psum", [128, 512], "float32")
+    SCRATCH["R%d" % _p] = ("psum", [128, 512], "float32")
 for _s in range(3):
-    SCRATCH["sc%d" % _s] = ("sbuf", [128, 24], "float32")
+    SCRATCH["ls%d" % _s] = ("sbuf", [128, 256], "float32")
+    SCRATCH["sc%d" % _s] = ("sbuf", [128, 8], "float32")
     SCRATCH["ofv%d" % _s] = ("sbuf", [128, 128], "uint16")
     SCRATCH["ofs%d" % _s] = ("sbuf", [128, 128], "uint16")
     SCRATCH["pa%d" % _s] = ("sbuf", [128, 256], "float32")
     SCRATCH["pn%d" % _s] = ("sbuf", [128, 256], "float16")
 
-LOADS = ["lo", "hi", "x", "home", "y", "h"]
+LOADS = ["y", "lo", "hi", "x", "home", "ha", "hb"]
 SEMAPHORES = (["cV", "cS", "cT", "cG", "snt", "st"] + ["ld_" + k for k in LOADS]
               + ["arr%d_%d" % (p, l) for p in range(2) for l in range(L - 1)])
 
@@ -72,16 +66,15 @@ def build(g, core, T, topo, rank):
     GE, CY, PE = COST["GE"], COST["CY"], COST["PE"]
 
     def add(q, dur, fn, r=(), w=(), n=1, sem=None, val=0, lat=0.0, grp=None):
-        i = len(ops); deps = {}
+        i = len(ops); deps = set()
         for t in r:
-            if t in last_w: deps[last_w[t]] = "raw"
+            if t in last_w: deps.add(last_w[t])
         for t in w:
-            if t in last_w: deps.setdefault(last_w[t], "waw")
-            for k in readers.get(t, ()):
-                if k != i: deps.setdefault(k, "war")
+            if t in last_w: deps.add(last_w[t])
+            deps.update(k for k in readers.get(t, ()) if k != i)
         for t in r: readers.setdefault(t, []).append(i)
         for t in w: last_w[t] = i; readers[t] = []
-        ops.append(dict(q=q, dur=dur, fn=fn, deps=deps, n=n, sem=sem, val=val, lat=lat, grp=grp, tag=ctx[0]))
+        ops.append(dict(q=q, dur=dur, fn=fn, deps=sorted(deps), n=n, sem=sem, val=val, lat=lat, grp=grp, tag=ctx[0]))
         return i
 
     V, S, G, TE, SY = g.vector, g.scalar, g, g.tensor, g.sync
@@ -92,297 +85,287 @@ def build(g, core, T, topo, rank):
         else: add("V", sv(n, c), lambda: V.tensor_scalar(out, in0, s1, s2, o0, o1), r, w)
     def tt(out, a, b, op, r, w, n, c=2.0, gather=False):
         add("V", 0.05 + n * GE if gather else sv(n, c), lambda: V.tensor_tensor(out, a, b, op), r, w)
-    def cp(out, in_, r, w, n, c=1.0, gather=False):
-        add("V", 0.05 + n * GE if gather else sv(n, c), lambda: V.tensor_copy(out, in_), r, w)
+    def cp(out, in_, r, w, n, c=1.0):
+        add("V", sv(n, c), lambda: V.tensor_copy(out, in_), r, w)
     def ms(ap, v, w, n, r=()):
         add("V", sv(n), lambda: V.memset(ap, v), r, w)
-    def scan(out, d0, d1, init, o0, o1, r, w, n):
-        add("V", sv(n), lambda: V.tensor_tensor_scan(out, d0, d1, init, o0, o1), r, w)
-    def act(out, in_, r, w, n, bias=0.0, scale=1.0, f=F.Abs):
-        add("S", 0.065 + n * CY, lambda: S.activation(out, in_, f, bias=bias, scale=scale), r, w)
+    def scan(out, d0, d1, o1, r, w, n):
+        add("V", sv(n), lambda: V.tensor_tensor_scan(out, d0, d1, 0.0, A.add, o1), r, w)
+    def act(out, in_, r, w, n, bias=0.0, scale=1.0, f=F.Abs, gather=False):
+        add("S", 0.065 + n * GE if gather else COST["SF"] + n * CY, lambda: S.activation(out, in_, f, bias=bias, scale=scale), r, w)
+    def mms(calls, r, w, grp=None):
+        def fn(last=False):
+            return [TE.matmul(o, a, b, st, (last and k == len(calls) - 1) if sp is None else sp) for k, (o, a, b, n, st, sp) in enumerate(calls)]
+        add("T", sum(max(64, c[3]) for c in calls) * PE, fn, r, w, n=len(calls), grp=grp)
 
-    def load(q, key, out, in_, tok, lat):
+    def load(q, key, out, in_, lat):
         eng = SY if q == "SY" else S
-        add(q, 0.1, lambda: eng.dma_start(out, in_), (), (tok,), sem="ld_" + key, val=16, lat=lat)
-    load("S", "lo", T.lh[:, 0:4], T.lo0[:], "lo", 1.8)
-    load("SY", "hi", T.lh[:, 4:8], T.hi0[:], "hi", 1.8)
-    load("S", "x", T.x0[:], T.xrow[:], "x0", 2.2)
-    load("SY", "home", T.hm[:], T.home[:], "hm", 2.2)
-    load("SY", "y", T.yt[:], T.ytab[:], "yt", COST["YT"])
-    for l in range(L - 1):
-        for k, (nm, q) in enumerate((("ha", "S"), ("hb", "SY"))):
-            eng = SY if q == "SY" else S
-            add(q, 0.1, lambda eng=eng, o=8 * l + 4 * k, t=T[nm][:, 4 * l:4 * l + 4]: eng.dma_start(T.hi40[:, o:o + 4], t), (), ("%s%d" % (nm, l),), sem="ld_h", val=32 * (L - 1), lat=7.5)
-    HT = ["%s%d" % (nm, l) for l in range(L - 1) for nm in ("ha", "hb")]
+        ctx[0] = ("setup", 0, 0, len(ops) * 1e-3 - 1)
+        add(q, 0.1, lambda: eng.dma_start(out, in_), (), (key,), sem="ld_" + key, val=16, lat=lat)
+    load("SY", "lo", T.lh[:, 0:4], T.lo0[:], 1.8)
+    load("S", "hi", T.lh[:, 4:8], T.hi0[:], 1.8)
+    load("S", "x", T.x0[:], T.xrow[:], 2.0)
+    load("SY", "home", T.hm[:], T.home[:], 2.0)
+    load("SY", "ha", T.hab[:, 0:20], T.ha[:], 2.0)
+    load("S", "hb", T.hab[:, 20:40], T.hb[:], 2.0)
+    load("SY", "y", T.yt[:], T.ytab[:], COST["YT"])
 
-    ms(T.ones[:], 1.0, ["ones"], 128)
-    def aff(out, in_, pat, op, base, cm, r, w): add("G", 0.4, lambda: G.affine_select(out, in_, pat, op, 0.0, base, cm), r, w)
-    add("G", 0.25, lambda: G.iota(T.etab[:], [[1, 64]], 0, 0, allow_small_or_imprecise_dtypes=True), (), ["etab"])
-    aff(T.idm[:], T.ones[:], [[-1, 128]], A.is_equal, 0, 1, ["ones"], ["idm"])
-    aff(T.bo1[:], T.ones[:], [[-16, 8], [0, 16]], A.is_ge, 0, 1, ["ones"], ["bo1"])
-    aff(T.bo[:], T.bo1[:], [[16, 8], [0, 16]], A.is_ge, 15, -1, ["bo1"], ["bo"])
-    add("G", 0.35, lambda: G.iota(T.e0[:], [[0, 8], [1, 16]], 0, 0, allow_small_or_imprecise_dtypes=True), (), ["e0"])
-    add("G", 0.15, lambda: G.iota(T.cli[:], [[1, 4]], 0, 0), (), ["cli"])
-    cp(T.clist[:], T.cli[:], ["cli"], ["clist"], 4)
-    ms(T.seg[:], -1.0, ["seg0"], 64)
-    ms(T.seg[:, 0:1], BIG, ["seg"], 1, ["seg0"])
-    tt(T.m1[:], T.idm[:, 0:64], T.idm[:, 64:128], A.add, ["idm"], ["m1"], 64)
-    tt(T.m2[:], T.m1[:, 0:32], T.m1[:, 32:64], A.add, ["m1"], ["m2"], 32)
-    tt(T.mk[:, 0:16], T.m2[:, 0:16], T.m2[:, 16:32], A.add, ["m2"], ["mk16"], 16)
-    cp(T.mk[:, 16:32], T.mk[:, 0:16], ["mk16"], ["mk32"], 16)
-    cp(T.mk[:, 32:64], T.mk[:, 0:32], ["mk16", "mk32"], ["mk"], 32)
-    add("V", sv(8), lambda: V.tensor_reduce(T.col[:, 0:1], T.mk[:, 1:16:2], AxisListType.X, A.add), ["mk16"], ["odd"])
-    ts(T.col[:, 1:2], T.col[:, 0:1], 2.0, -1.0, A.mult, A.add, ["odd"], ["sgn"], 1)
-    tt(T.col[:, 2:3], T.mk[:, 0:1], T.mk[:, 1:2], A.add, ["mk16"], ["ab"], 1)
-    ts(T.col[:, 3:4], T.mk[:, 0:1], -64.0, None, A.mult, None, ["mk16"], ["a64_0"], 1)
-    for c in range(1, 4):
-        ts(T.col[:, 3 + c:4 + c], T.col[:, 2:3], 16.0 * c, T.col[:, 3:4], A.mult, A.add, ["ab", "a64_0"], ["a64_%d" % c], 1)
+    ctx[0] = ("setup", 0, 0, 0)
+    def iota(out, pat, cm, tok, n, fl=True):
+        if fl: add("G", 0.13 + 2 * n * CY, lambda: G.iota(out, pat, 0, cm, allow_small_or_imprecise_dtypes=True), (), [tok])
+        else: add("G", 0.13 + 2 * n * CY, lambda: G.iota(out, pat, 0, cm), (), [tok])
+    iota(T.pi[:], [[512, 2], [128, 2], [256, 2]], 1, "pi", 8, False)
+    iota(T.gtab[:], [[16, 8], [0, 16]], 0, "gtab", 128)
+    iota(T.ctab[:], [[1, 160]], 0, "ctab", 160)
+    iota(T.e0[:], [[0, 8], [1, 16]], 0, "e0", 128)
+    iota(T.t2[:], [[0, 4], [1, 16], [0, 2]], 0, "t2", 128)
+    etab = T.ctab[:, 0:64]
+    ts(T.pj[:, 0:8], T.pi[:], 15, None, A.bitwise_and, None, ["pi"], ["pj0"], 8)
+    ts(T.pj[:, 8:16], T.pi[:], 7, None, A.arith_shift_right, None, ["pi"], ["pj1"], 8)
+    ts(T.pj[:, 16:17], T.pi[:, 0:1], 112, None, A.bitwise_and, None, ["pi"], ["pj2"], 1)
+    ts(T.pj[:, 17:18], T.pi[:, 0:1], 127, None, A.bitwise_and, None, ["pi"], ["pj3"], 1)
+    cp(T.hr[:, 0:8], T.pj[:, 0:8], ["pj0"], ["hr0"], 8)
+    cp(T.hl[:, 0:8], T.pj[:, 8:16], ["pj1"], ["hl0"], 8)
+    f16, g16, pp, zc, ab = [T.col[:, k:k + 1] for k in range(5)]
+    cp(f16, T.pj[:, 0:1], ["pj0"], ["f16"], 1)
+    cp(T.col[:, 1:3], T.pj[:, 16:18], ["pj2", "pj3"], ["g16", "pp"], 2)
+    ts(zc, g16, 15.0, None, A.add, None, ["g16"], ["zc"], 1)
+    ts(ab, f16, 2.0, 1.0 / 64, A.is_lt, A.mult, ["f16"], ["ab"], 1)
+    ts(T.col[:, 5:6], f16, 0.0, -1.0, A.is_equal, A.mult, ["f16"], ["a0"], 1)
+    ts(T.col[:, 6:10], T.ctab[:, 0:64:16], ab, T.col[:, 5:6], A.mult, A.add, ["ctab", "ab", "a0"], ["a64"], 4)
+    def table(nm, src, tok, c, ctok, v, n=128, sl=slice(None)):
+        ts(T[nm][:, sl], T[src][:, sl], c, v, A.is_equal, A.mult, [src, ctok], [tok], n)
+    table("bos", "gtab", "bosA", g16, "g16", -1.0, 64, slice(0, 128, 2))
+    table("bos", "gtab", "bosB", g16, "g16", 1.0, 64, slice(1, 128, 2))
+    for nm, v in (("bo", 1.0), ("bop", 1.0 / 64), ("bon", -1.0 / 64)): table(nm, "gtab", nm, g16, "g16", v)
+    for nm, v in (("idb", 1.0), ("idh", 1.0), ("i64", 64.0)):
+        ts(T[nm][:], T.ctab[:, 0:128], pp, v, A.is_equal, A.mult, ["ctab", "pp"], [nm], 128)
+    table("zs", "ctab", "zs", zc, "zc", 64.0, 160)
+    for nm, src, v, n in (("zr", "zs", 2.0, 160), ("zd", "zs", -1.0, 160), ("idn", "idb", -1.0, 128)):
+        act(T[nm][:], T[src][:], [src], [nm], n, scale=v, f=F.Identity)
     for c in range(4):
         q = T.qt[:, 128 * c:128 * c + 128]
-        act(q, T.e0[:], ["e0", "ab", "a64_%d" % c], ["qt%d" % c], 128, bias=T.col[:, 3 + c:4 + c], scale=T.col[:, 2:3], f=F.Identity)
-        tt(T.qw[:, 128 * c:128 * c + 128], q, T.bo[:], A.mult, ["qt%d" % c, "bo"], ["qw%d" % c], 128)
+        act(q, T.e0[:], ["e0", "ab", "a64"], ["qt%d" % c], 128, bias=T.col[:, 6 + c:7 + c], scale=ab, f=F.Identity)
+        tt(T.qw[:, 128 * c:128 * c + 128], q, T.bo[:], A.mult, ["qt%d" % c, "bo"], ["qw%d" % c], 128, 1.0)
     QWT = ["qw%d" % c for c in range(4)]
-    ts(T.bos[:, 0:128:2], T.bo[:, 0:128:2], -1.0, None, A.mult, None, ["bo"], ["bosA"], 64)
-    cp(T.bos[:, 1:128:2], T.bo[:, 1:128:2], ["bo"], ["bosB"], 64)
-    act(T.idb[:], T.idm[:], ["idm"], ["idb"], 128, f=F.Identity)
-    for nm, c in (("zs", 64.0), ("zr", 128.0), ("zd", -64.0)):
-        ms(T[nm][:], 0.0, [nm + "0"], 160)
-        act(T[nm][:, 15:143:16], T.bo[:, 0:128:16], ["bo", nm + "0"], [nm], 8, scale=c, f=F.Identity)
-    ts(T.i64[:], T.idm[:], 64.0, None, A.mult, None, ["idm"], ["i64"], 128)
-    ts(T.nst[:], T.e0[:], 0.0, None, A.is_gt, None, ["e0"], ["nst"], 128)
-    for k in range(2):
-        act(T.mks[:, 64 * k:64 * k + 64], T.mk[:], ["mk16", "mk32", "mk", "sgn"], ["mks%d" % k], 64, scale=T.col[:, 1:2], f=F.Identity)
+    ts(T.c1[:, 128:256], T.t2[:], f16, -OFF, A.not_equal, A.mult, ["t2", "f16"], ["c1b"], 128)
+    ts(T.c1[:, 0:128], T.c1[:, 128:256], -1.0, 2048.0, A.mult, A.max, ["c1b"], ["c1a"], 128, 0.5)
+    ts(T.c2[:], T.gtab[:], 0.0, -DL, A.mult, A.add, ["gtab"], ["c2"], 128)
+    iota(T.zero[:], [[0, 128]], 0, "zero", 128)
+    ts(T.m16[:], T.ctab[:, 0:16], f16, None, A.is_equal, None, ["ctab", "f16"], ["m16"], 16)
+    for nm, n, st, v0, v1 in (("seg", 128, 64, -1.0, BIG), ("sgp", 64, 32, 0.0, BIG), ("sgn", 64, 32, 0.0, -BIG), ("sgz", 64, 2, 0.0, -BIG)):
+        ms(T[nm][:], v0, [nm + "0"], n)
+        ms(T[nm][:, 0:n:st], v1, [nm], n // st, [nm + "0"])
 
-    for k, nm in ((0, "lo"), (4, "hi")):
-        ts(T.lob[:, k:k + 4], T.lh[:, k:k + 4], -2048.0, 1.0 / 64, A.add, A.mult, [nm], [nm + "b"], 4)
-    cp(T.hf[:], T.hm[:], ["hm"], ["hf"], 24)
-    ts(T.h1[:], T.hi40[:], 384.0, -384.0, A.is_ge, A.mult, HT, ["h1"], 40)
-    tt(T.h2[:], T.hi40[:], T.h1[:], A.add, HT + ["h1"], ["h2"], 40)
-    ts(T.h3[:], T.h2[:], 960, None, A.bitwise_and, None, ["h2"], ["h3"], 40)
+    ts(T.lob[:], T.lh[:], -2048.0, None, A.add, None, ["lo", "hi"], ["lob"], 8)
+    for k, a in enumerate(BLK): cp(T.hf[:, k:24:4], T.hm[:, a:24:4], ["home"], ["hf%d" % k], 6)
+    HF = ["hf%d" % k for k in range(4)]
+    def masks(l, tok):
+        act(T.mk[:, 128 * l:128 * l + 128], T.m16[:].indirect(T.hr[:, 8 * l:8 * l + 8]), ["m16", tok], ["mk%d" % l], 128, f=F.Identity, gather=True)
+    masks(0, "hr0")
+    ctx[0] = ("hints", 0, 0, 0); HT = []
+    for h, nm in enumerate(("ha", "hb")):
+        for k, a in enumerate(BLK):
+            cp(T.h1[:, 4 * h + k:40:8], T.hab[:, 20 * h + a:20 * h + 20:4], [nm], ["h1.%d%d" % (h, k)], 5); HT.append("h1.%d%d" % (h, k))
+    ts(T.h2[:], T.h1[:], 4, None, A.arith_shift_right, None, HT, ["h2"], 40)
+    ts(T.h3[:], T.h2[:], 24.0, -24.0, A.is_ge, A.mult, ["h2"], ["h3"], 40)
     tt(T.h4[:], T.h2[:], T.h3[:], A.add, ["h2", "h3"], ["h4"], 40)
-    ts(T.h5[:], T.h1[:], -1.0 / 6, None, A.mult, None, ["h1"], ["h5"], 40)
-    tt(T.h6[:], T.h4[:], T.h5[:], A.add, ["h4", "h5"], ["h6"], 40)
-    cp(T.hl[:], T.h6[:], ["h6"], ["hl"], 40)
-    cp(T.hs[:], T.h6[:, 0:40:2], ["h6"], ["hs"], 20)
+    ts(T.h5[:], T.h4[:], 28, None, A.bitwise_and, None, ["h4"], ["h5"], 40)
+    ts(T.h3[:], T.h2[:], 24.0, -20.0, A.is_ge, A.mult, ["h2"], ["h3"], 40)
+    tt(T.h6[:], T.h2[:], T.h3[:], A.add, ["h2", "h3"], ["h6"], 40)
+    tt(T.h4[:], T.h5[:], T.h6[:], A.add, ["h5", "h6"], ["h4"], 40)
+    cp(T.hl[:, 8:48], T.h4[:], ["h4"], ["hl"], 40)
+    ts(T.h7[:], T.h1[:], 15, None, A.bitwise_and, None, HT, ["h7"], 40)
+    cp(T.hr[:, 8:48], T.h7[:], ["h7"], ["hr"], 40)
+    for l in range(1, L): masks(l, "hr")
 
-    def xtok(p, l, a): return "x0" if p == 0 else "x1.%d.%d" % (l, a)
-    reptok = {}
-    def reps(p, l, u):
-        vb = CFG[p, l][0][u][1]; ctx[0] = ("reps", p, l, u)
-        o = 2 * CH * l + CH * u; t = "rep%d.%d.%d" % (p, l, u)
-        x = T["x%d" % p]; q = 1 - p; nb = len(vb); n = 16
-        def mm():
-            return [TE.matmul(T["Q%d" % q][:, k:k + n], T.idb[:], x[:, 64 * l + 16 * vb[k // n % nb]:64 * l + 16 * vb[k // n % nb] + n], True, True) for k in range(0, CH, n)]
-        add("T", CH // n * 64 * PE, mm, ["idb"] + [xtok(p, l, a) for a in vb], ["Q%d" % q], n=CH // n)
-        act(T["rep%d" % p][:, o:o + CH], T["Q%d" % q][:, 0:CH], ["Q%d" % q], [t], CH, f=F.Identity)
-        reptok[p, l, u] = [t]
-
-    def lists(p, s, l, lotok):
-        sc = T["sc%d" % s]; t = "sc%d." % s
-        lo, hi = (T.lob[:, 0:4], T.lob[:, 4:8]) if s == 2 else (sc[:, 0:4], sc[:, 4:8])
-        tt(sc[:, 8:12], hi, lo, A.subtract, lotok, [t + "D"], 4)
-        ts(sc[:, 12:16], lo, 64.0, CJ, A.mult, A.add, lotok, [t + "B1"], 4)
-        tt(sc[:, 16:20], sc[:, 12:16], T.hf[:, 4 * l:4 * l + 4], A.subtract, [t + "B1", "hf"], [t + "B2"], 4)
-        pa = T["pa%d" % s]; po = 0; vo = 0; pt = []
-        for sb, vb in CFG[p, l][0]:
-            nb = len(vb); o = po + 64 * len(sb)
-            for k, a in enumerate(vb):
-                ts(T["ofv%d" % s][:, vo + k:vo + 64 * nb:nb], T.etab[:], sc[:, 8 + a:9 + a], sc[:, 12 + a:13 + a], A.mult, A.add, ["etab", t + "D", t + "B1"], ["ofv%d.%d" % (s, a)], 64)
-            for k, a in enumerate(sb + vb):
-                out = pa[:, po + 64 * k:po + 64 * k + 64] if a in sb else pa[:, o + k - len(sb):o + 64 * nb:nb]
-                act(out, T.etab[:], ["etab", t + "D", t + "B2"], ["pa%d.%d" % (s, a)], 64, bias=sc[:, 16 + a:17 + a], scale=sc[:, 8 + a:9 + a])
-                pt.append("pa%d.%d" % (s, a))
-            po = o + 64 * nb; vo += 64 * nb
-        ts(T["pn%d" % s][:], pa[:], 1.0 / 16, 1280.0 - 15.0 / 32, A.mult, A.add, pt, ["pn%d" % s], 256)
-
-    def slist(s, p):
-        def mm():
-            return [TE.matmul(T["Q%d" % p][:, c:128:4], T.qw[:, 128 * c:128 * c + 128], T["z%d" % p][:], True, True) for c in range(4)]
-        add("T", 4 * 64 * PE, mm, QWT + ["z%d" % p], ["Q%d" % p], n=4)
-        ts(T["ofs%d" % s][:], T["Q%d" % p][:, 0:128], CJ, None, A.add, None, ["Q%d" % p], ["ofs%d" % s], 128)
-
-    def prep0():
-        ctx[0] = ("prep", 0, 0, 0); r = []
-        for k, nm in ((0, "lob"), (1, "hib")):
-            for j, a in enumerate(SBL):
-                ts(T.dg0[:, 32 * k + 16 * j:32 * k + 16 * j + 16], T.mk[:, 0:16], T.lob[:, 4 * k + a:4 * k + a + 1], None, A.mult, None, ["mk16", nm], ["dg0.%d%d" % (k, a)], 16)
-                r.append("dg0.%d%d" % (k, a))
-        add("T", 0.05, lambda: TE.matmul(T.KN1[:, 0:64], T.bos[:], T.dg0[:, 0:64], True, True), ["bosA", "bosB"] + r, ["KN1"])
-        cp(T.vz0[:], T.KN1[:, 32:64], ["KN1"], ["vz0"], 32)
-        tt(T.z0[:], T.KN1[:, 0:32], T.vz0[:], A.max, ["KN1", "vz0"], ["z0"], 32, 1.0)
-        slist(2, 0)
-        lists(0, 2, 0, ["lob", "hib"])
-
-    def prep(p, l):
-        ctx[0] = ("prep", p, l, 0); w = T["win%d" % p]; win = w[:, 0:128 * l]; sc = T["sc%d" % p]
-        wt = ["w%d.%d.%s" % (p, k, x) for k in range(l) for x in ("own", "rem")]
-        h = 8 * (l - 1); hh = 4 * (l - 1)
-        um, us, vz, z = T["um%d" % p], T["us%d" % p], T["vz%d" % p], T["z%d" % p]
-        tt(um[:], win.indirect(T.hl[:, h:h + 8]), T.mks[:], A.mult, wt + ["hl", "mks0", "mks1"], ["um%d" % p], 128, gather=True)
-        scan(us[:], T.nst[:], um[:], 0.0, A.mult, A.add, ["nst", "um%d" % p], ["us%d" % p], 128)
-        cp(vz[:], win.indirect(T.hs[:, hh + 2:hh + 4]), wt + ["hs"], ["vz%d" % p], 32, gather=True)
-        tt(z[:], win.indirect(T.hs[:, hh:hh + 2]), vz[:], A.max, wt + ["hs", "vz%d" % p], ["z%d" % p], 32, gather=True)
-        u, v = us[:, 15:64:16], us[:, 79:128:16]
-        tt(sc[:, 0:4], u, v, A.min, ["us%d" % p], ["sc%d.lo" % p], 4)
-        tt(sc[:, 4:8], u, v, A.max, ["us%d" % p], ["sc%d.hi" % p], 4)
-        slist(p, p)
-        lists(p, p, l, ["sc%d.lo" % p, "sc%d.hi" % p])
+    def reps0():
+        ctx[0] = ("reps", 0, 0, 0); n = 2 * L
+        cp(T.rep0[:, :, 0:32], T.x0[:], ["x"], ["rep.16"], 32 * n, 0.5)
+        k = 16
+        while k < CH:
+            cp(T.rep0[:, :, 16 + k:16 + 2 * k], T.rep0[:, :, 16:16 + k], ["rep.%d" % k], ["rep.%d" % (2 * k)], k * n, 0.5)
+            k *= 2
+    REP = "rep.%d" % CH
 
     def sets(p, l): return 2 if l == 0 else p
+    def B1(s, k): return T["ls%d" % s][:, 32 * k + 31:32 * k + 32]
+    def DD(s, k): return T["ls%d" % s][:, 128 + 32 * k + 31:128 + 32 * k + 32]
 
-    def keys(p, l, u):
-        sb, vb = CFG[p, l][0][u]
-        return ["s%d.%d" % (a, i) for a in sb for i in range(16)] + ["v%s%d" % (k, h) for k in "dr" for h in range(len(vb))]
+    def prep(p, l):
+        s = sets(p, l); P = "%d" % p; t = "%d." % s; Rb = T["R" + P]; rh = T["rh" + P]; z = T["z" + P]; ls = T["ls%d" % s]; sc = T["sc%d" % s]
+        at = 0 if l else -2 * p
+        ctx[0] = ("const", p, l, at)
+        mms([(Rb[:, 0:256], T.idh[:], T.c1[:], 256, True, False), (Rb[:, 0:128], T.idh[:], T.c2[:], 128, False, False)], ["idh", "c1a", "c1b", "c2"], ["R" + P])
+        ctx[0] = ("z", p, l, at)
+        if l == 0: win, wt = T.lob[:], ["lob", "hl0"]
+        else: win, wt = T["win" + P][:, 0:8 * l], ["hl"] + ["w%d.%d.%d" % (p, k, x) for k in range(l) for x in range(5)]
+        tt(rh[:], win.indirect(T.hl[:, 8 * l:8 * l + 8]), T.mk[:, 128 * l:128 * l + 128], A.mult, wt + ["mk%d" % l], ["rh" + P], 128, gather=True)
+        mms([(T.Z[:, h:64:2], T.bos[:], rh[:, 64 * h:64 * h + 32], 32, True, True) for h in range(2)], ["bosA", "bosB", "rh" + P], ["Z"])
+        scan(z[:], T.sgz[:], T.Z[:, 0:64], A.max, ["sgz", "Z"], ["z" + P], 64)
+        mms([(T.Z[:, 64 + c:192:4], T.qw[:, 128 * c:128 * c + 128], z[:, 1:64:2], 32, True, True) for c in range(4)], QWT + ["z" + P], ["Z"])
+        ts(T["ofs%d" % s][:], T.Z[:, 64:192], 2048.0 - DL, None, A.add, None, ["Z"], ["ofs%d" % s], 128)
+        ctx[0] = ("prep", p, l, at)
+        a, b = rh[:, 0:64], rh[:, 64:128]
+        mms([(Rb[:, 0:128:2], T.bo[:], a, 64, False, False), (Rb[:, 1:128:2], T.bo[:], b, 64, False, False),
+             (Rb[:, 128:256:2], T.bop[:], a, 64, False, False), (Rb[:, 128:256:2], T.bon[:], b, 64, False, False),
+             (Rb[:, 129:256:2], T.bon[:], a, 64, False, False), (Rb[:, 129:256:2], T.bop[:], b, 64, False, True)], ["bo", "bop", "bon", "rh" + P, "R" + P], ["R" + P])
+        for h in (1, 0):
+            scan(ls[:, 64 * h:64 * h + 64], T.sgp[:], Rb[:, 64 * h:64 * h + 64], A.min, ["sgp", "R" + P], [t + "B%d" % h], 64)
+            scan(ls[:, 128 + 64 * h:192 + 64 * h], T.sgn[:], Rb[:, 128 + 64 * h:192 + 64 * h], A.max, ["sgn", "R" + P], [t + "D%d" % h], 64)
+        for u in range(2):
+            ts(T["ofv%d" % s][:, 64 * u:64 * u + 64], etab, DD(s, 2 + u), B1(s, 2 + u), A.mult, A.add, ["ctab", t + "B1", t + "D1"], ["ofv%d.%d" % (s, u)], 64)
+        ctx[0] = ("pen", p, l, at); bt = [t + "B0", t + "B1"]
+        act(sc[:, 0:4], ls[:, 31:128:32], bt, [t + "C"], 4, bias=-2048.0, f=F.Identity)
+        tt(sc[:, 4:8], ls[:, 31:128:32], T.hf[:, 4 * l:4 * l + 4], A.subtract, bt + HF, [t + "H"], 4)
+        pa = T["pa%d" % s]
+        for k in range(4):
+            o = 128 * (k % 2) + 64 * (k // 2)
+            act(pa[:, o:o + 64], etab, ["ctab", t + "D%d" % (k // 2), t + "H"], ["pa%d.%d" % (s, k)], 64, bias=sc[:, 4 + k:5 + k], scale=DD(s, k))
+        ts(T["pn%d" % s][:], pa[:], 1.0 / 16, 1280.0 - 15.0 / 32, A.mult, A.add, ["pa%d.%d" % (s, k) for k in range(4)], ["pn%d" % s], 256)
+
+    KEYS = ["s%d" % i for i in range(16)] + ["d", "r", "p"]
 
     def search(p, l, u):
-        ctx[0] = ("search", p, l, u); s = sets(p, l); units = CFG[p, l][0]
-        sb, vb = units[u]; nb = len(vb)
-        po = sum(64 * len(a + b) for a, b in units[:u]); vo = sum(64 * len(b) for a, b in units[:u])
-        K = T["K%d%d" % (p, u)]; kt = lambda x: "K%d%d.%s" % (p, u, x)
-        x = T["x%d" % p]; w = 64 * (len(sb) + nb); ko = 64 * len(sb)
-        grp = (p, l, u)
-        kx = [kt(q) for q in keys(p, l, u)]
-        add("T", w * PE, lambda: TE.matmul(K[:, 0:w], T.i64[:], T["pn%d" % s][:, po:po + w], True, False), ["i64", "pn%d" % s], kx + [kt("0")])
-        for j, a in enumerate(sb):
-            for i in range(16):
-                r = 16 * SBL.index(a) + i
-                o = T["as%d" % p][:, 64 * r:64 * r + 64]
-                add("S", 0.065 + 64 * GE, lambda o=o, r=r, a=a, i=i: S.activation(o, T.yt[:].indirect(T["ofs%d" % s][:, 4 * r:4 * r + 4]), F.Abs, bias=x[:, 64 * l + 16 * a + i:64 * l + 16 * a + i + 1], scale=-1.0),
-                    ["yt", "ofs%d" % s, xtok(p, l, a)], ["as%d.%d" % (p, r)])
-                add("T", 64 * PE, lambda stop, o=o, j=j, i=i: TE.matmul(K[:, 64 * j:64 * j + 64], T.zs[:, 15 - i:143 - i], o, False, stop), ["zs", "as%d.%d" % (p, r), kt("0")], [kt("s%d.%d" % (a, i))], grp=grp)
-        nc = 64 * 16 * nb // CH
-        dv, rv = T["dv%d" % p], T["rv%d" % p]
-        for h in range(nb):
-            cs = range(h * nc // nb, (h + 1) * nc // nb)
-            for c in cs:
-                d = 16 * vo + CH * c
-                tt(dv[:, d:d + CH], T.yt[:].indirect(T["ofv%d" % s][:, vo + CH // 16 * c:vo + CH // 16 * (c + 1)]), T["rep%d" % p][:, 2 * CH * l + CH * u:2 * CH * l + CH * u + CH], A.subtract,
-                   ["yt"] + ["ofv%d.%d" % (s, a) for a in vb] + reptok[p, l, u], ["dv%d.%d" % (p, d)], CH, gather=True)
-                if c % 2 == 1:
-                    d -= CH; ctx[0] = ("relu", p, l, u)
-                    ts(rv[:, d:d + 2 * CH], dv[:, d:d + 2 * CH], 0.0, None, A.max, None, ["dv%d.%d" % (p, d), "dv%d.%d" % (p, d + CH)], ["rv%d.%d" % (p, d)], 2 * CH, 0.5)
-                    ctx[0] = ("search", p, l, u)
-            d0 = 16 * vo + CH * cs[0]; d1 = 16 * vo + CH * (cs[-1] + 1)
-            for kind, buf, z in (("d", dv, "zd"), ("r", rv, "zr")):
-                toks = ["%sv%d.%d" % (kind, p, q) for q in range(d0, d1, CH if kind == "d" else 2 * CH)]
-                def mm(stop, h=h, buf=buf, z=z, d0=d0, d1=d1):
-                    return [TE.matmul(K[:, ko + 64 * h:ko + 64 * h + 64], T[z][:, 15 - i:143 - i], buf[:, d0 + i:d1:16], False, stop and i == 15) for i in range(16)]
-                add("T", 16 * 64 * PE, mm, [z, kt("0")] + toks, [kt("v%s%d" % (kind, h))], n=16, grp=grp)
+        ctx[0] = ("search", p, l, u); s = sets(p, l)
+        K = T["K%d%d" % (p, u)]; kt = lambda x: "K%d%d.%s" % (p, u, x); grp = (p, l, u)
+        xt = "x" if p == 0 else "xr%d.%d" % (l, u); o1 = 2 * l + u
+        mms([(K[:, 0:128], T.idb[:], T.zero[:], 128, True, False)], ["idb", "zero"], [kt(q) for q in KEYS] + [kt("0")])
+        mms([(K[:, 0:128], T.i64[:], T["pn%d" % s][:, 128 * u:128 * u + 128], 128, False, None)], ["i64", "pn%d" % s, kt("0")], [kt("p")], grp)
+        for i in range(16):
+            ctx[0] = ("search", p, l, u + i / 16)
+            r = 16 * u + i; o = T["as%d" % p][:, 64 * r:64 * r + 64]
+            act(o, T.yt[:].indirect(T["ofs%d" % s][:, 4 * r:4 * r + 4]), ["y", "ofs%d" % s, xt], ["as%d.%d" % (p, r)], 64,
+                bias=T["xr" if p else "x0"][:, o1, i:i + 1], scale=-1.0, gather=True)
+            mms([(K[:, 0:64], T.zs[:, 15 - i:143 - i], o, 64, False, None)], ["zs", "as%d.%d" % (p, r), kt("0")], [kt("s%d" % i)], grp)
+        shared = OPT["share"] and p == 1 and l == 0
+        pd = 0 if shared else p
+        dv, rv = T["dv%d" % pd], T["rv%d" % p]; d0 = 1024 * u; nr = OPT["nrelu"]
+        rep = T["xr" if p else "rep0"][:, o1, 16:XW]
+        rt = REP if p == 0 else xt
+        if shared:
+            Rb = T["R%d" % u]
+            mms([(Rb[:, 0:CH], T.idb[:], rep, CH, True, False), (Rb[:, 0:CH], T.idn[:], T.rep0[:, o1, 16:XW], CH, False, True)], ["idb", "idn", rt, REP], ["R%d" % u])
+        for c in range(1024 // CH):
+            d = d0 + CH * c; ctx[0] = ("search", p, l, u + c * CH / 1024 - PRI["v"])
+            if shared:
+                tt(rv[:, d:d + CH], dv[:, d:d + CH], Rb[:, 0:CH], A.max, ["dv0.%d" % d, "R%d" % u], ["rv1.%d" % d], CH, 1.0)
+                continue
+            tt(dv[:, d:d + CH], T.yt[:].indirect(T["ofv%d" % s][:, 64 * u + CH // 16 * c:64 * u + CH // 16 * (c + 1)]), rep, A.subtract,
+               ["y", "ofv%d.%d" % (s, u), rt], ["dv%d.%d" % (p, d)], CH, gather=True)
+            if c % nr == nr - 1:
+                e = d - (nr - 1) * CH; ctx[0] = ("search", p, l, u + (c + PRI["relu"]) * CH / 1024 - PRI["v"]); ds = range(e, d + CH, CH)
+                ts(rv[:, e:d + CH], dv[:, e:d + CH], 0.0, None, A.max, None, ["dv%d.%d" % (p, q) for q in ds], ["rv%d.%d" % (p, q) for q in ds], nr * CH, 0.5)
+        ctx[0] = ("search", p, l, u + PRI["mv"])
+        for kind, buf, z, pb in (("d", dv, "zd", pd), ("r", rv, "zr", p)):
+            mms([(K[:, 64:128], T[z][:, 15 - i:143 - i], buf[:, d0 + i:d0 + 1024:16], 64, False, None) for i in range(16)],
+                [z, kt("0")] + ["%sv%d.%d" % (kind, pb, q) for q in range(d0, d0 + 1024, CH)], [kt(kind)], grp)
 
     def post(p, l, us):
-        ctx[0] = ("post", p, l, us[0]); s = sets(p, l); units = CFG[p, l][0]
-        ks, sc = T["ks%d" % p], T["sc%d" % s]; P = "%d" % p
-        bl = []; kst = []
+        ctx[0] = ("post", p, l, us[0]); s = sets(p, l); P = "%d" % p; ks = T["ks" + P]; t = "%d." % s; w = T["win" + P]
         for u in us:
-            sb, vb = units[u]; K = T["K%d%d" % (p, u)]; ko = 64 * len(sb); nb = len(vb)
-            kt = ["K%d%d.%s" % (p, u, q) for q in keys(p, l, u)]
-            for j, a in enumerate(sb + vb):
-                src = K[:, 64 * j:64 * j + 64] if a in sb else K[:, ko + j - len(sb):ko + 64 * nb:nb]
-                scan(ks[:, 64 * a:64 * a + 64], T.seg[:], src, BIG, A.add, A.min, kt + ["seg"], ["ks%d.%d" % (p, a)], 64)
-                kst.append("ks%d.%d" % (p, a)); bl.append(a)
-        bl.sort(); c0, c1 = bl[0], bl[-1] + 1; n = c1 - c0; q = P + ".%d" % c0
-        c = slice(c0, c1); wall = T.wall[:, 24 * p + 4 * l + c0:24 * p + 4 * l + c1]
-        ts(T["ki" + P][:, c], ks[:, 64 * c0 + 63:64 * c1:64], 63.0, None, A.add, None, kst, ["ki" + q], 4)
-        ts(T["ei" + P][:, c], T["ki" + P][:, c], 63, None, A.bitwise_and, None, ["ki" + q], ["ei" + q], 4)
-        tt(T["tf" + P][:, c], T["ei" + P][:, c], sc[:, 8 + c0:8 + c1], A.mult, ["ei" + q, "sc%d.D" % s], ["tf" + q], 4)
-        ctx[0] = ("win", p, l, us[0]); wt = "wall%d.%d.%d" % (p, l, c0)
-        tt(wall, T["tf" + P][:, c], sc[:, 12 + c0:12 + c1], A.add, ["tf" + q, "sc%d.B1" % s], [wt], 4)
-        ctx[0] = ("xup", p, l, us[0])
-        cp(T["wo" + P][:, 2 * c0:2 * c0 + n], wall, [wt], ["wo" + q], 4)
-        r0, r1 = 64 * l + 16 * c0, 64 * l + 16 * c1
-        tt(T["dx" + P][:, 16 * c0:16 * c1], T.yt[:].indirect(T["wo" + P][:, 2 * c0:2 * c0 + n]), T["x" + P][:, r0:r1], A.subtract, ["yt", "wo" + q] + [xtok(p, l, a) for a in bl], ["dx" + q], 16 * n, gather=True)
-        if p == 0:
-            act(T.x1[:, r0:r1], T.dx0[:, 16 * c0:16 * c1], ["dx" + q], [xtok(1, l, a) for a in bl], 16 * n)
-        else:
-            act(T.xf[:, r0:r1], T.dx1[:, 16 * c0:16 * c1], ["dx" + q], ["xf.%d.%d" % (l, a) for a in bl], 16 * n)
-        return wt
+            scan(ks[:, 128 * u:128 * u + 128], T.seg[:], T["K%d%d" % (p, u)][:, 0:128], A.min, ["K%d%d.%s" % (p, u, q) for q in KEYS] + ["seg"], ["ks%d.%d" % (p, u)], 128)
+        c0, c1 = 2 * us[0], 2 * us[-1] + 2; c = slice(c0, c1)
+        kk, ee = ["ki%d.%d" % (p, u) for u in us], ["ei%d.%d" % (p, u) for u in us]
+        ts(T["ki" + P][:, c], ks[:, 64 * c0 + 63:64 * c1:64], 63.0 + 64 * 8192, None, A.add, None, ["ks%d.%d" % (p, u) for u in us], kk, 4)
+        ts(T["ei" + P][:, c], T["ki" + P][:, c], 63, None, A.bitwise_and, None, kk, ee, 4)
+        for a in range(c0, c1):
+            k = BLK.index(a)
+            ts(w[:, 8 * l + a:8 * l + a + 1], T["ei" + P][:, a:a + 1], DD(s, k), T["sc%d" % s][:, k:k + 1], A.mult, A.add, ee + [t + "D%d" % (k // 2), t + "C"], ["w%d.%d.%d" % (p, l, a)], 1)
 
-    def known(p, l, wts):
-        ctx[0] = ("known", p, l, 0); P = "%d" % p; dg = T["dg%d" % (p + 1)]; w = T["win" + P]
-        ts(T["wf" + P][:, 0:4], T.wall[:, 24 * p + 4 * l:24 * p + 4 * l + 4], -2048.0, 1.0 / 64, A.add, A.mult, wts, ["wf" + P], 4)
-        tt(dg[:], T["wf" + P][:, 0:4].indirect(T.clist[:]), T.mk[:], A.mult, ["wf" + P, "clist", "mk16", "mk32", "mk"], ["dg%d" % (p + 1)], 64, gather=True)
-        add("T", 64 * PE, lambda: TE.matmul(T["KN" + P][:, 0:64], T.bos[:], dg[:], True, True), ["bosA", "bosB", "dg%d" % (p + 1)], ["KN" + P])
-        own = w[:, 128 * l:128 * l + 64]; ot = "w%d.%d.own" % (p, l)
-        cp(own, T["KN" + P][:, 0:64], ["KN" + P], [ot], 64)
+    def left(p, l, us):
+        ctx[0] = ("xup" if p == 0 else "late", p, l, us[0]); P = "%d" % p; c0, c1 = 2 * us[0], 2 * us[-1] + 2
+        wk = ["wo%d.%d" % (p, u) for u in us]; yk = ["dx%d.%d" % (p, u) for u in us]
+        ts(T["wo" + P][:, c0:c1], T["win" + P][:, 8 * l + c0:8 * l + c1], 2048.0, None, A.add, None, ["w%d.%d.%d" % (p, l, a) for a in range(c0, c1)], wk, 4)
+        yw = T["dx" + P]; n = 16 * (c1 - c0); o = 16 * c0
+        act(yw[:, o:o + n], T.yt[:].indirect(T["wo" + P][:, c0:c1]), ["y"] + wk, yk, n, f=F.Identity, gather=True)
+        if p == 0:
+            o1 = 2 * l + us[0]
+            mms([(T.X[:, 0:XW], T.idn[:], T.rep0[:, o1, :], XW, True, False), (T.X[:, 0:32], T.idb[:], yw[:, o:o + 32], 32, False, False)]
+                + [(T.X[:, k:k + 16], T.idb[:], yw[:, o + 16:o + 32], 16, False, k == XW - 16) for k in range(32, XW, 16)], ["idb", "idn", REP] + yk, ["X"])
+            act(T.xr[:, o1, :], T.X[:, 0:XW], ["X"], ["xr%d.%d" % (l, us[0])], XW)
+        else:
+            mms([(T.X[:, 0:n], T.idb[:], yw[:, o:o + n], n, True, False)]
+                + [(T.X[:, 32 * k:32 * k + 32], T.idn[:], T.xr[:, 2 * l + u, 0:32], 32, False, u == us[-1]) for k, u in enumerate(us)],
+                ["idb", "idn"] + yk + ["xr%d.%d" % (l, u) for u in us], ["X"])
+            act(T.xf[:, 64 * l + o:64 * l + o + n], T.X[:, 0:n], ["X"], ["xf%d.%d" % (l, u) for u in us], n)
+
+    def send(p, l):
+        ctx[0] = ("post", p, l, 0); w = T["win%d" % p]
         dst = T.cores[(rank - 1) % len(T.cores)]
         rid, pid, _ = topo.addr(dst)
         m = topo.mask(core, dst)
-        def send():
-            G.remote_dma(w[:, 128 * l + 64:128 * l + 128], own, T.sem["arr%d_%d" % (p, l)], T.sem.snt, pid, rid, m)
-        add("G", 1.0, send, [ot], ["w%d.%d.rem" % (p, l)], n=0, sem="arr%d_%d" % (p, l), val=len(topo.engines(core, dst)), lat=COST["REMOTE"])
+        def fn():
+            G.remote_dma(w[:, 8 * l + 4:8 * l + 8], w[:, 8 * l:8 * l + 4], T.sem["arr%d_%d" % (p, l)], T.sem.snt, pid, rid, m)
+        add("G", 0.5, fn, ["w%d.%d.%d" % (p, l, a) for a in range(4)], ["w%d.%d.4" % (p, l)], n=0, sem="arr%d_%d" % (p, l), val=len(topo.engines(core, dst)), lat=COST["REMOTE"])
 
     stores = [0]
-    def store(out, in_, r):
-        stores[0] += 1
-        add("SY", 0.1, lambda: SY.dma_start(out, in_), r, [], sem="st", val=None, lat=2.0)
+    def store(q, out, in_, r):
+        stores[0] += 1; eng = SY if q == "SY" else S
+        add(q, 0.1, lambda: eng.dma_start(out, in_), r, [], sem="st", val=None, lat=2.0)
 
-    prep0()
-    allw = {0: [], 1: []}
+    prep(1, 0)
+    reps0()
     for k in range(2 * L):
         p, l = k % 2, k // 2
-        units, posts = CFG[p, l]
-        if p == 0:
-            for u in range(len(units)): reps(0, l, u)
         if l: prep(p, l)
-        for u in range(len(units)):
-            if p == 1: reps(1, l, u)
-            search(p, l, u)
-        wts = [post(p, l, us) for us in posts]
-        allw[p] += wts
-        if l < L - 1: known(p, l, wts)
-        else:
-            cp(T.am[:, 24 * p:24 * p + 24], T.wall[:, 24 * p:24 * p + 24], allw[p], ["am%d" % p], 24)
-            store(T.argm[:, 24 * p:24 * p + 24], T.am[:, 24 * p:24 * p + 24], ["am%d" % p])
-        if p == 1 and l in (2, 4, 5):
-            f = {2: 0, 4: 3, 5: 5}[l]
-            store(T.xo[:, 64 * f:64 * l + 64], T.xf[:, 64 * f:64 * l + 64], ["xf.%d.%d" % (q, a) for q in range(f, l + 1) for a in range(4)])
+        for u in range(2): search(p, l, u)
+        for us in ([[0, 1]] if p and OPT["joint"] else [[0], [1]]): post(p, l, us)
+        if l < L - 1: send(p, l)
+        for us in ([[0, 1]] if p and l < L - 1 else [[0], [1]]): left(p, l, us)
+        ctx[0] = ("late", p, l, 0)
+        if l == L - 1:
+            w = T["win%d" % p]; am = T.am[:, 24 * p:24 * p + 24]
+            ts(T.am[:, 24 * p + 20:24 * p + 24], w[:, 8 * l:8 * l + 4], 2048.0, None, A.add, None, ["w%d.%d.%d" % (p, l, a) for a in range(4)], ["am%d.4" % p], 4)
+            for a in range(4):
+                ts(T.am[:, 24 * p + a:24 * p + 20:4], w[:, a:40:8], 2048.0, None, A.add, None, ["w%d.%d.%d" % (p, q, x) for q in range(L - 1) for x in (a, 4)], ["am%d.%d" % (p, a)], 5)
+            store("SY", T.argm[:, 24 * p:24 * p + 24], am, ["am%d.%d" % (p, a) for a in range(5)])
+        if p == 1 and l in (3, 4, 5):
+            f = l if l > 3 else 0
+            store("SY" if l < 5 else "S", T.xo[:, 64 * f:64 * l + 64], T.xf[:, 64 * f:64 * l + 64], ["xf%d.%d" % (q, u) for q in range(f, l + 1) for u in range(2)])
     return ops, stores
 
 
-def early(tag):
-    k, p = tag[0], tag[1]; v = 0.0
-    if k in ("prep", "post", "win", "known"): v += PRI["chain"]
-    if k in ("xup", "reps"): v += PRI["xup"]
-    if k == "relu": v += PRI["relu"]
-    if k != "setup": v += PRI["p1"] * p
-    return v
+def due(tag):
+    k, p, l, u = tag
+    return 4 * l + 2 * p + u + PRI[k]
 
 
 def plan(ops):
-    n = len(ops); WAKE = COST["WAKE"]
+    n = len(ops); WAKE = COST["WAKE"]; LOOK = COST["LOOK"]
     succ = [[] for _ in range(n)]
     for i, o in enumerate(ops):
         for d in o["deps"]: succ[d].append(i)
     way = [0.0] * n
     for i in range(n - 1, -1, -1):
         o = ops[i]
-        way[i] = o["dur"] + max([o["lat"] + WAKE + way[j] for j in succ[i]] + [0.0])
-    pri = [way[i] + early(ops[i]["tag"]) for i in range(n)]
+        way[i] = o["dur"] + max([o["lat"] + WAKE + way[j] for j in succ[i]] + [o["lat"]])
+    pri = [(-due(ops[i]["tag"]), way[i]) for i in range(n)]
     left = [len(o["deps"]) for o in ops]
     ready = [0.0] * n
     free = {"V": 0.0, "S": 0.0, "G": 0.0, "T": 0.0, "SY": 0.0}
     cand = {q: [] for q in free}
     for i in range(n):
         if left[i] == 0: cand[ops[i]["q"]].append(i)
-    order, start = [], [0.0] * n
+    order = []
     while len(order) < n:
-        best = None
-        for q in cand:
-            for i in cand[q]:
-                key = (max(free[q], ready[i]), -pri[i], i)
-                if best is None or key < best: best = key
-        t, i = best[0], best[2]
-        o = ops[i]; q = o["q"]
+        t0, q = min((max(free[q], min(ready[i] for i in cand[q])), q) for q in cand if cand[q])
+        i = max((i for i in cand[q] if ready[i] <= t0), key=lambda i: (pri[i], -i))
+        soon = [j for j in cand[q] if t0 < ready[j] < t0 + ops[i]["dur"] - COST["TOL"] and pri[j][0] > pri[i][0] + COST["GAP"]]
+        if soon:
+            tr = min(ready[j] for j in soon)
+            fit = [j for j in cand[q] if ready[j] <= t0 and t0 + ops[j]["dur"] <= tr + COST["TOL"]]
+            if fit: i = max(fit, key=lambda i: (pri[i], -i))
+            elif tr - t0 <= LOOK: i = max((j for j in soon if ready[j] == tr), key=lambda i: (pri[i], -i))
+        o = ops[i]; t = max(t0, ready[i])
         cand[q].remove(i)
-        start[i] = t; fin = t + o["dur"]; free[q] = fin
+        fin = t + o["dur"]; free[q] = fin
         order.append(i)
         for j in succ[i]:
             same = ops[j]["q"] == q and q == "T"
             ready[j] = max(ready[j], t if same else fin + o["lat"] + WAKE)
             left[j] -= 1
             if left[j] == 0: cand[ops[j]["q"]].append(j)
-    pos = {i: k for k, i in enumerate(order)}
-    order.sort(key=lambda i: (start[i], pos[i]))
     return order
 
 
@@ -406,19 +389,20 @@ def rank_program(g, core, T, topo):
         o = ops[i]; q = o["q"]; need = {}
         for d in o["deps"]:
             if ops[d]["q"] == q and q == "T": continue
-            nm, v = done[d]
-            need[nm] = max(need.get(nm, 0), v)
-        for nm in sorted(need):
-            if seen[q].get(nm, 0) < need[nm]:
-                eng[q].wait_ge(T.sem[nm], need[nm]); seen[q][nm] = need[nm]
+            if done[d][1] > need.get(done[d][0], (0, 0))[0]: need[done[d][0]] = done[d][1:]
+        waits = sorted(nm for nm in need if seen[q].get(nm, 0) < need[nm][0])
+        waits = [nm for nm in waits if not any(need[m][1].get(nm, 0) >= need[nm][0] for m in waits if m != nm)]
+        for nm in waits:
+            eng[q].wait_ge(T.sem[nm], need[nm][0]); seen[q][nm] = need[nm][0]
+            for m, v in need[nm][1].items(): seen[q][m] = max(seen[q].get(m, 0), v)
         res = o["fn"](last[o["grp"]] == i) if o["grp"] else o["fn"]()
         if o["sem"] is not None:
             if q != "G": res.then_inc(T.sem[o["sem"]], 16)
-            done[i] = (o["sem"], o["val"])
+            done[i] = (o["sem"], o["val"], {})
         else:
-            for x in (res if o["n"] > 1 else [res]): x.then_inc(csem[q], 1)
+            for x in (res if q == "T" else [res]): x.then_inc(csem[q], 1)
             count[q] += o["n"]
-            done[i] = ("c" + q, count[q])
+            done[i] = ("c" + q, count[q], dict(seen[q]))
     g.sync.wait_ge(T.sem.st, 16 * stores[0])
     dst = T.cores[(rank - 1) % len(T.cores)]
     g.wait_ge(T.sem.snt, 2 * (L - 1) * len(topo.engines(core, dst)))

@@ -1,4 +1,5 @@
 import numpy as np
+from concourse.bass import DstId, RemoteDMATransfer
 from concourse.mybir import AluOpType, AxisListType, ActivationFunctionType
 
 A = AluOpType
@@ -9,10 +10,16 @@ OFF = 16384.0
 DL = 63.0 / 128.0
 BLK = [0, 2, 1, 3]
 CH = 256
+WL = 24
 XW = 16 + CH
-COST = dict(GE=1.3e-3, CY=0.95e-3, WAKE=0.15, REMOTE=2.5, PE=0.5e-3, FIX=0.01, YT=5.5, SF=0.05, LOOK=0.03, TOL=0.0, GAP=0.3)
-PRI = dict(setup=-9.0, hints=-3.0, reps=-5.0, const=-3.0, z=-5.0, prep=-5.0, pen=0.5, search=0.0, post=-3.0, xup=-2.0, late=3.0, v=0.0, relu=2.0, mv=0.0)
-OPT = dict(joint=1, nrelu=2, share=1)
+SLOW = np.array([1.2, 1.0, 1.45, 1.05, 1.3])
+COST = dict(CY=0.83e-3 * SLOW, GE=0.83e-3 * SLOW * np.array([1.6, 1.35, 2.0, 1.2, 1.3]), PE=1e-3 * SLOW * np.array([0.45, 0.45, 0.45, 0.45, 0.5]),
+            WAKE=np.array([0.24, 0.24, 0.2, 0.17, 0.3]), REMOTE=np.array([2.2, 1.9, 1.9, 1.6, 2.5]), YT=np.array([5.0, 4.3, 4.8, 4.3, 5.3]), FIX=0.0, SF=0.05, FIRST=1.2,
+            FOLD=np.array([4.0, 3.5, 3.5, 3.5, 5.0]))
+PRI = dict(setup=-9.0, hints=2.0, reps=-5.0, reps1=3.0, mask=2.0, mstep=0.5, const=-3.0, z=-5.0, prep=-5.0, pen=0.5, search=0.0, post=-5.0, xup=-2.0, late=3.0, v=0.0, relu=0.5, mv=0.0)
+PRI.update(relu00=0.0, relu01=0.0, relu10=0.5, relu11=0.0, pen1=0.0, post1=0.0, lsS=0.0)
+EACH = (256, 512, 768, 1024)
+OPT = dict(seed=1, rounds=60, sets=(1, 4), noise=0.6, polish=2000, periodic=600, same=4, tries=40, magic=1, xg=1, cV=0, dxA=1, rS00=0, rS01=0, rS10=0, rS11=0, vr00=0, vr01=0, vr10=0, vr11=0, ends={}, dxV=0, first=4, joint=1, share=1, nrelu00=EACH, nrelu01=EACH, nrelu10=EACH, nrelu11=EACH, cut00=(256,) * 4, cut01=(256,) * 4, cut10=(256,) * 4, cut11=(256,) * 4, rows=(4, 8, 12, 14, 15, 16), slack=0.2)
 
 SCRATCH = {
     "yt": ("sbuf", [128, NI], "bfloat16"), "x0": ("sbuf", [128, 2 * L, 32], "bfloat16"), "xf": ("sbuf", [128, R], "float32"),
@@ -24,24 +31,24 @@ SCRATCH = {
     "ctab": ("sbuf", [128, 160], "float32"), "gtab": ("sbuf", [128, 128], "float32"), "t2": ("sbuf", [128, 128], "float32"),
     "e0": ("sbuf", [128, 128], "float32"), "qt": ("sbuf", [128, 512], "bfloat16"), "qw": ("sbuf", [128, 512], "float16"),
     "bo": ("sbuf", [128, 128], "float16"), "bos": ("sbuf", [128, 128], "float16"), "bop": ("sbuf", [128, 128], "float16"),
-    "bon": ("sbuf", [128, 128], "float16"), "idh": ("sbuf", [128, 128], "float16"), "i64": ("sbuf", [128, 128], "float16"),
+    "bon": ("sbuf", [128, 128], "float16"), "idh": ("sbuf", [128, 128], "float16"), "i4": ("sbuf", [128, 128], "float32"), "i64": ("sbuf", [128, 128], "float16"),
+    "rl": ("sbuf", [128, 18], "uint16"), "ri": ("sbuf", [128, 18], "int32"), "huge": ("sbuf", [128, 128], "bfloat16"),
     "idb": ("sbuf", [128, 128], "bfloat16"), "idn": ("sbuf", [128, 128], "bfloat16"),
     "c1": ("sbuf", [128, 256], "float16"), "c2": ("sbuf", [128, 128], "float16"), "zero": ("sbuf", [128, 128], "bfloat16"),
     "zs": ("sbuf", [128, 160], "bfloat16"), "zr": ("sbuf", [128, 160], "bfloat16"), "zd": ("sbuf", [128, 160], "bfloat16"),
     "seg": ("sbuf", [128, 128], "float32"), "sgp": ("sbuf", [128, 64], "float32"), "sgn": ("sbuf", [128, 64], "float32"),
-    "sgz": ("sbuf", [128, 64], "float32"),
+    "fin": ("sbuf", [128, 3, 128], "float32"), "sgz": ("sbuf", [128, 64], "float32"),
     "Z": ("psum", [128, 512], "float32"), "X": ("psum", [128, 512], "float32"),
 }
 for _k in range(1, 8): SCRATCH["h%d" % _k] = ("sbuf", [128, 40], "int32")
 for _p in range(2):
-    SCRATCH["win%d" % _p] = ("sbuf", [128, 8 * L], "int32")
+    SCRATCH["win%d" % _p] = ("sbuf", [128, WL * L], "float32")
     SCRATCH["as%d" % _p] = ("sbuf", [128, 32 * 64], "bfloat16")
+    SCRATCH["ar%d" % _p] = ("sbuf", [128, 32 * 64], "bfloat16")
     SCRATCH["dv%d" % _p] = ("sbuf", [128, 32 * 64], "bfloat16")
     SCRATCH["rv%d" % _p] = ("sbuf", [128, 32 * 64], "bfloat16")
     SCRATCH["ks%d" % _p] = ("sbuf", [128, 256], "float32")
-    SCRATCH["ki%d" % _p] = ("sbuf", [128, 4], "int32")
-    SCRATCH["ei%d" % _p] = ("sbuf", [128, 4], "int32")
-    SCRATCH["wo%d" % _p] = ("sbuf", [128, 4], "uint16")
+    SCRATCH["wo%d" % _p] = ("sbuf", [128, 4 * L], "uint16")
     SCRATCH["dx%d" % _p] = ("sbuf", [128, 128], "bfloat16")
     SCRATCH["rh%d" % _p] = ("sbuf", [128, 128], "float16")
     SCRATCH["z%d" % _p] = ("sbuf", [128, 64], "float16")
@@ -52,16 +59,34 @@ for _s in range(3):
     SCRATCH["sc%d" % _s] = ("sbuf", [128, 8], "float32")
     SCRATCH["ofv%d" % _s] = ("sbuf", [128, 128], "uint16")
     SCRATCH["ofs%d" % _s] = ("sbuf", [128, 128], "uint16")
-    SCRATCH["pa%d" % _s] = ("sbuf", [128, 256], "float32")
     SCRATCH["pn%d" % _s] = ("sbuf", [128, 256], "float16")
+    SCRATCH["pa%d" % _s] = ("sbuf", [128, 256], "float32")
 
 LOADS = ["y", "lo", "hi", "x", "home", "ha", "hb"]
 SEMAPHORES = (["cV", "cS", "cT", "cG", "snt", "st"] + ["ld_" + k for k in LOADS]
               + ["arr%d_%d" % (p, l) for p in range(2) for l in range(L - 1)])
 
 
+FOLDS = []
+SEMAPHORES += ["f%s%d" % (x, k) for x in "ab" for k in range(len(FOLDS))]
+SCRATCH["land"] = ("sbuf", [128, max(1, len(FOLDS)), 1024], "bfloat16")
+SCRATCH["zw"] = ("sbuf", [128, 1024], "bfloat16")
+
+
+def helper(core, T, topo):
+    return [c for c in topo.cores_of(core) if T.rank_of(c) is None and topo.die(c) == topo.die(core)][0]
+
+
+def hand_back(g, core, T, topo, owner):
+    rid, pid, _ = topo.addr(owner)
+    for k, (p, l, u) in enumerate(FOLDS):
+        g.wait_ge(T.sem["fa%d" % k], len(topo.engines(owner, core)))
+        g.remote_dma(T["rv%d" % p][:, 1024 * u:1024 * u + 1024], T.land[:, k, :], T.sem["fb%d" % k], T.sem.snt, pid, rid, topo.mask(core, owner))
+    g.wait_ge(T.sem.snt, len(FOLDS) * len(topo.engines(core, owner)))
+
+
 def build(g, core, T, topo, rank):
-    ops = []; ctx = [("setup", 0, 0, 0)]
+    ops = []; ctx = [("setup", 0, 0, 0)]; lv = [(-1, 0)]
     last_w, readers = {}, {}
     GE, CY, PE = COST["GE"], COST["CY"], COST["PE"]
 
@@ -74,7 +99,7 @@ def build(g, core, T, topo, rank):
             deps.update(k for k in readers.get(t, ()) if k != i)
         for t in r: readers.setdefault(t, []).append(i)
         for t in w: last_w[t] = i; readers[t] = []
-        ops.append(dict(q=q, dur=dur, fn=fn, deps=sorted(deps), n=n, sem=sem, val=val, lat=lat, grp=grp, tag=ctx[0]))
+        ops.append(dict(q=q, dur=dur, fn=fn, deps=sorted(deps), n=n, sem=sem, val=val, lat=lat, grp=grp, tag=ctx[0], lv=lv[0]))
         return i
 
     V, S, G, TE, SY = g.vector, g.scalar, g, g.tensor, g.sync
@@ -94,21 +119,19 @@ def build(g, core, T, topo, rank):
     def act(out, in_, r, w, n, bias=0.0, scale=1.0, f=F.Abs, gather=False):
         add("S", 0.065 + n * GE if gather else COST["SF"] + n * CY, lambda: S.activation(out, in_, f, bias=bias, scale=scale), r, w)
     def mms(calls, r, w, grp=None):
-        def fn(last=False):
-            return [TE.matmul(o, a, b, st, (last and k == len(calls) - 1) if sp is None else sp) for k, (o, a, b, n, st, sp) in enumerate(calls)]
+        def fn(last=False, first=False):
+            return [TE.matmul(o, a, b, st or (first and k == 0), (last and k == len(calls) - 1) if sp is None else sp) for k, (o, a, b, n, st, sp) in enumerate(calls)]
         add("T", sum(max(64, c[3]) for c in calls) * PE, fn, r, w, n=len(calls), grp=grp)
 
     def load(q, key, out, in_, lat):
         eng = SY if q == "SY" else S
         ctx[0] = ("setup", 0, 0, len(ops) * 1e-3 - 1)
         add(q, 0.1, lambda: eng.dma_start(out, in_), (), (key,), sem="ld_" + key, val=16, lat=lat)
-    load("SY", "lo", T.lh[:, 0:4], T.lo0[:], 1.8)
-    load("S", "hi", T.lh[:, 4:8], T.hi0[:], 1.8)
-    load("S", "x", T.x0[:], T.xrow[:], 2.0)
-    load("SY", "home", T.hm[:], T.home[:], 2.0)
-    load("SY", "ha", T.hab[:, 0:20], T.ha[:], 2.0)
-    load("S", "hb", T.hab[:, 20:40], T.hb[:], 2.0)
+    small = [("lo", T.lh[:, 0:4], T.lo0[:]), ("hi", T.lh[:, 4:8], T.hi0[:]), ("x", T.x0[:], T.xrow[:]), ("home", T.hm[:], T.home[:]),
+             ("ha", T.hab[:, 0:20], T.ha[:]), ("hb", T.hab[:, 20:40], T.hb[:])]
+    for k, (key, out, in_) in enumerate(small[:OPT["first"]]): load(("SY", "S")[k % 2], key, out, in_, 1.1 + 0.3 * k)
     load("SY", "y", T.yt[:], T.ytab[:], COST["YT"])
+    for key, out, in_ in small[OPT["first"]:]: load("SY", key, out, in_, COST["YT"])
 
     ctx[0] = ("setup", 0, 0, 0)
     def iota(out, pat, cm, tok, n, fl=True):
@@ -138,7 +161,7 @@ def build(g, core, T, topo, rank):
     table("bos", "gtab", "bosA", g16, "g16", -1.0, 64, slice(0, 128, 2))
     table("bos", "gtab", "bosB", g16, "g16", 1.0, 64, slice(1, 128, 2))
     for nm, v in (("bo", 1.0), ("bop", 1.0 / 64), ("bon", -1.0 / 64)): table(nm, "gtab", nm, g16, "g16", v)
-    for nm, v in (("idb", 1.0), ("idh", 1.0), ("i64", 64.0)):
+    for nm, v in (("idb", 1.0), ("idh", 1.0), ("i4", 4.0) if OPT["magic"] else ("i64", 64.0)):
         ts(T[nm][:], T.ctab[:, 0:128], pp, v, A.is_equal, A.mult, ["ctab", "pp"], [nm], 128)
     table("zs", "ctab", "zs", zc, "zc", 64.0, 160)
     for nm, src, v, n in (("zr", "zs", 2.0, 160), ("zd", "zs", -1.0, 160), ("idn", "idb", -1.0, 128)):
@@ -151,8 +174,15 @@ def build(g, core, T, topo, rank):
     ts(T.c1[:, 128:256], T.t2[:], f16, -OFF, A.not_equal, A.mult, ["t2", "f16"], ["c1b"], 128)
     ts(T.c1[:, 0:128], T.c1[:, 128:256], -1.0, 2048.0, A.mult, A.max, ["c1b"], ["c1a"], 128, 0.5)
     ts(T.c2[:], T.gtab[:], 0.0, -DL, A.mult, A.add, ["gtab"], ["c2"], 128)
-    iota(T.zero[:], [[0, 128]], 0, "zero", 128)
+    if OPT["magic"]:
+        ms(T.zero[:], -30.0, ["zero"], 64)
+        ms(T.huge[:], 1.5 * 2 ** 29, ["huge"], 64)
+    if OPT["xg"]:
+        ts(T.ri[:], T.ctab[:, 0:18], 1.0, 16.0, A.min, A.mult, ["ctab"], ["ri"], 18)
+        ts(T.rl[:], T.ri[:], f16, None, A.add, None, ["ri", "f16"], ["rl"], 18)
     ts(T.m16[:], T.ctab[:, 0:16], f16, None, A.is_equal, None, ["ctab", "f16"], ["m16"], 16)
+    ms(T.fin[:], 1.0, ["fin0"], 384)
+    for o, v in ((1, 63.0), (3, 1.5 * 2 ** 23), (4, -1.5 * 2 ** 23 - 2048)): ms(T.fin[:, :, o:64:16], v, ["fin"], 12, ["fin0"])
     for nm, n, st, v0, v1 in (("seg", 128, 64, -1.0, BIG), ("sgp", 64, 32, 0.0, BIG), ("sgn", 64, 32, 0.0, -BIG), ("sgz", 64, 2, 0.0, -BIG)):
         ms(T[nm][:], v0, [nm + "0"], n)
         ms(T[nm][:, 0:n:st], v1, [nm], n // st, [nm + "0"])
@@ -173,20 +203,22 @@ def build(g, core, T, topo, rank):
     ts(T.h5[:], T.h4[:], 28, None, A.bitwise_and, None, ["h4"], ["h5"], 40)
     ts(T.h3[:], T.h2[:], 24.0, -20.0, A.is_ge, A.mult, ["h2"], ["h3"], 40)
     tt(T.h6[:], T.h2[:], T.h3[:], A.add, ["h2", "h3"], ["h6"], 40)
-    tt(T.h4[:], T.h5[:], T.h6[:], A.add, ["h5", "h6"], ["h4"], 40)
+    ts(T.h3[:], T.h5[:], 5.0, 16.0, A.mult, A.add, ["h5"], ["h3"], 40)
+    tt(T.h4[:], T.h3[:], T.h6[:], A.add, ["h3", "h6"], ["h4"], 40)
     cp(T.hl[:, 8:48], T.h4[:], ["h4"], ["hl"], 40)
     ts(T.h7[:], T.h1[:], 15, None, A.bitwise_and, None, HT, ["h7"], 40)
     cp(T.hr[:, 8:48], T.h7[:], ["h7"], ["hr"], 40)
-    for l in range(1, L): masks(l, "hr")
+    for l in range(1, L):
+        ctx[0] = ("mask", 0, 0, (l - 1) * PRI["mstep"]); masks(l, "hr")
 
-    def reps0():
-        ctx[0] = ("reps", 0, 0, 0); n = 2 * L
-        cp(T.rep0[:, :, 0:32], T.x0[:], ["x"], ["rep.16"], 32 * n, 0.5)
+    def reps0(kind, n0, n1):
+        ctx[0] = (kind, 0, 0, 0); n = n1 - n0
+        cp(T.rep0[:, n0:n1, 0:32], T.x0[:, n0:n1, :], ["x"], ["rep%d.16" % n0], 32 * n, 0.5)
         k = 16
         while k < CH:
-            cp(T.rep0[:, :, 16 + k:16 + 2 * k], T.rep0[:, :, 16:16 + k], ["rep.%d" % k], ["rep.%d" % (2 * k)], k * n, 0.5)
+            cp(T.rep0[:, n0:n1, 16 + k:16 + 2 * k], T.rep0[:, n0:n1, 16:16 + k], ["rep%d.%d" % (n0, k)], ["rep%d.%d" % (n0, 2 * k)], k * n, 0.5)
             k *= 2
-    REP = "rep.%d" % CH
+    def reptok(l): return "rep%d.%d" % (2 if l else 0, CH)
 
     def sets(p, l): return 2 if l == 0 else p
     def B1(s, k): return T["ls%d" % s][:, 32 * k + 31:32 * k + 32]
@@ -199,7 +231,7 @@ def build(g, core, T, topo, rank):
         mms([(Rb[:, 0:256], T.idh[:], T.c1[:], 256, True, False), (Rb[:, 0:128], T.idh[:], T.c2[:], 128, False, False)], ["idh", "c1a", "c1b", "c2"], ["R" + P])
         ctx[0] = ("z", p, l, at)
         if l == 0: win, wt = T.lob[:], ["lob", "hl0"]
-        else: win, wt = T["win" + P][:, 0:8 * l], ["hl"] + ["w%d.%d.%d" % (p, k, x) for k in range(l) for x in range(5)]
+        else: win, wt = T["win" + P][:, 0:WL * l], ["hl"] + ["w%d.%d.%d" % (p, k, x) for k in range(l) for x in range(5)]
         tt(rh[:], win.indirect(T.hl[:, 8 * l:8 * l + 8]), T.mk[:, 128 * l:128 * l + 128], A.mult, wt + ["mk%d" % l], ["rh" + P], 128, gather=True)
         mms([(T.Z[:, h:64:2], T.bos[:], rh[:, 64 * h:64 * h + 32], 32, True, True) for h in range(2)], ["bosA", "bosB", "rh" + P], ["Z"])
         scan(z[:], T.sgz[:], T.Z[:, 0:64], A.max, ["sgz", "Z"], ["z" + P], 64)
@@ -211,18 +243,31 @@ def build(g, core, T, topo, rank):
              (Rb[:, 128:256:2], T.bop[:], a, 64, False, False), (Rb[:, 128:256:2], T.bon[:], b, 64, False, False),
              (Rb[:, 129:256:2], T.bon[:], a, 64, False, False), (Rb[:, 129:256:2], T.bop[:], b, 64, False, True)], ["bo", "bop", "bon", "rh" + P, "R" + P], ["R" + P])
         for h in (1, 0):
+            ctx[0] = ("prep", p, l, at + (1 - h) * PRI["lsS"])
             scan(ls[:, 64 * h:64 * h + 64], T.sgp[:], Rb[:, 64 * h:64 * h + 64], A.min, ["sgp", "R" + P], [t + "B%d" % h], 64)
             scan(ls[:, 128 + 64 * h:192 + 64 * h], T.sgn[:], Rb[:, 128 + 64 * h:192 + 64 * h], A.max, ["sgn", "R" + P], [t + "D%d" % h], 64)
         for u in range(2):
+            ctx[0] = ("prep", p, l, at + u * PRI["lsS"])
             ts(T["ofv%d" % s][:, 64 * u:64 * u + 64], etab, DD(s, 2 + u), B1(s, 2 + u), A.mult, A.add, ["ctab", t + "B1", t + "D1"], ["ofv%d.%d" % (s, u)], 64)
-        ctx[0] = ("pen", p, l, at); bt = [t + "B0", t + "B1"]
-        act(sc[:, 0:4], ls[:, 31:128:32], bt, [t + "C"], 4, bias=-2048.0, f=F.Identity)
+        ctx[0] = ("pen", p, l, p * PRI["pen1"] if l else -6); bt = [t + "B0", t + "B1"]
+        if OPT["cV"]: cp(T.fin[:, s, 2:128:16], ls[:, 31:256:32], bt + [t + "D0", t + "D1", "fin"], [t + "C"], 8)
+        else: act(T.fin[:, s, 2:128:16], ls[:, 31:256:32], bt + [t + "D0", t + "D1", "fin"], [t + "C"], 8, f=F.Identity)
         tt(sc[:, 4:8], ls[:, 31:128:32], T.hf[:, 4 * l:4 * l + 4], A.subtract, bt + HF, [t + "H"], 4)
         pa = T["pa%d" % s]
         for k in range(4):
             o = 128 * (k % 2) + 64 * (k // 2)
             act(pa[:, o:o + 64], etab, ["ctab", t + "D%d" % (k // 2), t + "H"], ["pa%d.%d" % (s, k)], 64, bias=sc[:, 4 + k:5 + k], scale=DD(s, k))
-        ts(T["pn%d" % s][:], pa[:], 1.0 / 16, 1280.0 - 15.0 / 32, A.mult, A.add, ["pa%d.%d" % (s, k) for k in range(4)], ["pn%d" % s], 256)
+        if not OPT["magic"]:
+            ts(T["pn%d" % s][:], pa[:], 1.0 / 16, 1280.0 - 15.0 / 32, A.mult, A.add, ["pa%d.%d" % (s, k) for k in range(4)], ["pn%d" % s], 256)
+
+    def fold(k, a, b, r, w):
+        h = helper(core, T, topo); rid, pid, _ = topo.addr(h)
+        def fn():
+            G.remote_dma_fused([RemoteDMATransfer(dst_ids=[DstId(rid=rid, pnc=pid)], dma_engine_mask=topo.mask(core, h), remote_sem=T.sem["fa%d" % k],
+                                                  srcs=[a, b], dsts=[T.land[:, k, :]], alu_op=2)], local_sem=T.sem.snt)
+        add("G", 0.6, fn, r, w, n=0, sem="fb%d" % k, val=len(topo.engines(h, core)), lat=COST["FOLD"] + (0.0 if k else COST["FIRST"]))
+    if FOLDS:
+        ctx[0] = ("reps1", 0, 0, 0); ms(T.zw[:], 0.0, ["zw"], 512)
 
     KEYS = ["s%d" % i for i in range(16)] + ["d", "r", "p"]
 
@@ -230,59 +275,94 @@ def build(g, core, T, topo, rank):
         ctx[0] = ("search", p, l, u); s = sets(p, l)
         K = T["K%d%d" % (p, u)]; kt = lambda x: "K%d%d.%s" % (p, u, x); grp = (p, l, u)
         xt = "x" if p == 0 else "xr%d.%d" % (l, u); o1 = 2 * l + u
-        mms([(K[:, 0:128], T.idb[:], T.zero[:], 128, True, False)], ["idb", "zero"], [kt(q) for q in KEYS] + [kt("0")])
-        mms([(K[:, 0:128], T.i64[:], T["pn%d" % s][:, 128 * u:128 * u + 128], 128, False, None)], ["i64", "pn%d" % s, kt("0")], [kt("p")], grp)
+        if not OPT["magic"]:
+            mms([(K[:, o:o + 64], T.i64[:], T["pn%d" % s][:, 128 * u + o:128 * u + o + 64], 64, False, None) for o in (0, 64)], ["i64", "pn%d" % s], [kt("p")], grp)
+        else: mms([(K[:, 0:128], T.idb[:], T.zero[:], 128, True, False)], ["idb", "zero"], [kt(q) for q in KEYS] + [kt("0")])
+        if OPT["magic"]: mms([(K[:, 0:128], T.i4[:], T["pa%d" % s][:, 128 * u:128 * u + 128], 512, False, False), (K[:, 0:128], T.idb[:], T.huge[:], 128, False, False),
+             (K[:, 0:128], T.idn[:], T.huge[:], 128, False, None)], ["i4", "idb", "idn", "huge", "pa%d.%d" % (s, u), "pa%d.%d" % (s, 2 + u), kt("0")], [kt("p")], grp)
+        nv = OPT["ends"].get((p, l), OPT["vr%d%d" % (p, u)]); b = T["as%d" % p]
         for i in range(16):
             ctx[0] = ("search", p, l, u + i / 16)
-            r = 16 * u + i; o = T["as%d" % p][:, 64 * r:64 * r + 64]
-            act(o, T.yt[:].indirect(T["ofs%d" % s][:, 4 * r:4 * r + 4]), ["y", "ofs%d" % s, xt], ["as%d.%d" % (p, r)], 64,
-                bias=T["xr" if p else "x0"][:, o1, i:i + 1], scale=-1.0, gather=True)
-            mms([(K[:, 0:64], T.zs[:, 15 - i:143 - i], o, 64, False, None)], ["zs", "as%d.%d" % (p, r), kt("0")], [kt("s%d" % i)], grp)
+            r = 16 * u + i; o = b[:, 64 * r:64 * r + 64]
+            y, x = T.yt[:].indirect(T["ofs%d" % s][:, 4 * r:4 * r + 4]), T["xr" if p else "x0"][:, o1, i:i + 1]
+            if i < nv:
+                add("V", 0.05 + 64 * GE, lambda o=o, y=y, x=x: V.tensor_scalar(o, y, x, None, A.subtract), ["y", "ofs%d" % s, xt], ["as%d.%d" % (p, r)])
+                if i == nv - 1:
+                    ar = T["ar%d" % p]; a0 = 1024 * u; at = ["as%d.%d" % (p, 16 * u + j) for j in range(nv)]
+                    ts(ar[:, a0:a0 + 64 * nv], b[:, a0:a0 + 64 * nv], 0.0, None, A.max, None, at, ["ar%d.%d" % (p, u)], 64 * nv, 0.5)
+                    mms([(K[:, 0:64], T[z][:, 15 - j:143 - j], q[:, a0 + 64 * j:a0 + 64 * j + 64], 64, False, None) for z, q in (("zd", b), ("zr", ar)) for j in range(nv)],
+                        ["zd", "zr", kt("0"), "ar%d.%d" % (p, u)] + at, [kt("s%d" % j) for j in range(nv)], grp)
+                continue
+            act(o, y, ["y", "ofs%d" % s, xt], ["as%d.%d" % (p, r)], 64, bias=x, scale=-1.0, gather=True)
+            if i + 1 in OPT["rows"]:
+                js = range(max([nv] + [q for q in OPT["rows"] if q <= i]), i + 1)
+                mms([(K[:, 0:64], T.zs[:, 15 - j:143 - j], b[:, 64 * (16 * u + j):64 * (16 * u + j + 1)], 64, False, None) for j in js],
+                    ["zs", kt("0")] + ["as%d.%d" % (p, 16 * u + j) for j in js], [kt("s%d" % j) for j in js], grp)
+                if i < 12: ops[-1]["slack"] = OPT["slack"]
         shared = OPT["share"] and p == 1 and l == 0
         pd = 0 if shared else p
-        dv, rv = T["dv%d" % pd], T["rv%d" % p]; d0 = 1024 * u; nr = OPT["nrelu"]
+        dv, rv = T["dv%d" % pd], T["rv%d" % p]; d0 = 1024 * u; nr = OPT["nrelu%d%d" % (p, u)]
         rep = T["xr" if p else "rep0"][:, o1, 16:XW]
-        rt = REP if p == 0 else xt
+        REP = reptok(l); rt = REP if p == 0 else xt
         if shared:
             Rb = T["R%d" % u]
             mms([(Rb[:, 0:CH], T.idb[:], rep, CH, True, False), (Rb[:, 0:CH], T.idn[:], T.rep0[:, o1, 16:XW], CH, False, True)], ["idb", "idn", rt, REP], ["R%d" % u])
-        for c in range(1024 // CH):
-            d = d0 + CH * c; ctx[0] = ("search", p, l, u + c * CH / 1024 - PRI["v"])
-            if shared:
-                tt(rv[:, d:d + CH], dv[:, d:d + CH], Rb[:, 0:CH], A.max, ["dv0.%d" % d, "R%d" % u], ["rv1.%d" % d], CH, 1.0)
-                continue
-            tt(dv[:, d:d + CH], T.yt[:].indirect(T["ofv%d" % s][:, 64 * u + CH // 16 * c:64 * u + CH // 16 * (c + 1)]), rep, A.subtract,
-               ["y", "ofv%d.%d" % (s, u), rt], ["dv%d.%d" % (p, d)], CH, gather=True)
-            if c % nr == nr - 1:
-                e = d - (nr - 1) * CH; ctx[0] = ("search", p, l, u + (c + PRI["relu"]) * CH / 1024 - PRI["v"]); ds = range(e, d + CH, CH)
-                ts(rv[:, e:d + CH], dv[:, e:d + CH], 0.0, None, A.max, None, ["dv%d.%d" % (p, q) for q in ds], ["rv%d.%d" % (p, q) for q in ds], nr * CH, 0.5)
+        tok = lambda kind, q, a, b: ["%sv%d.%d" % (kind, q, m) for m in range(a, b, 128)]
+        d = e = d0
+        for n in ((CH,) * 4 if l == 0 else OPT["cut%d%d" % (p, u)]):
+            ctx[0] = ("search", p, l, u + (d - d0) / 1024 - PRI["v"]); f = d + n
+            if shared: tt(rv[:, d:f], dv[:, d:f], Rb[:, 0:n], A.max, tok("d", 0, d, f) + ["R%d" % u], tok("r", 1, d, f), n, 1.0)
+            else:
+                tt(dv[:, d:f], T.yt[:].indirect(T["ofv%d" % s][:, d // 16:f // 16]), T["xr" if p else "rep0"][:, o1, 16:16 + n], A.subtract,
+                   ["y", "ofv%d.%d" % (s, u), rt], tok("d", p, d, f), n, gather=True)
+                if f - d0 in nr:
+                    ctx[0] = ("search", p, l, u + PRI["relu"] + (d - d0) / 1024 - PRI["v"])
+                    ts(rv[:, e:f], dv[:, e:f], 0.0, None, A.max, None, tok("d", p, e, f), tok("r", p, e, f), f - e, 0.5); e = f
+            d = f
         ctx[0] = ("search", p, l, u + PRI["mv"])
         for kind, buf, z, pb in (("d", dv, "zd", pd), ("r", rv, "zr", p)):
             mms([(K[:, 64:128], T[z][:, 15 - i:143 - i], buf[:, d0 + i:d0 + 1024:16], 64, False, None) for i in range(16)],
-                [z, kt("0")] + ["%sv%d.%d" % (kind, pb, q) for q in range(d0, d0 + 1024, CH)], [kt(kind)], grp)
+                [z, kt("0")] + tok(kind, pb, d0, d0 + 1024) + ([] if kind == "d" else [kt("d")] + [kt("p")] * shared), [kt(kind)], grp)
 
     def post(p, l, us):
-        ctx[0] = ("post", p, l, us[0]); s = sets(p, l); P = "%d" % p; ks = T["ks" + P]; t = "%d." % s; w = T["win" + P]
+        ctx[0] = ("post", p, l, us[0] + p * PRI["post1"]); s = sets(p, l); P = "%d" % p; ks = T["ks" + P]; t = "%d." % s; w = T["win" + P]
         for u in us:
             scan(ks[:, 128 * u:128 * u + 128], T.seg[:], T["K%d%d" % (p, u)][:, 0:128], A.min, ["K%d%d.%s" % (p, u, q) for q in KEYS] + ["seg"], ["ks%d.%d" % (p, u)], 128)
         c0, c1 = 2 * us[0], 2 * us[-1] + 2; c = slice(c0, c1)
-        kk, ee = ["ki%d.%d" % (p, u) for u in us], ["ei%d.%d" % (p, u) for u in us]
-        ts(T["ki" + P][:, c], ks[:, 64 * c0 + 63:64 * c1:64], 63.0 + 64 * 8192, None, A.add, None, ["ks%d.%d" % (p, u) for u in us], kk, 4)
-        ts(T["ei" + P][:, c], T["ki" + P][:, c], 63, None, A.bitwise_and, None, kk, ee, 4)
+        for a in range(c0, c1):
+            k = BLK.index(a); u = a // 2; K = T["K%d%d" % (p, u)]
+            add("V", sv(64), lambda k=k, a=a, K=K: V.tensor_reduce(T.fin[:, s, 16 * k:16 * k + 1], K[:, 64 * (a % 2):64 * (a % 2) + 64], AxisListType.X, A.min, negate=True),
+                ["K%d%d.%s" % (p, u, q) for q in KEYS] + ["fin"], [t + "r%d" % k])
         for a in range(c0, c1):
             k = BLK.index(a)
-            ts(w[:, 8 * l + a:8 * l + a + 1], T["ei" + P][:, a:a + 1], DD(s, k), T["sc%d" % s][:, k:k + 1], A.mult, A.add, ee + [t + "D%d" % (k // 2), t + "C"], ["w%d.%d.%d" % (p, l, a)], 1)
+            add("V", sv(5), lambda k=k, a=a: V.tensor_tensor_scan(w[:, WL * l + a:WL * l + 20:4], T.fin[:, s, 16 * k:16 * k + 5], T.fin[:, s, 65 + 16 * k:70 + 16 * k], ks[:, 64 * a + 63:64 * a + 64], A.add, A.mult),
+                ["ks%d.%d" % (p, a // 2), t + "r%d" % k, t + "C", "fin"], ["w%d.%d.%d" % (p, l, a)])
 
     def left(p, l, us):
         ctx[0] = ("xup" if p == 0 else "late", p, l, us[0]); P = "%d" % p; c0, c1 = 2 * us[0], 2 * us[-1] + 2
-        wk = ["wo%d.%d" % (p, u) for u in us]; yk = ["dx%d.%d" % (p, u) for u in us]
-        ts(T["wo" + P][:, c0:c1], T["win" + P][:, 8 * l + c0:8 * l + c1], 2048.0, None, A.add, None, ["w%d.%d.%d" % (p, l, a) for a in range(c0, c1)], wk, 4)
+        yk = ["dx%d.%d" % (p, u) for u in us]
+        wo = T["wo" + P][:, 4 * l + c0:4 * l + c1]; wk = ["wo%d.%d.%d" % (p, l, u) for u in us]
+        ts(wo, T["win" + P][:, WL * l + 16 + c0:WL * l + 16 + c1], 2048.0, None, A.add, None, ["w%d.%d.%d" % (p, l, a) for a in range(c0, c1)], wk, 4)
         yw = T["dx" + P]; n = 16 * (c1 - c0); o = 16 * c0
-        act(yw[:, o:o + n], T.yt[:].indirect(T["wo" + P][:, c0:c1]), ["y"] + wk, yk, n, f=F.Identity, gather=True)
+        if p == 1 and (OPT["dxV"] or l == L - 1):
+            for u in us:
+                tt(yw[:, 32 * u:32 * u + 32], T.yt[:].indirect(T.wo1[:, 4 * l + 2 * u:4 * l + 2 * u + 2]), T.xr[:, 2 * l + u, 0:32], A.subtract, ["y", "xr%d.%d" % (l, u)] + wk, ["dx1.%d" % u], 32, gather=True)
+            act(T.xf[:, 64 * l + o:64 * l + o + n], yw[:, o:o + n], yk, ["xf%d.%d" % (l, u) for u in us], n)
+            return
+        if p == 0 and OPT["dxA"]:
+            o1 = 2 * l + us[0]
+            tt(yw[:, o:o + n], T.yt[:].indirect(wo), T.x0[:, o1, :], A.subtract, ["y", "x"] + wk, yk, n, gather=True)
+            if OPT["xg"]:
+                act(T.xr[:, o1, :], yw[:, o:o + 32].indirect(T.rl[:, 0:XW // 16]), ["rl"] + yk, ["xr%d.%d" % (l, us[0])], XW, gather=True)
+                return
+            mms([(T.X[:, 0:32], T.idb[:], yw[:, o:o + 32], 32, True, True)] + [(T.X[:, k:k + 16], T.idb[:], yw[:, o + 16:o + 32], 16, True, True) for k in range(32, XW, 16)], ["idb"] + yk, ["X"])
+            act(T.xr[:, o1, :], T.X[:, 0:XW], ["X"], ["xr%d.%d" % (l, us[0])], XW)
+            return
+        act(yw[:, o:o + n], T.yt[:].indirect(wo), ["y"] + wk, yk, n, f=F.Identity, gather=True)
         if p == 0:
             o1 = 2 * l + us[0]
             mms([(T.X[:, 0:XW], T.idn[:], T.rep0[:, o1, :], XW, True, False), (T.X[:, 0:32], T.idb[:], yw[:, o:o + 32], 32, False, False)]
-                + [(T.X[:, k:k + 16], T.idb[:], yw[:, o + 16:o + 32], 16, False, k == XW - 16) for k in range(32, XW, 16)], ["idb", "idn", REP] + yk, ["X"])
+                + [(T.X[:, k:k + 16], T.idb[:], yw[:, o + 16:o + 32], 16, False, k == XW - 16) for k in range(32, XW, 16)], ["idb", "idn", reptok(l)] + yk, ["X"])
             act(T.xr[:, o1, :], T.X[:, 0:XW], ["X"], ["xr%d.%d" % (l, us[0])], XW)
         else:
             mms([(T.X[:, 0:n], T.idb[:], yw[:, o:o + n], n, True, False)]
@@ -296,8 +376,9 @@ def build(g, core, T, topo, rank):
         rid, pid, _ = topo.addr(dst)
         m = topo.mask(core, dst)
         def fn():
-            G.remote_dma(w[:, 8 * l + 4:8 * l + 8], w[:, 8 * l:8 * l + 4], T.sem["arr%d_%d" % (p, l)], T.sem.snt, pid, rid, m)
-        add("G", 0.5, fn, ["w%d.%d.%d" % (p, l, a) for a in range(4)], ["w%d.%d.4" % (p, l)], n=0, sem="arr%d_%d" % (p, l), val=len(topo.engines(core, dst)), lat=COST["REMOTE"])
+            G.remote_dma(w[:, WL * l + 20:WL * l + 24], w[:, WL * l + 16:WL * l + 20], T.sem["arr%d_%d" % (p, l)], T.sem.snt, pid, rid, m)
+        add("G", 0.6, fn, ["w%d.%d.%d" % (p, l, a) for a in range(4)], ["w%d.%d.4" % (p, l)], n=0, sem="arr%d_%d" % (p, l), val=len(topo.engines(core, dst)),
+            lat=COST["REMOTE"] + (0.0 if p + l else COST["FIRST"]))
 
     stores = [0]
     def store(q, out, in_, r):
@@ -305,21 +386,20 @@ def build(g, core, T, topo, rank):
         add(q, 0.1, lambda: eng.dma_start(out, in_), r, [], sem="st", val=None, lat=2.0)
 
     prep(1, 0)
-    reps0()
+    reps0("reps", 0, 2)
+    reps0("reps1", 2, 2 * L)
     for k in range(2 * L):
-        p, l = k % 2, k // 2
+        p, l = k % 2, k // 2; lv[0] = (p, l)
         if l: prep(p, l)
         for u in range(2): search(p, l, u)
-        for us in ([[0, 1]] if p and OPT["joint"] else [[0], [1]]): post(p, l, us)
+        for us in ([[0, 1]] if p and OPT["joint"] and l < L - 1 else [[0], [1]]): post(p, l, us)
         if l < L - 1: send(p, l)
         for us in ([[0, 1]] if p and l < L - 1 else [[0], [1]]): left(p, l, us)
         ctx[0] = ("late", p, l, 0)
         if l == L - 1:
-            w = T["win%d" % p]; am = T.am[:, 24 * p:24 * p + 24]
-            ts(T.am[:, 24 * p + 20:24 * p + 24], w[:, 8 * l:8 * l + 4], 2048.0, None, A.add, None, ["w%d.%d.%d" % (p, l, a) for a in range(4)], ["am%d.4" % p], 4)
-            for a in range(4):
-                ts(T.am[:, 24 * p + a:24 * p + 20:4], w[:, a:40:8], 2048.0, None, A.add, None, ["w%d.%d.%d" % (p, q, x) for q in range(L - 1) for x in (a, 4)], ["am%d.%d" % (p, a)], 5)
-            store("SY", T.argm[:, 24 * p:24 * p + 24], am, ["am%d.%d" % (p, a) for a in range(5)])
+            am = T.am[:, 24 * p:24 * p + 24]
+            cp(am, T["wo%d" % p][:], ["wo%d.%d.%d" % (p, q, u) for q in range(L) for u in range(2)], ["am%d" % p], 24)
+            store("SY", T.argm[:, 24 * p:24 * p + 24], am, ["am%d" % p])
         if p == 1 and l in (3, 4, 5):
             f = l if l > 3 else 0
             store("SY" if l < 5 else "S", T.xo[:, 64 * f:64 * l + 64], T.xf[:, 64 * f:64 * l + 64], ["xf%d.%d" % (q, u) for q in range(f, l + 1) for u in range(2)])
@@ -331,7 +411,7 @@ def due(tag):
     return 4 * l + 2 * p + u + PRI[k]
 
 
-def plan(ops):
+def plan_old(ops):
     n = len(ops); WAKE = COST["WAKE"]; LOOK = COST["LOOK"]
     succ = [[] for _ in range(n)]
     for i, o in enumerate(ops):
@@ -363,9 +443,121 @@ def plan(ops):
         order.append(i)
         for j in succ[i]:
             same = ops[j]["q"] == q and q == "T"
-            ready[j] = max(ready[j], t if same else fin + o["lat"] + WAKE)
+            ready[j] = max(ready[j], t if same else fin + o["lat"] + WAKE + ops[j].get("slack", 0.0))
             left[j] -= 1
             if left[j] == 0: cand[ops[j]["q"]].append(j)
+    return order
+
+
+def place(ops, pred, succ, key, k, back):
+    n = len(ops); wake = float(COST["WAKE"][k]); left = [len(p) for p in pred]; ready = [0.0] * n; start = [0.0] * n
+    line = {q: [] for q in ("V", "S", "G", "T", "SY")}
+    todo = sorted((key[i], i) for i in range(n) if left[i] == 0)
+    while todo:
+        i = todo.pop(0)[1]; o = ops[i]; d = o["d"][k]; t = ready[i]; ln = line[o["q"]]
+        if back and not pred[i]: t = o["l"][k]
+        j = len(ln)
+        while j > 0 and ln[j - 1][1] > t: j -= 1
+        while j < len(ln) and ln[j][0] < t + d - 1e-9: t = max(t, ln[j][1]); j += 1
+        ln.insert(j, (t, t + d)); start[i] = t
+        for j in succ[i]:
+            gap = 0.0 if o["q"] == "T" and ops[j]["q"] == "T" else wake + ops[j if back else i]["l"][k]
+            if t + d + gap > ready[j]: ready[j] = t + d + gap
+            left[j] -= 1
+            if left[j] == 0:
+                e = (key[j], j); m = len(todo)
+                while m > 0 and todo[m - 1] > e: m -= 1
+                todo.insert(m, e)
+    return start
+
+
+def length(ops, order):
+    out = []
+    for k in range(len(COST["CY"])):
+        wake = float(COST["WAKE"][k]); free = {"V": 0.0, "S": 0.0, "G": 0.0, "T": 0.0, "SY": 0.0}; seen = [0.0] * len(ops); end = 0.0
+        for i in order:
+            o = ops[i]; t = free[o["q"]]
+            for d in o["far"]:
+                if seen[d] > t: t = seen[d]
+            t += o["d"][k]; free[o["q"]] = t; t += o["l"][k]; seen[i] = t + wake
+            if t > end: end = t
+        out.append(end)
+    return out
+
+
+def plan(ops):
+    n = len(ops); one = np.ones(len(COST["CY"]))
+    pred = [o["deps"] for o in ops]; succ = [[] for _ in range(n)]
+    for i, o in enumerate(ops):
+        o["d"] = [float(x) for x in o["dur"] * one]; o["l"] = [float(x) for x in o["lat"] * one]
+        o["far"] = [d for d in o["deps"] if not (o["q"] == "T" and ops[d]["q"] == "T")]
+        for d in o["deps"]: succ[d].append(i)
+    rng = np.random.default_rng(OPT["seed"]); best = None
+    key = [3.0 * due(o["tag"]) + 1e-4 * i for i, o in enumerate(ops)]
+    for it in range(OPT["rounds"]):
+        k = OPT["sets"][int(rng.integers(len(OPT["sets"])))]
+        start = place(ops, pred, succ, key, k, False)
+        if it % 2 == 0:
+            back = place(ops, succ, pred, [-start[i] - ops[i]["d"][k] for i in range(n)], k, True)
+            start = place(ops, pred, succ, [-back[i] - ops[i]["d"][k] for i in range(n)], k, False)
+        order = sorted(range(n), key=lambda i: (start[i] if i >= len(LOADS) else -1.0, i))
+        score = sum(t / c for t, c in zip(length(ops, order), COST["CY"] * 30 + COST["GE"] * 25))
+        if best is None or score < best[0]: best = (score, order, start)
+        st = best[2]; mid = rng.random() * max(st); wide = 1.0 + 6.0 * rng.random(); size = OPT["noise"] * rng.random()
+        key = [st[i] + (size * rng.standard_normal() if abs(st[i] - mid) < wide else 0.0) for i in range(n)]
+    count = {}; kind = []
+    for o in ops:
+        lv = o["lv"]; count[lv] = count.get(lv, 0) + 1
+        kind.append((lv[0], 3 if 1 <= lv[1] <= OPT["same"] else lv[1], count[lv]))
+    st = best[2]; first = lambda l: min(st[i] for i in range(n) if ops[i]["lv"] == (0, l) and ops[i]["tag"][0] == "search" and ops[i]["q"] == "S")
+    period = (first(4) - first(2)) / 2
+    off = {kind[i]: st[i] - period * ops[i]["lv"][1] for i in range(n) if kind[i][1] == ops[i]["lv"][1]}
+    kinds = sorted(off); cur = None
+    for it in range(OPT["periodic"]):
+        new = dict(off)
+        if it:
+            a = int(rng.integers(len(kinds))); d = 0.6 * rng.standard_normal()
+            for m in kinds[a:a + int(rng.integers(1, 5))]: new[m] += d
+        start = place(ops, pred, succ, [new[kind[i]] + period * ops[i]["lv"][1] for i in range(n)], OPT["sets"][0], False)
+        order = sorted(range(n), key=lambda i: (start[i] if i >= len(LOADS) else -1.0, i))
+        score = sum(t / c for t, c in zip(length(ops, order), COST["CY"] * 30 + COST["GE"] * 25))
+        if cur is None or score <= cur: cur, off = score, new
+        if score < best[0]: best = (score, order, start)
+    return polish(ops, best[1], succ, rng)
+
+
+def polish(ops, order, succ, rng):
+    norm = list(COST["CY"] * 30 + COST["GE"] * 25); K = len(norm)
+    def score(od): return sum(t / c for t, c in zip(length(ops, od), norm))
+    cur = score(order); it = 0
+    while it < OPT["polish"]:
+        k = int(rng.integers(K)); wake = float(COST["WAKE"][k])
+        free = {}; prev = {}; seen = [0.0] * len(ops); why = [None] * len(ops); end = (0.0, 0)
+        for i in order:
+            o = ops[i]; t = free.get(o["q"], 0.0); w = (prev.get(o["q"]), True)
+            for d in o["far"]:
+                if seen[d] > t: t = seen[d]; w = (d, False)
+            why[i] = w; t += o["d"][k]; free[o["q"]] = t; prev[o["q"]] = i; t += o["l"][k]; seen[i] = t + wake
+            if t > end[0]: end = (t, i)
+        pairs = []; i = end[1]
+        while why[i][0] is not None:
+            if why[i][1]: pairs.append((why[i][0], i))
+            i = why[i][0]
+        pos = {i: m for m, i in enumerate(order)}
+        for m in rng.permutation(len(pairs))[:OPT["tries"]]:
+            i, j = pairs[m]; a, b = pos[i], pos[j]; it += 1
+            for _ in range(int(rng.integers(3))):
+                c = a - 1
+                while c >= 0 and ops[order[c]]["q"] != ops[j]["q"]: c -= 1
+                if c >= 0: a = c
+            if a < len(LOADS): continue
+            if all(pos[d] < a for d in ops[j]["deps"]): new = order[:a] + [j] + order[a:b] + order[b + 1:]
+            elif all(pos[d] > b for d in succ[i]): new = order[:pos[i]] + order[pos[i] + 1:b + 1] + [i] + order[b + 1:]
+            else: continue
+            sc = score(new)
+            if sc <= cur + 1e-9:
+                order, cur = new, sc
+                break
     return order
 
 
@@ -375,6 +567,8 @@ CACHE = {}
 def rank_program(g, core, T, topo):
     rank = T.rank_of(core)
     if rank is None:
+        for owner in T.cores:
+            if FOLDS and helper(owner, T, topo) == core: hand_back(g, core, T, topo, owner)
         return
     ops, stores = build(g, core, T, topo, rank)
     if "order" not in CACHE: CACHE["order"] = plan(ops)
@@ -384,6 +578,7 @@ def rank_program(g, core, T, topo):
     count = {q: 0 for q in csem}
     done = {}
     seen = {q: {} for q in eng}
+    first = {ops[i]["grp"]: i for i in order[::-1] if ops[i]["grp"]}
     last = {ops[i]["grp"]: i for i in order if ops[i]["grp"]}
     for i in order:
         o = ops[i]; q = o["q"]; need = {}
@@ -395,7 +590,7 @@ def rank_program(g, core, T, topo):
         for nm in waits:
             eng[q].wait_ge(T.sem[nm], need[nm][0]); seen[q][nm] = need[nm][0]
             for m, v in need[nm][1].items(): seen[q][m] = max(seen[q].get(m, 0), v)
-        res = o["fn"](last[o["grp"]] == i) if o["grp"] else o["fn"]()
+        res = o["fn"](last[o["grp"]] == i, not OPT["magic"] and first[o["grp"]] == i) if o["grp"] else o["fn"]()
         if o["sem"] is not None:
             if q != "G": res.then_inc(T.sem[o["sem"]], 16)
             done[i] = (o["sem"], o["val"], {})
@@ -405,6 +600,6 @@ def rank_program(g, core, T, topo):
             done[i] = ("c" + q, count[q], dict(seen[q]))
     g.sync.wait_ge(T.sem.st, 16 * stores[0])
     dst = T.cores[(rank - 1) % len(T.cores)]
-    g.wait_ge(T.sem.snt, 2 * (L - 1) * len(topo.engines(core, dst)))
+    g.wait_ge(T.sem.snt, 2 * (L - 1) * len(topo.engines(core, dst)) + len(FOLDS) * len(topo.engines(core, helper(core, T, topo))))
     for q in ("V", "S", "T", "G"):
         g.sync.wait_ge(csem[q], count[q])

@@ -10,44 +10,45 @@ OFF = 16384.0
 DL = 63.0 / 128.0
 BLK = [0, 2, 1, 3]
 CH = 256
-WL = 24
+WL = 36
+STEPS = [(0, 31.5), (2, 1.5 * 2 ** 29), (4, -1.5 * 2 ** 29), (7, -1.0), (8, 63.0), (12, 1.5 * 2 ** 23), (14, -1.5 * 2 ** 23 - 2048)]
 XW = 16 + CH
 SLOW = np.array([1.2, 1.0, 1.45, 1.05, 1.3])
 COST = dict(CY=0.83e-3 * SLOW, GE=0.83e-3 * SLOW * np.array([1.6, 1.35, 2.0, 1.2, 1.3]), PE=1e-3 * SLOW * np.array([0.45, 0.45, 0.45, 0.45, 0.5]),
             WAKE=np.array([0.24, 0.24, 0.2, 0.17, 0.3]), REMOTE=np.array([2.2, 1.9, 1.9, 1.6, 2.5]), YT=np.array([5.0, 4.3, 4.8, 4.3, 5.3]), FIX=0.0, SF=0.05, FIRST=1.2,
             FOLD=np.array([4.0, 3.5, 3.5, 3.5, 5.0]))
-PRI = dict(setup=-9.0, hints=2.0, reps=-5.0, reps1=3.0, mask=2.0, mstep=0.5, const=-3.0, z=-5.0, prep=-5.0, pen=0.5, search=0.0, post=-5.0, xup=-2.0, late=3.0, v=0.0, relu=0.5, mv=0.0)
-PRI.update(relu00=0.0, relu01=0.0, relu10=0.5, relu11=0.0, pen1=0.0, post1=0.0, lsS=0.0)
+PRI = dict(setup=-9.0, hints=2.0, reps=-5.0, reps1=3.0, mask=2.0, mstep=0.5, const=-3.0, z=-1.5, prep=-1.0, pen=0.0, search=0.0, post=1.5, xup=1.0, late=3.0, v=1.0, relu=0.5, mv=-0.5,
+           wait0=0.0, wait1=-1.0, post00=0.0, post01=0.0, vs=1.0)
+PRI.update(relu00=0.0, relu01=0.0, relu10=0.5, relu11=0.0, pen1=0.0, post1=-1.0, lsS=0.0)
 EACH = (256, 512, 768, 1024)
-OPT = dict(seed=1, rounds=60, sets=(1, 4), noise=0.6, polish=2000, periodic=600, same=4, tries=40, magic=1, xg=1, cV=0, dxA=1, rS00=0, rS01=0, rS10=0, rS11=0, vr00=0, vr01=0, vr10=0, vr11=0, ends={}, dxV=0, first=4, joint=1, share=1, nrelu00=EACH, nrelu01=EACH, nrelu10=EACH, nrelu11=EACH, cut00=(256,) * 4, cut01=(256,) * 4, cut10=(256,) * 4, cut11=(256,) * 4, rows=(4, 8, 12, 14, 15, 16), slack=0.2)
+OPT = dict(seed=1, back=0, part=16, rounds=30, sets=(1,), noise=0.3, polish=3000, periodic=150, same=4, tries=40, every=0.5, magic=1, xg=128, old=(), cV=0, dxA=1, rS00=0, rS01=0, rS10=0, rS11=0, vr00=0, vr01=0, vr10=0, vr11=0, ends={}, dxV=1, first=4, joint=1, share=1, nrelu00=EACH, nrelu01=EACH, nrelu10=EACH, nrelu11=EACH, cut00=(256,) * 4, cut01=(256,) * 4, cut10=(256,) * 4, cut11=(256,) * 4, rows=(4, 8, 12, 14, 15, 16), slack=0.2)
 
 SCRATCH = {
     "yt": ("sbuf", [128, NI], "bfloat16"), "x0": ("sbuf", [128, 2 * L, 32], "bfloat16"), "xf": ("sbuf", [128, R], "float32"),
     "rep0": ("sbuf", [128, 2 * L, XW], "bfloat16"), "xr": ("sbuf", [128, 2 * L, XW], "bfloat16"), "m16": ("sbuf", [128, 16], "bfloat16"),
-    "am": ("sbuf", [128, 48], "float32"), "hm": ("sbuf", [128, 24], "int32"), "hf": ("sbuf", [128, 24], "float32"),
-    "lh": ("sbuf", [128, 8], "int32"), "lob": ("sbuf", [128, 8], "float32"), "hab": ("sbuf", [128, 40], "int32"),
+    "am": ("sbuf", [128, 48], "float32"), "hm": ("sbuf", [128, L, 4], "int32"), "hf": ("sbuf", [128, L, 4], "float32"),
+    "lh": ("sbuf", [128, 8], "int32"), "lob": ("sbuf", [128, 8], "float32"), "hab": ("sbuf", [128, 2, L - 1, 4], "int32"),
     "hl": ("sbuf", [128, 48], "uint16"), "hr": ("sbuf", [128, 48], "uint16"), "mk": ("sbuf", [128, L * 128], "bfloat16"),
     "pi": ("sbuf", [128, 8], "int32"), "pj": ("sbuf", [128, 24], "int32"), "col": ("sbuf", [128, 16], "float32"),
-    "ctab": ("sbuf", [128, 160], "float32"), "gtab": ("sbuf", [128, 128], "float32"), "t2": ("sbuf", [128, 128], "float32"),
-    "e0": ("sbuf", [128, 128], "float32"), "qt": ("sbuf", [128, 512], "bfloat16"), "qw": ("sbuf", [128, 512], "float16"),
-    "bo": ("sbuf", [128, 128], "float16"), "bos": ("sbuf", [128, 128], "float16"), "bop": ("sbuf", [128, 128], "float16"),
-    "bon": ("sbuf", [128, 128], "float16"), "idh": ("sbuf", [128, 128], "float16"), "i4": ("sbuf", [128, 128], "float32"), "i64": ("sbuf", [128, 128], "float16"),
-    "rl": ("sbuf", [128, 18], "uint16"), "ri": ("sbuf", [128, 18], "int32"), "huge": ("sbuf", [128, 128], "bfloat16"),
+    "ctab": ("sbuf", [128, 160], "float32"), "gtab": ("sbuf", [128, 128], "float32"), "t2": ("sbuf", [128, 64], "float32"),
+    "e0": ("sbuf", [128, 128], "float32"), "qt": ("sbuf", [128, 512], "bfloat16"), "qw": ("sbuf", [128, 512], "bfloat16"),
+    "bo": ("sbuf", [128, 128], "bfloat16"), "bos": ("sbuf", [128, 128], "bfloat16"), "bw": ("sbuf", [128, 6, 128], "bfloat16"),
+    "i4": ("sbuf", [128, 128], "float32"), "z1t": ("sbuf", [128, 160], "bfloat16"),
+    "rl": ("sbuf", [128, 18], "uint16"), "ri": ("sbuf", [128, 18], "float32"), "huge": ("sbuf", [128, 128], "bfloat16"),
     "idb": ("sbuf", [128, 128], "bfloat16"), "idn": ("sbuf", [128, 128], "bfloat16"),
-    "c1": ("sbuf", [128, 256], "float16"), "c2": ("sbuf", [128, 128], "float16"), "zero": ("sbuf", [128, 128], "bfloat16"),
+    "c1": ("sbuf", [128, 128], "bfloat16"), "c2": ("sbuf", [128, 64], "bfloat16"), "zero": ("sbuf", [128, 128], "bfloat16"),
     "zs": ("sbuf", [128, 160], "bfloat16"), "zr": ("sbuf", [128, 160], "bfloat16"), "zd": ("sbuf", [128, 160], "bfloat16"),
-    "seg": ("sbuf", [128, 128], "float32"), "sgp": ("sbuf", [128, 64], "float32"), "sgn": ("sbuf", [128, 64], "float32"),
-    "fin": ("sbuf", [128, 3, 128], "float32"), "sgz": ("sbuf", [128, 64], "float32"),
+    "seg": ("sbuf", [128, 64], "float32"), "sgp": ("sbuf", [128, 64], "float32"), "sgn": ("sbuf", [128, 64], "float32"),
+    "ks": ("sbuf", [128, 2, 18 * 256], "float32"), "sgz": ("sbuf", [128, 64], "float32"),
     "Z": ("psum", [128, 512], "float32"), "X": ("psum", [128, 512], "float32"),
 }
-for _k in range(1, 8): SCRATCH["h%d" % _k] = ("sbuf", [128, 40], "int32")
+for _k in range(1, 8): SCRATCH["h%d" % _k] = ("sbuf", [128, L - 1, 8], "int32")
 for _p in range(2):
     SCRATCH["win%d" % _p] = ("sbuf", [128, WL * L], "float32")
     SCRATCH["as%d" % _p] = ("sbuf", [128, 32 * 64], "bfloat16")
     SCRATCH["ar%d" % _p] = ("sbuf", [128, 32 * 64], "bfloat16")
     SCRATCH["dv%d" % _p] = ("sbuf", [128, 32 * 64], "bfloat16")
     SCRATCH["rv%d" % _p] = ("sbuf", [128, 32 * 64], "bfloat16")
-    SCRATCH["ks%d" % _p] = ("sbuf", [128, 256], "float32")
     SCRATCH["wo%d" % _p] = ("sbuf", [128, 4 * L], "uint16")
     SCRATCH["dx%d" % _p] = ("sbuf", [128, 128], "bfloat16")
     SCRATCH["rh%d" % _p] = ("sbuf", [128, 128], "float16")
@@ -55,7 +56,7 @@ for _p in range(2):
     for _u in range(2): SCRATCH["K%d%d" % (_p, _u)] = ("psum", [128, 512], "float32")
     SCRATCH["R%d" % _p] = ("psum", [128, 512], "float32")
 for _s in range(3):
-    SCRATCH["ls%d" % _s] = ("sbuf", [128, 256], "float32")
+    SCRATCH["ls%d" % _s] = ("sbuf", [128, 128], "float32")
     SCRATCH["sc%d" % _s] = ("sbuf", [128, 8], "float32")
     SCRATCH["ofv%d" % _s] = ("sbuf", [128, 128], "uint16")
     SCRATCH["ofs%d" % _s] = ("sbuf", [128, 128], "uint16")
@@ -128,7 +129,7 @@ def build(g, core, T, topo, rank):
         ctx[0] = ("setup", 0, 0, len(ops) * 1e-3 - 1)
         add(q, 0.1, lambda: eng.dma_start(out, in_), (), (key,), sem="ld_" + key, val=16, lat=lat)
     small = [("lo", T.lh[:, 0:4], T.lo0[:]), ("hi", T.lh[:, 4:8], T.hi0[:]), ("x", T.x0[:], T.xrow[:]), ("home", T.hm[:], T.home[:]),
-             ("ha", T.hab[:, 0:20], T.ha[:]), ("hb", T.hab[:, 20:40], T.hb[:])]
+             ("ha", T.hab[:, 0, :, :], T.ha[:]), ("hb", T.hab[:, 1, :, :], T.hb[:])]
     for k, (key, out, in_) in enumerate(small[:OPT["first"]]): load(("SY", "S")[k % 2], key, out, in_, 1.1 + 0.3 * k)
     load("SY", "y", T.yt[:], T.ytab[:], COST["YT"])
     for key, out, in_ in small[OPT["first"]:]: load("SY", key, out, in_, COST["YT"])
@@ -141,18 +142,17 @@ def build(g, core, T, topo, rank):
     iota(T.gtab[:], [[16, 8], [0, 16]], 0, "gtab", 128)
     iota(T.ctab[:], [[1, 160]], 0, "ctab", 160)
     iota(T.e0[:], [[0, 8], [1, 16]], 0, "e0", 128)
-    iota(T.t2[:], [[0, 4], [1, 16], [0, 2]], 0, "t2", 128)
+    iota(T.t2[:], [[0, 4], [2, 8], [0, 2]], 0, "t2", 64)
     etab = T.ctab[:, 0:64]
     ts(T.pj[:, 0:8], T.pi[:], 15, None, A.bitwise_and, None, ["pi"], ["pj0"], 8)
-    ts(T.pj[:, 8:16], T.pi[:], 7, None, A.arith_shift_right, None, ["pi"], ["pj1"], 8)
-    ts(T.pj[:, 16:17], T.pi[:, 0:1], 112, None, A.bitwise_and, None, ["pi"], ["pj2"], 1)
-    ts(T.pj[:, 17:18], T.pi[:, 0:1], 127, None, A.bitwise_and, None, ["pi"], ["pj3"], 1)
+    ts(T.pj[:, 16:24], T.pi[:], 7, None, A.arith_shift_right, None, ["pi"], ["pj1"], 8)
+    ts(T.pj[:, 8:9], T.pi[:, 0:1], 112, None, A.bitwise_and, None, ["pi"], ["pj2"], 1)
+    ts(T.pj[:, 9:10], T.pi[:, 0:1], 14, None, A.bitwise_and, None, ["pi"], ["pj3"], 1)
     cp(T.hr[:, 0:8], T.pj[:, 0:8], ["pj0"], ["hr0"], 8)
-    cp(T.hl[:, 0:8], T.pj[:, 8:16], ["pj1"], ["hl0"], 8)
-    f16, g16, pp, zc, ab = [T.col[:, k:k + 1] for k in range(5)]
-    cp(f16, T.pj[:, 0:1], ["pj0"], ["f16"], 1)
-    cp(T.col[:, 1:3], T.pj[:, 16:18], ["pj2", "pj3"], ["g16", "pp"], 2)
-    ts(zc, g16, 15.0, None, A.add, None, ["g16"], ["zc"], 1)
+    cp(T.hl[:, 0:8], T.pj[:, 16:24], ["pj1"], ["hl0"], 8)
+    f16, g16, f14, pp, ab = [T.col[:, k:k + 1] for k in range(5)]
+    cp(T.col[:, 0:3], T.pj[:, 7:10], ["pj0", "pj2", "pj3"], ["f16", "g16"], 3)
+    cp(pp, T.pi[:, 0:1], ["pi"], ["pp"], 1)
     ts(ab, f16, 2.0, 1.0 / 64, A.is_lt, A.mult, ["f16"], ["ab"], 1)
     ts(T.col[:, 5:6], f16, 0.0, -1.0, A.is_equal, A.mult, ["f16"], ["a0"], 1)
     ts(T.col[:, 6:10], T.ctab[:, 0:64:16], ab, T.col[:, 5:6], A.mult, A.add, ["ctab", "ab", "a0"], ["a64"], 4)
@@ -160,52 +160,56 @@ def build(g, core, T, topo, rank):
         ts(T[nm][:, sl], T[src][:, sl], c, v, A.is_equal, A.mult, [src, ctok], [tok], n)
     table("bos", "gtab", "bosA", g16, "g16", -1.0, 64, slice(0, 128, 2))
     table("bos", "gtab", "bosB", g16, "g16", 1.0, 64, slice(1, 128, 2))
-    for nm, v in (("bo", 1.0), ("bop", 1.0 / 64), ("bon", -1.0 / 64)): table(nm, "gtab", nm, g16, "g16", v)
-    for nm, v in (("idb", 1.0), ("idh", 1.0), ("i4", 4.0) if OPT["magic"] else ("i64", 64.0)):
-        ts(T[nm][:], T.ctab[:, 0:128], pp, v, A.is_equal, A.mult, ["ctab", "pp"], [nm], 128)
-    table("zs", "ctab", "zs", zc, "zc", 64.0, 160)
-    for nm, src, v, n in (("zr", "zs", 2.0, 160), ("zd", "zs", -1.0, 160), ("idn", "idb", -1.0, 128)):
+    act(T.bo[:], T.bos[:], ["bosA", "bosB"], ["bo"], 128)
+    for par in range(2):
+        act(T.bw[:, par, :], T.bos[:], ["bosA", "bosB"], ["bw%d" % par], 128, scale=2.0 * par - 1, f=F.Relu)
+        act(T.bw[:, 2 + par, :], T.bos[:], ["bosA", "bosB"], ["bw%d" % (2 + par)], 128, scale=(2.0 * par - 1) / 64, f=F.Relu)
+        ts(T.bw[:, 4 + par, :], T.bos[:], (1 - 2.0 * par) / 64, 0.0, A.mult, A.min, ["bosA", "bosB"], ["bw%d" % (4 + par)], 128, 0.5)
+    ts(T.idb[:], T.ctab[:, 0:128], pp, None, A.is_equal, None, ["ctab", "pp"], ["idb"], 128)
+    ts(T.z1t[:], T.ctab[:], g16, 15.0, A.subtract, A.is_equal, ["ctab", "g16"], ["z1t"], 160)
+    for nm, src, v, n in (("zs", "z1t", 64.0, 160), ("zr", "z1t", 128.0, 160), ("zd", "z1t", -64.0, 160), ("idn", "idb", -1.0, 128), ("i4", "idb", 4.0, 128)):
         act(T[nm][:], T[src][:], [src], [nm], n, scale=v, f=F.Identity)
     for c in range(4):
         q = T.qt[:, 128 * c:128 * c + 128]
         act(q, T.e0[:], ["e0", "ab", "a64"], ["qt%d" % c], 128, bias=T.col[:, 6 + c:7 + c], scale=ab, f=F.Identity)
         tt(T.qw[:, 128 * c:128 * c + 128], q, T.bo[:], A.mult, ["qt%d" % c, "bo"], ["qw%d" % c], 128, 1.0)
     QWT = ["qw%d" % c for c in range(4)]
-    ts(T.c1[:, 128:256], T.t2[:], f16, -OFF, A.not_equal, A.mult, ["t2", "f16"], ["c1b"], 128)
-    ts(T.c1[:, 0:128], T.c1[:, 128:256], -1.0, 2048.0, A.mult, A.max, ["c1b"], ["c1a"], 128, 0.5)
-    ts(T.c2[:], T.gtab[:], 0.0, -DL, A.mult, A.add, ["gtab"], ["c2"], 128)
-    if OPT["magic"]:
-        ms(T.zero[:], -30.0, ["zero"], 64)
-        ms(T.huge[:], 1.5 * 2 ** 29, ["huge"], 64)
-    if OPT["xg"]:
-        ts(T.ri[:], T.ctab[:, 0:18], 1.0, 16.0, A.min, A.mult, ["ctab"], ["ri"], 18)
-        ts(T.rl[:], T.ri[:], f16, None, A.add, None, ["ri", "f16"], ["rl"], 18)
+    ts(T.c1[:, 64:128], T.t2[:], f14, -OFF, A.not_equal, A.mult, ["t2", "f16"], ["c1b"], 64)
+    act(T.c1[:, 0:64], T.c1[:, 64:128], ["c1b"], ["c1a"], 64, scale=2048.0 / OFF - 1, bias=2048.0, f=F.Identity)
+    def fill(out, v, src, r, w, n): act(out, src, r, w, n, scale=0.0, bias=v, f=F.Identity)
+    fill(T.c2[:], -DL, T.gtab[:, 0:64], ["gtab"], ["c2"], 64)
+    fill(T.zero[:], -30.0, T.gtab[:], ["gtab"], ["zero"], 128)
+    fill(T.huge[:], 1.5 * 2 ** 29, T.gtab[:], ["gtab"], ["huge"], 128)
+    act(T.ri[:], T.ctab[:, 0:18], ["ctab"], ["ri"], 18, f=F.Sign)
+    ts(T.rl[:], T.ri[:], 16.0, f16, A.mult, A.add, ["ri", "f16"], ["rl"], 18)
     ts(T.m16[:], T.ctab[:, 0:16], f16, None, A.is_equal, None, ["ctab", "f16"], ["m16"], 16)
-    ms(T.fin[:], 1.0, ["fin0"], 384)
-    for o, v in ((1, 63.0), (3, 1.5 * 2 ** 23), (4, -1.5 * 2 ** 23 - 2048)): ms(T.fin[:, :, o:64:16], v, ["fin"], 12, ["fin0"])
-    for nm, n, st, v0, v1 in (("seg", 128, 64, -1.0, BIG), ("sgp", 64, 32, 0.0, BIG), ("sgn", 64, 32, 0.0, -BIG), ("sgz", 64, 2, 0.0, -BIG)):
-        ms(T[nm][:], v0, [nm + "0"], n)
-        ms(T[nm][:, 0:n:st], v1, [nm], n // st, [nm + "0"])
+    ms(T.ks[:, :, 63:18 * 256:64], 1.0, ["fin0"], 144)
+    for k, (row, v) in list(enumerate(STEPS))[::-1]:
+        fill(T.ks[:, :, 256 * row + 63:256 * row + 256:64], v, T.x0[:, 0:2, 0:4], ["x", "fin0"] + ([] if k else ["fin.%d" % m for m in range(1, len(STEPS))]), ["fin.%d" % k if k else "fin"], 8)
+    ms(T.seg[:], -1.0, ["seg0"], 64)
+    ms(T.seg[:, 0:1], BIG, ["seg"], 1, ["seg0"])
+    ts(T.sgp[:], T.e0[:, 0:64], 0.0, BIG, A.is_equal, A.mult, ["e0"], ["sgp"], 64)
+    act(T.sgn[:], T.sgp[:], ["sgp"], ["sgn"], 64, scale=-1.0, f=F.Identity)
+    ms(T.sgz[:], 0.0, ["sgz0"], 64)
+    ms(T.sgz[:, 0:64:2], -BIG, ["sgz"], 32, ["sgz0"])
 
     ts(T.lob[:], T.lh[:], -2048.0, None, A.add, None, ["lo", "hi"], ["lob"], 8)
-    for k, a in enumerate(BLK): cp(T.hf[:, k:24:4], T.hm[:, a:24:4], ["home"], ["hf%d" % k], 6)
-    HF = ["hf%d" % k for k in range(4)]
+    for k in range(2): cp(T.hf[:, :, 2 * k:2 * k + 2], T.hm[:, :, k:4:2], ["home"], ["hf%d" % k], 12)
+    HF = ["hf0", "hf1"]
     def masks(l, tok):
         act(T.mk[:, 128 * l:128 * l + 128], T.m16[:].indirect(T.hr[:, 8 * l:8 * l + 8]), ["m16", tok], ["mk%d" % l], 128, f=F.Identity, gather=True)
     masks(0, "hr0")
     ctx[0] = ("hints", 0, 0, 0); HT = []
     for h, nm in enumerate(("ha", "hb")):
-        for k, a in enumerate(BLK):
-            cp(T.h1[:, 4 * h + k:40:8], T.hab[:, 20 * h + a:20 * h + 20:4], [nm], ["h1.%d%d" % (h, k)], 5); HT.append("h1.%d%d" % (h, k))
-    ts(T.h2[:], T.h1[:], 4, None, A.arith_shift_right, None, HT, ["h2"], 40)
-    ts(T.h3[:], T.h2[:], 24.0, -24.0, A.is_ge, A.mult, ["h2"], ["h3"], 40)
-    tt(T.h4[:], T.h2[:], T.h3[:], A.add, ["h2", "h3"], ["h4"], 40)
-    ts(T.h5[:], T.h4[:], 28, None, A.bitwise_and, None, ["h4"], ["h5"], 40)
-    ts(T.h3[:], T.h2[:], 24.0, -20.0, A.is_ge, A.mult, ["h2"], ["h3"], 40)
-    tt(T.h6[:], T.h2[:], T.h3[:], A.add, ["h2", "h3"], ["h6"], 40)
-    ts(T.h3[:], T.h5[:], 5.0, 16.0, A.mult, A.add, ["h5"], ["h3"], 40)
-    tt(T.h4[:], T.h3[:], T.h6[:], A.add, ["h3", "h6"], ["h4"], 40)
-    cp(T.hl[:, 8:48], T.h4[:], ["h4"], ["hl"], 40)
+        for k in range(2):
+            cp(T.h1[:, :, 4 * h + 2 * k:4 * h + 2 * k + 2], T.hab[:, h, :, k:4:2], [nm], ["h1.%d%d" % (h, k)], 10); HT.append("h1.%d%d" % (h, k))
+    ts(T.h2[:], T.h1[:], 6, None, A.arith_shift_right, None, HT, ["h2"], 40)
+    ts(T.h3[:], T.h1[:], 4, 3, A.arith_shift_right, A.bitwise_and, HT, ["h3"], 40)
+    ts(T.h4[:], T.h1[:], float(R), 4.0 - L * WL, A.is_ge, A.mult, HT, ["h4"], 40)
+    ts(T.h5[:], T.h2[:], float(WL), WL - 8.0, A.mult, A.add, ["h2"], ["h5"], 40)
+    tt(T.h6[:], T.h3[:], T.h4[:], A.add, ["h3", "h4"], ["h6"], 40)
+    tt(T.h2[:], T.h5[:], T.h6[:], A.add, ["h5", "h6"], ["h2"], 40)
+    cp(T.hl[:, 8:48], T.h2[:], ["h2"], ["hl"], 40)
     ts(T.h7[:], T.h1[:], 15, None, A.bitwise_and, None, HT, ["h7"], 40)
     cp(T.hr[:, 8:48], T.h7[:], ["h7"], ["hr"], 40)
     for l in range(1, L):
@@ -221,14 +225,16 @@ def build(g, core, T, topo, rank):
     def reptok(l): return "rep%d.%d" % (2 if l else 0, CH)
 
     def sets(p, l): return 2 if l == 0 else p
-    def B1(s, k): return T["ls%d" % s][:, 32 * k + 31:32 * k + 32]
-    def DD(s, k): return T["ls%d" % s][:, 128 + 32 * k + 31:128 + 32 * k + 32]
+    def against0(p, l, u): return p == 1 and (l == 0 or u in OPT["old"])
+    def B1(s, k): return T["ls%d" % s][:, 16 * k + 15:16 * k + 16]
+    def DD(s, k): return T["ls%d" % s][:, 64 + 16 * k + 15:64 + 16 * k + 16]
 
     def prep(p, l):
         s = sets(p, l); P = "%d" % p; t = "%d." % s; Rb = T["R" + P]; rh = T["rh" + P]; z = T["z" + P]; ls = T["ls%d" % s]; sc = T["sc%d" % s]
         at = 0 if l else -2 * p
         ctx[0] = ("const", p, l, at)
-        mms([(Rb[:, 0:256], T.idh[:], T.c1[:], 256, True, False), (Rb[:, 0:128], T.idh[:], T.c2[:], 128, False, False)], ["idh", "c1a", "c1b", "c2"], ["R" + P])
+        mms([(Rb[:, 0:128], T.idb[:], T.c1[:], 128, True, False), (Rb[:, 0:64], T.idb[:], T.c2[:], 64, False, False)], ["idb", "c1a", "c1b", "c2"], ["R" + P])
+        if l: at = PRI["wait%d" % p]
         ctx[0] = ("z", p, l, at)
         if l == 0: win, wt = T.lob[:], ["lob", "hl0"]
         else: win, wt = T["win" + P][:, 0:WL * l], ["hl"] + ["w%d.%d.%d" % (p, k, x) for k in range(l) for x in range(5)]
@@ -238,25 +244,23 @@ def build(g, core, T, topo, rank):
         mms([(T.Z[:, 64 + c:192:4], T.qw[:, 128 * c:128 * c + 128], z[:, 1:64:2], 32, True, True) for c in range(4)], QWT + ["z" + P], ["Z"])
         ts(T["ofs%d" % s][:], T.Z[:, 64:192], 2048.0 - DL, None, A.add, None, ["Z"], ["ofs%d" % s], 128)
         ctx[0] = ("prep", p, l, at)
-        a, b = rh[:, 0:64], rh[:, 64:128]
-        mms([(Rb[:, 0:128:2], T.bo[:], a, 64, False, False), (Rb[:, 1:128:2], T.bo[:], b, 64, False, False),
-             (Rb[:, 128:256:2], T.bop[:], a, 64, False, False), (Rb[:, 128:256:2], T.bon[:], b, 64, False, False),
-             (Rb[:, 129:256:2], T.bon[:], a, 64, False, False), (Rb[:, 129:256:2], T.bop[:], b, 64, False, True)], ["bo", "bop", "bon", "rh" + P, "R" + P], ["R" + P])
-        for h in (1, 0):
-            ctx[0] = ("prep", p, l, at + (1 - h) * PRI["lsS"])
-            scan(ls[:, 64 * h:64 * h + 64], T.sgp[:], Rb[:, 64 * h:64 * h + 64], A.min, ["sgp", "R" + P], [t + "B%d" % h], 64)
-            scan(ls[:, 128 + 64 * h:192 + 64 * h], T.sgn[:], Rb[:, 128 + 64 * h:192 + 64 * h], A.max, ["sgn", "R" + P], [t + "D%d" % h], 64)
+        mms([(Rb[:, o:o - o % 2 + 64:2], T.bw[:, 2 * m + par, :], rh[:, 64 * h + par:64 * h + 64:2], 32, False, par + h + m == 4)
+             for par in range(2) for h in range(2) for m, o in enumerate((h, 64 + h, 65 - h))], ["bw%d" % m for m in range(6)] + ["rh" + P, "R" + P], ["R" + P])
+        scan(ls[:, 0:64], T.sgp[:], Rb[:, 0:64], A.min, ["sgp", "R" + P], [t + "B"], 64)
+        scan(ls[:, 64:128], T.sgn[:], Rb[:, 64:128], A.max, ["sgn", "R" + P], [t + "D"], 64)
         for u in range(2):
             ctx[0] = ("prep", p, l, at + u * PRI["lsS"])
-            ts(T["ofv%d" % s][:, 64 * u:64 * u + 64], etab, DD(s, 2 + u), B1(s, 2 + u), A.mult, A.add, ["ctab", t + "B1", t + "D1"], ["ofv%d.%d" % (s, u)], 64)
-        ctx[0] = ("pen", p, l, p * PRI["pen1"] if l else -6); bt = [t + "B0", t + "B1"]
-        if OPT["cV"]: cp(T.fin[:, s, 2:128:16], ls[:, 31:256:32], bt + [t + "D0", t + "D1", "fin"], [t + "C"], 8)
-        else: act(T.fin[:, s, 2:128:16], ls[:, 31:256:32], bt + [t + "D0", t + "D1", "fin"], [t + "C"], 8, f=F.Identity)
-        tt(sc[:, 4:8], ls[:, 31:128:32], T.hf[:, 4 * l:4 * l + 4], A.subtract, bt + HF, [t + "H"], 4)
+            ts(T["ofv%d" % s][:, 64 * u:64 * u + 64], etab, DD(s, 2 + u), B1(s, 2 + u), A.mult, A.add, ["ctab", t + "B", t + "D"], ["ofv%d.%d" % (s, u)], 64)
+        ctx[0] = ("pen", p, l, p * PRI["pen1"] if l else -6)
+        for q in ([p] if l else [0, 1]):
+            o = T.ks[:, q, 10 * 256 + 63:12 * 256:64]
+            if OPT["cV"]: cp(o, ls[:, 15:128:16], [t + "B", t + "D", "fin"], ["C%d" % q], 8)
+            else: act(o, ls[:, 15:128:16], [t + "B", t + "D", "fin"], ["C%d" % q], 8, f=F.Identity)
+        tt(sc[:, 4:8], ls[:, 15:64:16], T.hf[:, l, :], A.subtract, [t + "B"] + HF, [t + "H"], 4)
         pa = T["pa%d" % s]
         for k in range(4):
             o = 128 * (k % 2) + 64 * (k // 2)
-            act(pa[:, o:o + 64], etab, ["ctab", t + "D%d" % (k // 2), t + "H"], ["pa%d.%d" % (s, k)], 64, bias=sc[:, 4 + k:5 + k], scale=DD(s, k))
+            act(pa[:, o:o + 64], etab, ["ctab", t + "D", t + "H"], ["pa%d.%d" % (s, k)], 64, bias=sc[:, 4 + k:5 + k], scale=DD(s, k))
         if not OPT["magic"]:
             ts(T["pn%d" % s][:], pa[:], 1.0 / 16, 1280.0 - 15.0 / 32, A.mult, A.add, ["pa%d.%d" % (s, k) for k in range(4)], ["pn%d" % s], 256)
 
@@ -269,7 +273,7 @@ def build(g, core, T, topo, rank):
     if FOLDS:
         ctx[0] = ("reps1", 0, 0, 0); ms(T.zw[:], 0.0, ["zw"], 512)
 
-    KEYS = ["s%d" % i for i in range(16)] + ["d", "r", "p"]
+    KEYS = ["s%d" % i for i in range(16)] + ["%s%d" % (x, h) for x in "dr" for h in range(0, 16, OPT["part"])] + ["p"]
 
     def search(p, l, u):
         ctx[0] = ("search", p, l, u); s = sets(p, l)
@@ -303,46 +307,46 @@ def build(g, core, T, topo, rank):
         pd = 0 if shared else p
         dv, rv = T["dv%d" % pd], T["rv%d" % p]; d0 = 1024 * u; nr = OPT["nrelu%d%d" % (p, u)]
         rep = T["xr" if p else "rep0"][:, o1, 16:XW]
-        REP = reptok(l); rt = REP if p == 0 else xt
-        if shared:
-            Rb = T["R%d" % u]
-            mms([(Rb[:, 0:CH], T.idb[:], rep, CH, True, False), (Rb[:, 0:CH], T.idn[:], T.rep0[:, o1, 16:XW], CH, False, True)], ["idb", "idn", rt, REP], ["R%d" % u])
+        REP = reptok(l); rt = REP if p == 0 else xt + "w"
+        old = against0(p, l, u); m = OPT["xg"]
+        if old:
+            bank = "R%d" % u if shared else "X"; Rb = T[bank]
+            mms([(Rb[:, 0:m], T.idb[:], T.xr[:, o1, 16:16 + m], m, True, False), (Rb[:, 0:m], T.idn[:], T.rep0[:, o1, 16:16 + m], m, False, True)], ["idb", "idn", xt, REP], [bank])
         tok = lambda kind, q, a, b: ["%sv%d.%d" % (kind, q, m) for m in range(a, b, 128)]
         d = e = d0
         for n in ((CH,) * 4 if l == 0 else OPT["cut%d%d" % (p, u)]):
-            ctx[0] = ("search", p, l, u + (d - d0) / 1024 - PRI["v"]); f = d + n
-            if shared: tt(rv[:, d:f], dv[:, d:f], Rb[:, 0:n], A.max, tok("d", 0, d, f) + ["R%d" % u], tok("r", 1, d, f), n, 1.0)
-            else:
-                tt(dv[:, d:f], T.yt[:].indirect(T["ofv%d" % s][:, d // 16:f // 16]), T["xr" if p else "rep0"][:, o1, 16:16 + n], A.subtract,
-                   ["y", "ofv%d.%d" % (s, u), rt], tok("d", p, d, f), n, gather=True)
-                if f - d0 in nr:
-                    ctx[0] = ("search", p, l, u + PRI["relu"] + (d - d0) / 1024 - PRI["v"])
-                    ts(rv[:, e:f], dv[:, e:f], 0.0, None, A.max, None, tok("d", p, e, f), tok("r", p, e, f), f - e, 0.5); e = f
+            ctx[0] = ("search", p, l, PRI["vs"] * d / 1024 - PRI["v"]); f = d + n
+            if not shared:
+                tt(dv[:, d:f], T.yt[:].indirect(T["ofv%d" % s][:, d // 16:f // 16]), T["xr" if p and not old else "rep0"][:, o1, 16:16 + n], A.subtract,
+                   ["y", "ofv%d.%d" % (s, u), REP if old else xt if p and n <= m else rt], tok("d", p, d, f), n, gather=True)
+            ctx[0] = ("search", p, l, PRI["relu"] + PRI["vs"] * d / 1024 - PRI["v"])
+            if old:
+                for q in range(d, f, m): tt(rv[:, q:q + m], dv[:, q:q + m], Rb[:, 0:m], A.max, tok("d", pd, q, q + m) + [bank], tok("r", 1, q, q + m), m, 1.0)
+            elif f - d0 in nr:
+                ts(rv[:, e:f], dv[:, e:f], 0.0, None, A.max, None, tok("d", p, e, f), tok("r", p, e, f), f - e, 0.5); e = f
             d = f
-        ctx[0] = ("search", p, l, u + PRI["mv"])
+        ctx[0] = ("search", p, l, PRI["vs"] * u + PRI["mv"])
         for kind, buf, z, pb in (("d", dv, "zd", pd), ("r", rv, "zr", p)):
-            mms([(K[:, 64:128], T[z][:, 15 - i:143 - i], buf[:, d0 + i:d0 + 1024:16], 64, False, None) for i in range(16)],
-                [z, kt("0")] + tok(kind, pb, d0, d0 + 1024) + ([] if kind == "d" else [kt("d")] + [kt("p")] * shared), [kt(kind)], grp)
+            for h in range(0, 16, OPT["part"]):
+                mms([(K[:, 64:128], T[z][:, 15 - i:143 - i], buf[:, d0 + i:d0 + 1024:16], 64, False, None) for i in range(h, h + OPT["part"])],
+                    [z, kt("0")] + tok(kind, pb, d0, d0 + 1024) + ([] if kind == "d" else [kt("d%d" % h)] + [kt("p")] * old), [kt("%s%d" % (kind, h))], grp)
 
     def post(p, l, us):
-        ctx[0] = ("post", p, l, us[0] + p * PRI["post1"]); s = sets(p, l); P = "%d" % p; ks = T["ks" + P]; t = "%d." % s; w = T["win" + P]
-        for u in us:
-            scan(ks[:, 128 * u:128 * u + 128], T.seg[:], T["K%d%d" % (p, u)][:, 0:128], A.min, ["K%d%d.%s" % (p, u, q) for q in KEYS] + ["seg"], ["ks%d.%d" % (p, u)], 128)
+        ctx[0] = ("post", p, l, us[0] + p * PRI["post1"] + (1 - us[0]) * PRI["post0%d" % p]); s = sets(p, l); P = "%d" % p; w = T["win" + P]
         c0, c1 = 2 * us[0], 2 * us[-1] + 2; c = slice(c0, c1)
         for a in range(c0, c1):
-            k = BLK.index(a); u = a // 2; K = T["K%d%d" % (p, u)]
-            add("V", sv(64), lambda k=k, a=a, K=K: V.tensor_reduce(T.fin[:, s, 16 * k:16 * k + 1], K[:, 64 * (a % 2):64 * (a % 2) + 64], AxisListType.X, A.min, negate=True),
-                ["K%d%d.%s" % (p, u, q) for q in KEYS] + ["fin"], [t + "r%d" % k])
+            o = 6 * 256 + 64 * BLK.index(a); u = a // 2
+            scan(T.ks[:, p, o:o + 64], T.seg[:], T["K%d%d" % (p, u)][:, 64 * (a % 2):64 * (a % 2) + 64], A.min, ["K%d%d.%s" % (p, u, q) for q in KEYS] + ["seg", "fin"], ["ks%d.%d" % (p, a)], 64)
         for a in range(c0, c1):
-            k = BLK.index(a)
-            add("V", sv(5), lambda k=k, a=a: V.tensor_tensor_scan(w[:, WL * l + a:WL * l + 20:4], T.fin[:, s, 16 * k:16 * k + 5], T.fin[:, s, 65 + 16 * k:70 + 16 * k], ks[:, 64 * a + 63:64 * a + 64], A.add, A.mult),
-                ["ks%d.%d" % (p, a // 2), t + "r%d" % k, t + "C", "fin"], ["w%d.%d.%d" % (p, l, a)])
+            o = 64 * BLK.index(a) + 63
+            add("V", sv(8), lambda o=o, a=a: V.tensor_tensor_scan(w[:, WL * l + a:WL * l + WL - 4:4], T.ks[:, p, o:16 * 256:512], T.ks[:, p, 768 + o:18 * 256:512], T.ks[:, p, 6 * 256 + o:6 * 256 + o + 1], A.add, A.mult),
+                ["ks%d.%d" % (p, a), "C%d" % p, "fin"], ["w%d.%d.%d" % (p, l, a)])
 
     def left(p, l, us):
         ctx[0] = ("xup" if p == 0 else "late", p, l, us[0]); P = "%d" % p; c0, c1 = 2 * us[0], 2 * us[-1] + 2
         yk = ["dx%d.%d" % (p, u) for u in us]
         wo = T["wo" + P][:, 4 * l + c0:4 * l + c1]; wk = ["wo%d.%d.%d" % (p, l, u) for u in us]
-        ts(wo, T["win" + P][:, WL * l + 16 + c0:WL * l + 16 + c1], 2048.0, None, A.add, None, ["w%d.%d.%d" % (p, l, a) for a in range(c0, c1)], wk, 4)
+        ts(wo, T["win" + P][:, WL * l + WL - 8 + c0:WL * l + WL - 8 + c1], 2048.0, None, A.add, None, ["w%d.%d.%d" % (p, l, a) for a in range(c0, c1)], wk, 4)
         yw = T["dx" + P]; n = 16 * (c1 - c0); o = 16 * c0
         if p == 1 and (OPT["dxV"] or l == L - 1):
             for u in us:
@@ -353,7 +357,10 @@ def build(g, core, T, topo, rank):
             o1 = 2 * l + us[0]
             tt(yw[:, o:o + n], T.yt[:].indirect(wo), T.x0[:, o1, :], A.subtract, ["y", "x"] + wk, yk, n, gather=True)
             if OPT["xg"]:
-                act(T.xr[:, o1, :], yw[:, o:o + 32].indirect(T.rl[:, 0:XW // 16]), ["rl"] + yk, ["xr%d.%d" % (l, us[0])], XW, gather=True)
+                m = OPT["xg"]; xt = "xr%d.%d" % (l, us[0])
+                act(T.xr[:, o1, 0:16 + m], yw[:, o:o + 32].indirect(T.rl[:, 0:1 + m // 16]), ["rl"] + yk, [xt, xt + "w"], 16 + m, gather=True)
+                while m < CH and not against0(1, l, us[0]):
+                    cp(T.xr[:, o1, 16 + m:16 + 2 * m], T.xr[:, o1, 16:16 + m], [xt + "w"], [xt + "w"], m, 0.5); m *= 2
                 return
             mms([(T.X[:, 0:32], T.idb[:], yw[:, o:o + 32], 32, True, True)] + [(T.X[:, k:k + 16], T.idb[:], yw[:, o + 16:o + 32], 16, True, True) for k in range(32, XW, 16)], ["idb"] + yk, ["X"])
             act(T.xr[:, o1, :], T.X[:, 0:XW], ["X"], ["xr%d.%d" % (l, us[0])], XW)
@@ -376,7 +383,7 @@ def build(g, core, T, topo, rank):
         rid, pid, _ = topo.addr(dst)
         m = topo.mask(core, dst)
         def fn():
-            G.remote_dma(w[:, WL * l + 20:WL * l + 24], w[:, WL * l + 16:WL * l + 20], T.sem["arr%d_%d" % (p, l)], T.sem.snt, pid, rid, m)
+            G.remote_dma(w[:, WL * l + WL - 4:WL * l + WL], w[:, WL * l + WL - 8:WL * l + WL - 4], T.sem["arr%d_%d" % (p, l)], T.sem.snt, pid, rid, m)
         add("G", 0.6, fn, ["w%d.%d.%d" % (p, l, a) for a in range(4)], ["w%d.%d.4" % (p, l)], n=0, sem="arr%d_%d" % (p, l), val=len(topo.engines(core, dst)),
             lat=COST["REMOTE"] + (0.0 if p + l else COST["FIRST"]))
 
@@ -392,7 +399,7 @@ def build(g, core, T, topo, rank):
         p, l = k % 2, k // 2; lv[0] = (p, l)
         if l: prep(p, l)
         for u in range(2): search(p, l, u)
-        for us in ([[0, 1]] if p and OPT["joint"] and l < L - 1 else [[0], [1]]): post(p, l, us)
+        for us in [[0], [1]]: post(p, l, us)
         if l < L - 1: send(p, l)
         for us in ([[0, 1]] if p and l < L - 1 else [[0], [1]]): left(p, l, us)
         ctx[0] = ("late", p, l, 0)
@@ -492,12 +499,19 @@ def plan(ops):
         o["d"] = [float(x) for x in o["dur"] * one]; o["l"] = [float(x) for x in o["lat"] * one]
         o["far"] = [d for d in o["deps"] if not (o["q"] == "T" and ops[d]["q"] == "T")]
         for d in o["deps"]: succ[d].append(i)
+    above = []
+    for o in ops:
+        far = 0
+        for d in o["far"]: far |= above[d]
+        o["far"] = [d for d in o["far"] if not far >> d & 1]
+        for d in o["deps"]: far |= above[d] | 1 << d
+        above.append(far)
     rng = np.random.default_rng(OPT["seed"]); best = None
     key = [3.0 * due(o["tag"]) + 1e-4 * i for i, o in enumerate(ops)]
     for it in range(OPT["rounds"]):
         k = OPT["sets"][int(rng.integers(len(OPT["sets"])))]
         start = place(ops, pred, succ, key, k, False)
-        if it % 2 == 0:
+        if it % 2 == OPT["back"]:
             back = place(ops, succ, pred, [-start[i] - ops[i]["d"][k] for i in range(n)], k, True)
             start = place(ops, pred, succ, [-back[i] - ops[i]["d"][k] for i in range(n)], k, False)
         order = sorted(range(n), key=lambda i: (start[i] if i >= len(LOADS) else -1.0, i))
@@ -530,6 +544,23 @@ def polish(ops, order, succ, rng):
     norm = list(COST["CY"] * 30 + COST["GE"] * 25); K = len(norm)
     def score(od): return sum(t / c for t, c in zip(length(ops, od), norm))
     cur = score(order); it = 0
+    count = {}; name = []
+    for o in ops:
+        count[o["lv"]] = count.get(o["lv"], 0) + 1; name.append(o["lv"] + (count[o["lv"]],))
+    twin = {nm: i for i, nm in enumerate(name) if nm[0] >= 0 and 1 <= nm[1] <= OPT["same"]}
+    def move(od, i, j, hop, down):
+        a, b = od.index(i), od.index(j); q = ops[i]["q"]
+        if a > b: return None
+        for _ in range(hop):
+            c = b + 1 if down else a - 1
+            while 0 <= c < len(od) and ops[od[c]]["q"] != q: c += 1 if down else -1
+            if not len(LOADS) <= c < len(od): break
+            if down: b = c
+            else: a = c
+        if a < len(LOADS): return None
+        between = set(od[a:b + 1])
+        if down: return None if any(d in between for d in succ[i]) else od[:a] + od[a + 1:b + 1] + [i] + od[b + 1:]
+        return None if any(d in between for d in ops[j]["deps"]) else od[:a] + [j] + od[a:b] + od[b + 1:]
     while it < OPT["polish"]:
         k = int(rng.integers(K)); wake = float(COST["WAKE"][k])
         free = {}; prev = {}; seen = [0.0] * len(ops); why = [None] * len(ops); end = (0.0, 0)
@@ -543,17 +574,15 @@ def polish(ops, order, succ, rng):
         while why[i][0] is not None:
             if why[i][1]: pairs.append((why[i][0], i))
             i = why[i][0]
-        pos = {i: m for m, i in enumerate(order)}
+        order = order[:len(LOADS)] + sorted(order[len(LOADS):], key=lambda i: seen[i] - ops[i]["l"][k] - ops[i]["d"][k])
         for m in rng.permutation(len(pairs))[:OPT["tries"]]:
-            i, j = pairs[m]; a, b = pos[i], pos[j]; it += 1
-            for _ in range(int(rng.integers(3))):
-                c = a - 1
-                while c >= 0 and ops[order[c]]["q"] != ops[j]["q"]: c -= 1
-                if c >= 0: a = c
-            if a < len(LOADS): continue
-            if all(pos[d] < a for d in ops[j]["deps"]): new = order[:a] + [j] + order[a:b] + order[b + 1:]
-            elif all(pos[d] > b for d in succ[i]): new = order[:pos[i]] + order[pos[i] + 1:b + 1] + [i] + order[b + 1:]
-            else: continue
+            i, j = pairs[m]; it += 1
+            hop, down, every = int(rng.integers(3)), rng.random() < 0.5, rng.random() < OPT["every"]
+            new = order
+            for s in (range(-L, L) if every else [0]):
+                i2, j2 = (twin.get((name[i][0], name[i][1] + s, name[i][2])), twin.get((name[j][0], name[j][1] + s, name[j][2]))) if s else (i, j)
+                if i2 is not None and j2 is not None: new = move(new, i2, j2, hop, down) or new
+            if new is order: continue
             sc = score(new)
             if sc <= cur + 1e-9:
                 order, cur = new, sc

import numpy as np
from concourse.bass import DstId, RemoteDMATransfer
from concourse.mybir import AluOpType, AxisListType, ActivationFunctionType

A = AluOpType
F = ActivationFunctionType
L, R, NI = 6, 384, 4096
BIG = float(2 ** 22)
OFF = 16384.0
DL = 63.0 / 128.0
BLK = [0, 2, 1, 3]
CH = 256
WL = 36
STEPS = [(0, 31.5), (2, 1.5 * 2 ** 29), (4, -1.5 * 2 ** 29), (7, -1.0), (8, 63.0), (12, 1.5 * 2 ** 23), (14, -1.5 * 2 ** 23 - 2048)]
XW = 16 + CH
SLOW = np.array([1.2, 1.0, 1.45, 1.05, 1.3])
COST = dict(CY=0.83e-3 * SLOW, GE=0.83e-3 * SLOW * np.array([1.6, 1.35, 2.0, 1.2, 1.3]), PE=1e-3 * SLOW * np.array([0.45, 0.45, 0.45, 0.45, 0.5]),
            WAKE=np.array([0.24, 0.24, 0.2, 0.17, 0.3]), REMOTE=np.array([2.2, 1.9, 1.9, 1.6, 2.5]), YT=np.array([5.0, 4.3, 4.8, 4.3, 5.3]), FIX=0.0, SF=0.05, FIRST=1.2,
            FOLD=np.array([4.0, 3.5, 3.5, 3.5, 5.0]))
PRI = dict(setup=-9.0, hints=2.0, reps=-5.0, reps1=3.0, mask=2.0, mstep=0.5, const=-3.0, z=-1.5, prep=-1.0, pen=0.0, search=0.0, post=1.5, xup=1.0, late=3.0, v=1.0, relu=0.5, mv=-0.5,
           wait0=0.0, wait1=-1.0, post00=0.0, post01=0.0, vs=1.0)
PRI.update(relu00=0.0, relu01=0.0, relu10=0.5, relu11=0.0, pen1=0.0, post1=-1.0, lsS=0.0)
EACH = (256, 512, 768, 1024)
OPT = dict(seed=1, back=0, part=16, rounds=30, sets=(1,), noise=0.3, polish=3000, periodic=150, same=4, tries=40, every=0.5, magic=1, xg=128, old=(), cV=0, dxA=1, rS00=0, rS01=0, rS10=0, rS11=0, vr00=0, vr01=0, vr10=0, vr11=0, ends={}, dxV=1, first=4, joint=1, share=1, nrelu00=EACH, nrelu01=EACH, nrelu10=EACH, nrelu11=EACH, cut00=(256,) * 4, cut01=(256,) * 4, cut10=(256,) * 4, cut11=(256,) * 4, rows=(4, 8, 12, 14, 15, 16), slack=0.2)

SCRATCH = {
    "yt": ("sbuf", [128, NI], "bfloat16"), "x0": ("sbuf", [128, 2 * L, 32], "bfloat16"), "xf": ("sbuf", [128, R], "float32"),
    "rep0": ("sbuf", [128, 2 * L, XW], "bfloat16"), "xr": ("sbuf", [128, 2 * L, XW], "bfloat16"), "m16": ("sbuf", [128, 16], "bfloat16"),
    "am": ("sbuf", [128, 48], "float32"), "hm": ("sbuf", [128, L, 4], "int32"), "hf": ("sbuf", [128, L, 4], "float32"),
    "lh": ("sbuf", [128, 8], "int32"), "lob": ("sbuf", [128, 8], "float32"), "hab": ("sbuf", [128, 2, L - 1, 4], "int32"),
    "hl": ("sbuf", [128, 48], "uint16"), "hr": ("sbuf", [128, 48], "uint16"), "mk": ("sbuf", [128, L * 128], "bfloat16"),
    "pi": ("sbuf", [128, 8], "int32"), "pj": ("sbuf", [128, 24], "int32"), "col": ("sbuf", [128, 16], "float32"),
    "ctab": ("sbuf", [128, 160], "float32"), "gtab": ("sbuf", [128, 128], "float32"), "t2": ("sbuf", [128, 64], "float32"),
    "e0": ("sbuf", [128, 128], "float32"), "qt": ("sbuf", [128, 512], "bfloat16"), "qw": ("sbuf", [128, 512], "bfloat16"),
    "bo": ("sbuf", [128, 128], "bfloat16"), "bos": ("sbuf", [128, 128], "bfloat16"), "bw": ("sbuf", [128, 6, 128], "bfloat16"),
    "i4": ("sbuf", [128, 128], "float32"), "z1t": ("sbuf", [128, 160], "bfloat16"),
    "rl": ("sbuf", [128, 18], "uint16"), "ri": ("sbuf", [128, 18], "float32"), "huge": ("sbuf", [128, 128], "bfloat16"),
    "idb": ("sbuf", [128, 128], "bfloat16"), "idn": ("sbuf", [128, 128], "bfloat16"),
    "c1": ("sbuf", [128, 128], "bfloat16"), "c2": ("sbuf", [128, 64], "bfloat16"), "zero": ("sbuf", [128, 128], "bfloat16"),
    "zs": ("sbuf", [128, 160], "bfloat16"), "zr": ("sbuf", [128, 160], "bfloat16"), "zd": ("sbuf", [128, 160], "bfloat16"),
    "seg": ("sbuf", [128, 64], "float32"), "sgp": ("sbuf", [128, 64], "float32"), "sgn": ("sbuf", [128, 64], "float32"),
    "ks": ("sbuf", [128, 2, 18 * 256], "float32"), "sgz": ("sbuf", [128, 64], "float32"),
    "Z": ("psum", [128, 512], "float32"), "X": ("psum", [128, 512], "float32"),
}
for _k in range(1, 8): SCRATCH["h%d" % _k] = ("sbuf", [128, L - 1, 8], "int32")
for _p in range(2):
    SCRATCH["win%d" % _p] = ("sbuf", [128, WL * L], "float32")
    SCRATCH["as%d" % _p] = ("sbuf", [128, 32 * 64], "bfloat16")
    SCRATCH["ar%d" % _p] = ("sbuf", [128, 32 * 64], "bfloat16")
    SCRATCH["dv%d" % _p] = ("sbuf", [128, 32 * 64], "bfloat16")
    SCRATCH["rv%d" % _p] = ("sbuf", [128, 32 * 64], "bfloat16")
    SCRATCH["wo%d" % _p] = ("sbuf", [128, 4 * L], "uint16")
    SCRATCH["dx%d" % _p] = ("sbuf", [128, 128], "bfloat16")
    SCRATCH["rh%d" % _p] = ("sbuf", [128, 128], "float16")
    SCRATCH["z%d" % _p] = ("sbuf", [128, 64], "float16")
    for _u in range(2): SCRATCH["K%d%d" % (_p, _u)] = ("psum", [128, 512], "float32")
    SCRATCH["R%d" % _p] = ("psum", [128, 512], "float32")
for _s in range(3):
    SCRATCH["ls%d" % _s] = ("sbuf", [128, 128], "float32")
    SCRATCH["sc%d" % _s] = ("sbuf", [128, 8], "float32")
    SCRATCH["ofv%d" % _s] = ("sbuf", [128, 128], "uint16")
    SCRATCH["ofs%d" % _s] = ("sbuf", [128, 128], "uint16")
    SCRATCH["pn%d" % _s] = ("sbuf", [128, 256], "float16")
    SCRATCH["pa%d" % _s] = ("sbuf", [128, 256], "float32")

LOADS = ["y", "lo", "hi", "x", "home", "ha", "hb"]
SEMAPHORES = (["cV", "cS", "cT", "cG", "snt", "st"] + ["ld_" + k for k in LOADS]
              + ["arr%d_%d" % (p, l) for p in range(2) for l in range(L - 1)])


FOLDS = []
SEMAPHORES += ["f%s%d" % (x, k) for x in "ab" for k in range(len(FOLDS))]
SCRATCH["land"] = ("sbuf", [128, max(1, len(FOLDS)), 1024], "bfloat16")
SCRATCH["zw"] = ("sbuf", [128, 1024], "bfloat16")


def helper(core, T, topo):
    return [c for c in topo.cores_of(core) if T.rank_of(c) is None and topo.die(c) == topo.die(core)][0]


def hand_back(g, core, T, topo, owner):
    rid, pid, _ = topo.addr(owner)
    for k, (p, l, u) in enumerate(FOLDS):
        g.wait_ge(T.sem["fa%d" % k], len(topo.engines(owner, core)))
        g.remote_dma(T["rv%d" % p][:, 1024 * u:1024 * u + 1024], T.land[:, k, :], T.sem["fb%d" % k], T.sem.snt, pid, rid, topo.mask(core, owner))
    g.wait_ge(T.sem.snt, len(FOLDS) * len(topo.engines(core, owner)))


def build(g, core, T, topo, rank):
    ops = []; ctx = [("setup", 0, 0, 0)]; lv = [(-1, 0)]
    last_w, readers = {}, {}
    GE, CY, PE = COST["GE"], COST["CY"], COST["PE"]

    def add(q, dur, fn, r=(), w=(), n=1, sem=None, val=0, lat=0.0, grp=None):
        i = len(ops); deps = set()
        for t in r:
            if t in last_w: deps.add(last_w[t])
        for t in w:
            if t in last_w: deps.add(last_w[t])
            deps.update(k for k in readers.get(t, ()) if k != i)
        for t in r: readers.setdefault(t, []).append(i)
        for t in w: last_w[t] = i; readers[t] = []
        ops.append(dict(q=q, dur=dur, fn=fn, deps=sorted(deps), n=n, sem=sem, val=val, lat=lat, grp=grp, tag=ctx[0], lv=lv[0]))
        return i

    V, S, G, TE, SY = g.vector, g.scalar, g, g.tensor, g.sync
    sv = lambda n, c=1.0: COST["FIX"] + max(64, n * c) * CY

    def ts(out, in0, s1, s2, o0, o1, r, w, n, c=1.0):
        if o1 is None: add("V", sv(n, c), lambda: V.tensor_scalar(out, in0, s1, None, o0), r, w)
        else: add("V", sv(n, c), lambda: V.tensor_scalar(out, in0, s1, s2, o0, o1), r, w)
    def tt(out, a, b, op, r, w, n, c=2.0, gather=False):
        add("V", 0.05 + n * GE if gather else sv(n, c), lambda: V.tensor_tensor(out, a, b, op), r, w)
    def cp(out, in_, r, w, n, c=1.0):
        add("V", sv(n, c), lambda: V.tensor_copy(out, in_), r, w)
    def ms(ap, v, w, n, r=()):
        add("V", sv(n), lambda: V.memset(ap, v), r, w)
    def scan(out, d0, d1, o1, r, w, n):
        add("V", sv(n), lambda: V.tensor_tensor_scan(out, d0, d1, 0.0, A.add, o1), r, w)
    def act(out, in_, r, w, n, bias=0.0, scale=1.0, f=F.Abs, gather=False):
        add("S", 0.065 + n * GE if gather else COST["SF"] + n * CY, lambda: S.activation(out, in_, f, bias=bias, scale=scale), r, w)
    def mms(calls, r, w, grp=None):
        def fn(last=False, first=False):
            return [TE.matmul(o, a, b, st or (first and k == 0), (last and k == len(calls) - 1) if sp is None else sp) for k, (o, a, b, n, st, sp) in enumerate(calls)]
        add("T", sum(max(64, c[3]) for c in calls) * PE, fn, r, w, n=len(calls), grp=grp)

    def load(q, key, out, in_, lat):
        eng = SY if q == "SY" else S
        ctx[0] = ("setup", 0, 0, len(ops) * 1e-3 - 1)
        add(q, 0.1, lambda: eng.dma_start(out, in_), (), (key,), sem="ld_" + key, val=16, lat=lat)
    small = [("lo", T.lh[:, 0:4], T.lo0[:]), ("hi", T.lh[:, 4:8], T.hi0[:]), ("x", T.x0[:], T.xrow[:]), ("home", T.hm[:], T.home[:]),
             ("ha", T.hab[:, 0, :, :], T.ha[:]), ("hb", T.hab[:, 1, :, :], T.hb[:])]
    for k, (key, out, in_) in enumerate(small[:OPT["first"]]): load(("SY", "S")[k % 2], key, out, in_, 1.1 + 0.3 * k)
    load("SY", "y", T.yt[:], T.ytab[:], COST["YT"])
    for key, out, in_ in small[OPT["first"]:]: load("SY", key, out, in_, COST["YT"])

    ctx[0] = ("setup", 0, 0, 0)
    def iota(out, pat, cm, tok, n, fl=True):
        if fl: add("G", 0.13 + 2 * n * CY, lambda: G.iota(out, pat, 0, cm, allow_small_or_imprecise_dtypes=True), (), [tok])
        else: add("G", 0.13 + 2 * n * CY, lambda: G.iota(out, pat, 0, cm), (), [tok])
    iota(T.pi[:], [[512, 2], [128, 2], [256, 2]], 1, "pi", 8, False)
    iota(T.gtab[:], [[16, 8], [0, 16]], 0, "gtab", 128)
    iota(T.ctab[:], [[1, 160]], 0, "ctab", 160)
    iota(T.e0[:], [[0, 8], [1, 16]], 0, "e0", 128)
    iota(T.t2[:], [[0, 4], [2, 8], [0, 2]], 0, "t2", 64)
    etab = T.ctab[:, 0:64]
    ts(T.pj[:, 0:8], T.pi[:], 15, None, A.bitwise_and, None, ["pi"], ["pj0"], 8)
    ts(T.pj[:, 16:24], T.pi[:], 7, None, A.arith_shift_right, None, ["pi"], ["pj1"], 8)
    ts(T.pj[:, 8:9], T.pi[:, 0:1], 112, None, A.bitwise_and, None, ["pi"], ["pj2"], 1)
    ts(T.pj[:, 9:10], T.pi[:, 0:1], 14, None, A.bitwise_and, None, ["pi"], ["pj3"], 1)
    cp(T.hr[:, 0:8], T.pj[:, 0:8], ["pj0"], ["hr0"], 8)
    cp(T.hl[:, 0:8], T.pj[:, 16:24], ["pj1"], ["hl0"], 8)
    f16, g16, f14, pp, ab = [T.col[:, k:k + 1] for k in range(5)]
    cp(T.col[:, 0:3], T.pj[:, 7:10], ["pj0", "pj2", "pj3"], ["f16", "g16"], 3)
    cp(pp, T.pi[:, 0:1], ["pi"], ["pp"], 1)
    ts(ab, f16, 2.0, 1.0 / 64, A.is_lt, A.mult, ["f16"], ["ab"], 1)
    ts(T.col[:, 5:6], f16, 0.0, -1.0, A.is_equal, A.mult, ["f16"], ["a0"], 1)
    ts(T.col[:, 6:10], T.ctab[:, 0:64:16], ab, T.col[:, 5:6], A.mult, A.add, ["ctab", "ab", "a0"], ["a64"], 4)
    def table(nm, src, tok, c, ctok, v, n=128, sl=slice(None)):
        ts(T[nm][:, sl], T[src][:, sl], c, v, A.is_equal, A.mult, [src, ctok], [tok], n)
    table("bos", "gtab", "bosA", g16, "g16", -1.0, 64, slice(0, 128, 2))
    table("bos", "gtab", "bosB", g16, "g16", 1.0, 64, slice(1, 128, 2))
    act(T.bo[:], T.bos[:], ["bosA", "bosB"], ["bo"], 128)
    for par in range(2):
        act(T.bw[:, par, :], T.bos[:], ["bosA", "bosB"], ["bw%d" % par], 128, scale=2.0 * par - 1, f=F.Relu)
        act(T.bw[:, 2 + par, :], T.bos[:], ["bosA", "bosB"], ["bw%d" % (2 + par)], 128, scale=(2.0 * par - 1) / 64, f=F.Relu)
        ts(T.bw[:, 4 + par, :], T.bos[:], (1 - 2.0 * par) / 64, 0.0, A.mult, A.min, ["bosA", "bosB"], ["bw%d" % (4 + par)], 128, 0.5)
    ts(T.idb[:], T.ctab[:, 0:128], pp, None, A.is_equal, None, ["ctab", "pp"], ["idb"], 128)
    ts(T.z1t[:], T.ctab[:], g16, 15.0, A.subtract, A.is_equal, ["ctab", "g16"], ["z1t"], 160)
    for nm, src, v, n in (("zs", "z1t", 64.0, 160), ("zr", "z1t", 128.0, 160), ("zd", "z1t", -64.0, 160), ("idn", "idb", -1.0, 128), ("i4", "idb", 4.0, 128)):
        act(T[nm][:], T[src][:], [src], [nm], n, scale=v, f=F.Identity)
    for c in range(4):
        q = T.qt[:, 128 * c:128 * c + 128]
        act(q, T.e0[:], ["e0", "ab", "a64"], ["qt%d" % c], 128, bias=T.col[:, 6 + c:7 + c], scale=ab, f=F.Identity)
        tt(T.qw[:, 128 * c:128 * c + 128], q, T.bo[:], A.mult, ["qt%d" % c, "bo"], ["qw%d" % c], 128, 1.0)
    QWT = ["qw%d" % c for c in range(4)]
    ts(T.c1[:, 64:128], T.t2[:], f14, -OFF, A.not_equal, A.mult, ["t2", "f16"], ["c1b"], 64)
    act(T.c1[:, 0:64], T.c1[:, 64:128], ["c1b"], ["c1a"], 64, scale=2048.0 / OFF - 1, bias=2048.0, f=F.Identity)
    def fill(out, v, src, r, w, n): act(out, src, r, w, n, scale=0.0, bias=v, f=F.Identity)
    fill(T.c2[:], -DL, T.gtab[:, 0:64], ["gtab"], ["c2"], 64)
    fill(T.zero[:], -30.0, T.gtab[:], ["gtab"], ["zero"], 128)
    fill(T.huge[:], 1.5 * 2 ** 29, T.gtab[:], ["gtab"], ["huge"], 128)
    act(T.ri[:], T.ctab[:, 0:18], ["ctab"], ["ri"], 18, f=F.Sign)
    ts(T.rl[:], T.ri[:], 16.0, f16, A.mult, A.add, ["ri", "f16"], ["rl"], 18)
    ts(T.m16[:], T.ctab[:, 0:16], f16, None, A.is_equal, None, ["ctab", "f16"], ["m16"], 16)
    ms(T.ks[:, :, 63:18 * 256:64], 1.0, ["fin0"], 144)
    for k, (row, v) in list(enumerate(STEPS))[::-1]:
        fill(T.ks[:, :, 256 * row + 63:256 * row + 256:64], v, T.x0[:, 0:2, 0:4], ["x", "fin0"] + ([] if k else ["fin.%d" % m for m in range(1, len(STEPS))]), ["fin.%d" % k if k else "fin"], 8)
    ms(T.seg[:], -1.0, ["seg0"], 64)
    ms(T.seg[:, 0:1], BIG, ["seg"], 1, ["seg0"])
    ts(T.sgp[:], T.e0[:, 0:64], 0.0, BIG, A.is_equal, A.mult, ["e0"], ["sgp"], 64)
    act(T.sgn[:], T.sgp[:], ["sgp"], ["sgn"], 64, scale=-1.0, f=F.Identity)
    ms(T.sgz[:], 0.0, ["sgz0"], 64)
    ms(T.sgz[:, 0:64:2], -BIG, ["sgz"], 32, ["sgz0"])

    ts(T.lob[:], T.lh[:], -2048.0, None, A.add, None, ["lo", "hi"], ["lob"], 8)
    for k in range(2): cp(T.hf[:, :, 2 * k:2 * k + 2], T.hm[:, :, k:4:2], ["home"], ["hf%d" % k], 12)
    HF = ["hf0", "hf1"]
    def masks(l, tok):
        act(T.mk[:, 128 * l:128 * l + 128], T.m16[:].indirect(T.hr[:, 8 * l:8 * l + 8]), ["m16", tok], ["mk%d" % l], 128, f=F.Identity, gather=True)
    masks(0, "hr0")
    ctx[0] = ("hints", 0, 0, 0); HT = []
    for h, nm in enumerate(("ha", "hb")):
        for k in range(2):
            cp(T.h1[:, :, 4 * h + 2 * k:4 * h + 2 * k + 2], T.hab[:, h, :, k:4:2], [nm], ["h1.%d%d" % (h, k)], 10); HT.append("h1.%d%d" % (h, k))
    ts(T.h2[:], T.h1[:], 6, None, A.arith_shift_right, None, HT, ["h2"], 40)
    ts(T.h3[:], T.h1[:], 4, 3, A.arith_shift_right, A.bitwise_and, HT, ["h3"], 40)
    ts(T.h4[:], T.h1[:], float(R), 4.0 - L * WL, A.is_ge, A.mult, HT, ["h4"], 40)
    ts(T.h5[:], T.h2[:], float(WL), WL - 8.0, A.mult, A.add, ["h2"], ["h5"], 40)
    tt(T.h6[:], T.h3[:], T.h4[:], A.add, ["h3", "h4"], ["h6"], 40)
    tt(T.h2[:], T.h5[:], T.h6[:], A.add, ["h5", "h6"], ["h2"], 40)
    cp(T.hl[:, 8:48], T.h2[:], ["h2"], ["hl"], 40)
    ts(T.h7[:], T.h1[:], 15, None, A.bitwise_and, None, HT, ["h7"], 40)
    cp(T.hr[:, 8:48], T.h7[:], ["h7"], ["hr"], 40)
    for l in range(1, L):
        ctx[0] = ("mask", 0, 0, (l - 1) * PRI["mstep"]); masks(l, "hr")

    def reps0(kind, n0, n1):
        ctx[0] = (kind, 0, 0, 0); n = n1 - n0
        cp(T.rep0[:, n0:n1, 0:32], T.x0[:, n0:n1, :], ["x"], ["rep%d.16" % n0], 32 * n, 0.5)
        k = 16
        while k < CH:
            cp(T.rep0[:, n0:n1, 16 + k:16 + 2 * k], T.rep0[:, n0:n1, 16:16 + k], ["rep%d.%d" % (n0, k)], ["rep%d.%d" % (n0, 2 * k)], k * n, 0.5)
            k *= 2
    def reptok(l): return "rep%d.%d" % (2 if l else 0, CH)

    def sets(p, l): return 2 if l == 0 else p
    def against0(p, l, u): return p == 1 and (l == 0 or u in OPT["old"])
    def B1(s, k): return T["ls%d" % s][:, 16 * k + 15:16 * k + 16]
    def DD(s, k): return T["ls%d" % s][:, 64 + 16 * k + 15:64 + 16 * k + 16]

    def prep(p, l):
        s = sets(p, l); P = "%d" % p; t = "%d." % s; Rb = T["R" + P]; rh = T["rh" + P]; z = T["z" + P]; ls = T["ls%d" % s]; sc = T["sc%d" % s]
        at = 0 if l else -2 * p
        ctx[0] = ("const", p, l, at)
        mms([(Rb[:, 0:128], T.idb[:], T.c1[:], 128, True, False), (Rb[:, 0:64], T.idb[:], T.c2[:], 64, False, False)], ["idb", "c1a", "c1b", "c2"], ["R" + P])
        if l: at = PRI["wait%d" % p]
        ctx[0] = ("z", p, l, at)
        if l == 0: win, wt = T.lob[:], ["lob", "hl0"]
        else: win, wt = T["win" + P][:, 0:WL * l], ["hl"] + ["w%d.%d.%d" % (p, k, x) for k in range(l) for x in range(5)]
        tt(rh[:], win.indirect(T.hl[:, 8 * l:8 * l + 8]), T.mk[:, 128 * l:128 * l + 128], A.mult, wt + ["mk%d" % l], ["rh" + P], 128, gather=True)
        mms([(T.Z[:, h:64:2], T.bos[:], rh[:, 64 * h:64 * h + 32], 32, True, True) for h in range(2)], ["bosA", "bosB", "rh" + P], ["Z"])
        scan(z[:], T.sgz[:], T.Z[:, 0:64], A.max, ["sgz", "Z"], ["z" + P], 64)
        mms([(T.Z[:, 64 + c:192:4], T.qw[:, 128 * c:128 * c + 128], z[:, 1:64:2], 32, True, True) for c in range(4)], QWT + ["z" + P], ["Z"])
        ts(T["ofs%d" % s][:], T.Z[:, 64:192], 2048.0 - DL, None, A.add, None, ["Z"], ["ofs%d" % s], 128)
        ctx[0] = ("prep", p, l, at)
        mms([(Rb[:, o:o - o % 2 + 64:2], T.bw[:, 2 * m + par, :], rh[:, 64 * h + par:64 * h + 64:2], 32, False, par + h + m == 4)
             for par in range(2) for h in range(2) for m, o in enumerate((h, 64 + h, 65 - h))], ["bw%d" % m for m in range(6)] + ["rh" + P, "R" + P], ["R" + P])
        scan(ls[:, 0:64], T.sgp[:], Rb[:, 0:64], A.min, ["sgp", "R" + P], [t + "B"], 64)
        scan(ls[:, 64:128], T.sgn[:], Rb[:, 64:128], A.max, ["sgn", "R" + P], [t + "D"], 64)
        for u in range(2):
            ctx[0] = ("prep", p, l, at + u * PRI["lsS"])
            ts(T["ofv%d" % s][:, 64 * u:64 * u + 64], etab, DD(s, 2 + u), B1(s, 2 + u), A.mult, A.add, ["ctab", t + "B", t + "D"], ["ofv%d.%d" % (s, u)], 64)
        ctx[0] = ("pen", p, l, p * PRI["pen1"] if l else -6)
        for q in ([p] if l else [0, 1]):
            o = T.ks[:, q, 10 * 256 + 63:12 * 256:64]
            if OPT["cV"]: cp(o, ls[:, 15:128:16], [t + "B", t + "D", "fin"], ["C%d" % q], 8)
            else: act(o, ls[:, 15:128:16], [t + "B", t + "D", "fin"], ["C%d" % q], 8, f=F.Identity)
        tt(sc[:, 4:8], ls[:, 15:64:16], T.hf[:, l, :], A.subtract, [t + "B"] + HF, [t + "H"], 4)
        pa = T["pa%d" % s]
        for k in range(4):
            o = 128 * (k % 2) + 64 * (k // 2)
            act(pa[:, o:o + 64], etab, ["ctab", t + "D", t + "H"], ["pa%d.%d" % (s, k)], 64, bias=sc[:, 4 + k:5 + k], scale=DD(s, k))
        if not OPT["magic"]:
            ts(T["pn%d" % s][:], pa[:], 1.0 / 16, 1280.0 - 15.0 / 32, A.mult, A.add, ["pa%d.%d" % (s, k) for k in range(4)], ["pn%d" % s], 256)

    def fold(k, a, b, r, w):
        h = helper(core, T, topo); rid, pid, _ = topo.addr(h)
        def fn():
            G.remote_dma_fused([RemoteDMATransfer(dst_ids=[DstId(rid=rid, pnc=pid)], dma_engine_mask=topo.mask(core, h), remote_sem=T.sem["fa%d" % k],
                                                  srcs=[a, b], dsts=[T.land[:, k, :]], alu_op=2)], local_sem=T.sem.snt)
        add("G", 0.6, fn, r, w, n=0, sem="fb%d" % k, val=len(topo.engines(h, core)), lat=COST["FOLD"] + (0.0 if k else COST["FIRST"]))
    if FOLDS:
        ctx[0] = ("reps1", 0, 0, 0); ms(T.zw[:], 0.0, ["zw"], 512)

    KEYS = ["s%d" % i for i in range(16)] + ["%s%d" % (x, h) for x in "dr" for h in range(0, 16, OPT["part"])] + ["p"]

    def search(p, l, u):
        ctx[0] = ("search", p, l, u); s = sets(p, l)
        K = T["K%d%d" % (p, u)]; kt = lambda x: "K%d%d.%s" % (p, u, x); grp = (p, l, u)
        xt = "x" if p == 0 else "xr%d.%d" % (l, u); o1 = 2 * l + u
        if not OPT["magic"]:
            mms([(K[:, o:o + 64], T.i64[:], T["pn%d" % s][:, 128 * u + o:128 * u + o + 64], 64, False, None) for o in (0, 64)], ["i64", "pn%d" % s], [kt("p")], grp)
        else: mms([(K[:, 0:128], T.idb[:], T.zero[:], 128, True, False)], ["idb", "zero"], [kt(q) for q in KEYS] + [kt("0")])
        if OPT["magic"]: mms([(K[:, 0:128], T.i4[:], T["pa%d" % s][:, 128 * u:128 * u + 128], 512, False, False), (K[:, 0:128], T.idb[:], T.huge[:], 128, False, False),
             (K[:, 0:128], T.idn[:], T.huge[:], 128, False, None)], ["i4", "idb", "idn", "huge", "pa%d.%d" % (s, u), "pa%d.%d" % (s, 2 + u), kt("0")], [kt("p")], grp)
        nv = OPT["ends"].get((p, l), OPT["vr%d%d" % (p, u)]); b = T["as%d" % p]
        for i in range(16):
            ctx[0] = ("search", p, l, u + i / 16)
            r = 16 * u + i; o = b[:, 64 * r:64 * r + 64]
            y, x = T.yt[:].indirect(T["ofs%d" % s][:, 4 * r:4 * r + 4]), T["xr" if p else "x0"][:, o1, i:i + 1]
            if i < nv:
                add("V", 0.05 + 64 * GE, lambda o=o, y=y, x=x: V.tensor_scalar(o, y, x, None, A.subtract), ["y", "ofs%d" % s, xt], ["as%d.%d" % (p, r)])
                if i == nv - 1:
                    ar = T["ar%d" % p]; a0 = 1024 * u; at = ["as%d.%d" % (p, 16 * u + j) for j in range(nv)]
                    ts(ar[:, a0:a0 + 64 * nv], b[:, a0:a0 + 64 * nv], 0.0, None, A.max, None, at, ["ar%d.%d" % (p, u)], 64 * nv, 0.5)
                    mms([(K[:, 0:64], T[z][:, 15 - j:143 - j], q[:, a0 + 64 * j:a0 + 64 * j + 64], 64, False, None) for z, q in (("zd", b), ("zr", ar)) for j in range(nv)],
                        ["zd", "zr", kt("0"), "ar%d.%d" % (p, u)] + at, [kt("s%d" % j) for j in range(nv)], grp)
                continue
            act(o, y, ["y", "ofs%d" % s, xt], ["as%d.%d" % (p, r)], 64, bias=x, scale=-1.0, gather=True)
            if i + 1 in OPT["rows"]:
                js = range(max([nv] + [q for q in OPT["rows"] if q <= i]), i + 1)
                mms([(K[:, 0:64], T.zs[:, 15 - j:143 - j], b[:, 64 * (16 * u + j):64 * (16 * u + j + 1)], 64, False, None) for j in js],
                    ["zs", kt("0")] + ["as%d.%d" % (p, 16 * u + j) for j in js], [kt("s%d" % j) for j in js], grp)
                if i < 12: ops[-1]["slack"] = OPT["slack"]
        shared = OPT["share"] and p == 1 and l == 0
        pd = 0 if shared else p
        dv, rv = T["dv%d" % pd], T["rv%d" % p]; d0 = 1024 * u; nr = OPT["nrelu%d%d" % (p, u)]
        rep = T["xr" if p else "rep0"][:, o1, 16:XW]
        REP = reptok(l); rt = REP if p == 0 else xt + "w"
        old = against0(p, l, u); m = OPT["xg"]
        if old:
            bank = "R%d" % u if shared else "X"; Rb = T[bank]
            mms([(Rb[:, 0:m], T.idb[:], T.xr[:, o1, 16:16 + m], m, True, False), (Rb[:, 0:m], T.idn[:], T.rep0[:, o1, 16:16 + m], m, False, True)], ["idb", "idn", xt, REP], [bank])
        tok = lambda kind, q, a, b: ["%sv%d.%d" % (kind, q, m) for m in range(a, b, 128)]
        d = e = d0
        for n in ((CH,) * 4 if l == 0 else OPT["cut%d%d" % (p, u)]):
            ctx[0] = ("search", p, l, PRI["vs"] * d / 1024 - PRI["v"]); f = d + n
            if not shared:
                tt(dv[:, d:f], T.yt[:].indirect(T["ofv%d" % s][:, d // 16:f // 16]), T["xr" if p and not old else "rep0"][:, o1, 16:16 + n], A.subtract,
                   ["y", "ofv%d.%d" % (s, u), REP if old else xt if p and n <= m else rt], tok("d", p, d, f), n, gather=True)
            ctx[0] = ("search", p, l, PRI["relu"] + PRI["vs"] * d / 1024 - PRI["v"])
            if old:
                for q in range(d, f, m): tt(rv[:, q:q + m], dv[:, q:q + m], Rb[:, 0:m], A.max, tok("d", pd, q, q + m) + [bank], tok("r", 1, q, q + m), m, 1.0)
            elif f - d0 in nr:
                ts(rv[:, e:f], dv[:, e:f], 0.0, None, A.max, None, tok("d", p, e, f), tok("r", p, e, f), f - e, 0.5); e = f
            d = f
        ctx[0] = ("search", p, l, PRI["vs"] * u + PRI["mv"])
        for kind, buf, z, pb in (("d", dv, "zd", pd), ("r", rv, "zr", p)):
            for h in range(0, 16, OPT["part"]):
                mms([(K[:, 64:128], T[z][:, 15 - i:143 - i], buf[:, d0 + i:d0 + 1024:16], 64, False, None) for i in range(h, h + OPT["part"])],
                    [z, kt("0")] + tok(kind, pb, d0, d0 + 1024) + ([] if kind == "d" else [kt("d%d" % h)] + [kt("p")] * old), [kt("%s%d" % (kind, h))], grp)

    def post(p, l, us):
        ctx[0] = ("post", p, l, us[0] + p * PRI["post1"] + (1 - us[0]) * PRI["post0%d" % p]); s = sets(p, l); P = "%d" % p; w = T["win" + P]
        c0, c1 = 2 * us[0], 2 * us[-1] + 2; c = slice(c0, c1)
        for a in range(c0, c1):
            o = 6 * 256 + 64 * BLK.index(a); u = a // 2
            scan(T.ks[:, p, o:o + 64], T.seg[:], T["K%d%d" % (p, u)][:, 64 * (a % 2):64 * (a % 2) + 64], A.min, ["K%d%d.%s" % (p, u, q) for q in KEYS] + ["seg", "fin"], ["ks%d.%d" % (p, a)], 64)
        for a in range(c0, c1):
            o = 64 * BLK.index(a) + 63
            add("V", sv(8), lambda o=o, a=a: V.tensor_tensor_scan(w[:, WL * l + a:WL * l + WL - 4:4], T.ks[:, p, o:16 * 256:512], T.ks[:, p, 768 + o:18 * 256:512], T.ks[:, p, 6 * 256 + o:6 * 256 + o + 1], A.add, A.mult),
                ["ks%d.%d" % (p, a), "C%d" % p, "fin"], ["w%d.%d.%d" % (p, l, a)])

    def left(p, l, us):
        ctx[0] = ("xup" if p == 0 else "late", p, l, us[0]); P = "%d" % p; c0, c1 = 2 * us[0], 2 * us[-1] + 2
        yk = ["dx%d.%d" % (p, u) for u in us]
        wo = T["wo" + P][:, 4 * l + c0:4 * l + c1]; wk = ["wo%d.%d.%d" % (p, l, u) for u in us]
        ts(wo, T["win" + P][:, WL * l + WL - 8 + c0:WL * l + WL - 8 + c1], 2048.0, None, A.add, None, ["w%d.%d.%d" % (p, l, a) for a in range(c0, c1)], wk, 4)
        yw = T["dx" + P]; n = 16 * (c1 - c0); o = 16 * c0
        if p == 1 and (OPT["dxV"] or l == L - 1):
            for u in us:
                tt(yw[:, 32 * u:32 * u + 32], T.yt[:].indirect(T.wo1[:, 4 * l + 2 * u:4 * l + 2 * u + 2]), T.xr[:, 2 * l + u, 0:32], A.subtract, ["y", "xr%d.%d" % (l, u)] + wk, ["dx1.%d" % u], 32, gather=True)
            act(T.xf[:, 64 * l + o:64 * l + o + n], yw[:, o:o + n], yk, ["xf%d.%d" % (l, u) for u in us], n)
            return
        if p == 0 and OPT["dxA"]:
            o1 = 2 * l + us[0]
            tt(yw[:, o:o + n], T.yt[:].indirect(wo), T.x0[:, o1, :], A.subtract, ["y", "x"] + wk, yk, n, gather=True)
            if OPT["xg"]:
                m = OPT["xg"]; xt = "xr%d.%d" % (l, us[0])
                act(T.xr[:, o1, 0:16 + m], yw[:, o:o + 32].indirect(T.rl[:, 0:1 + m // 16]), ["rl"] + yk, [xt, xt + "w"], 16 + m, gather=True)
                while m < CH and not against0(1, l, us[0]):
                    cp(T.xr[:, o1, 16 + m:16 + 2 * m], T.xr[:, o1, 16:16 + m], [xt + "w"], [xt + "w"], m, 0.5); m *= 2
                return
            mms([(T.X[:, 0:32], T.idb[:], yw[:, o:o + 32], 32, True, True)] + [(T.X[:, k:k + 16], T.idb[:], yw[:, o + 16:o + 32], 16, True, True) for k in range(32, XW, 16)], ["idb"] + yk, ["X"])
            act(T.xr[:, o1, :], T.X[:, 0:XW], ["X"], ["xr%d.%d" % (l, us[0])], XW)
            return
        act(yw[:, o:o + n], T.yt[:].indirect(wo), ["y"] + wk, yk, n, f=F.Identity, gather=True)
        if p == 0:
            o1 = 2 * l + us[0]
            mms([(T.X[:, 0:XW], T.idn[:], T.rep0[:, o1, :], XW, True, False), (T.X[:, 0:32], T.idb[:], yw[:, o:o + 32], 32, False, False)]
                + [(T.X[:, k:k + 16], T.idb[:], yw[:, o + 16:o + 32], 16, False, k == XW - 16) for k in range(32, XW, 16)], ["idb", "idn", reptok(l)] + yk, ["X"])
            act(T.xr[:, o1, :], T.X[:, 0:XW], ["X"], ["xr%d.%d" % (l, us[0])], XW)
        else:
            mms([(T.X[:, 0:n], T.idb[:], yw[:, o:o + n], n, True, False)]
                + [(T.X[:, 32 * k:32 * k + 32], T.idn[:], T.xr[:, 2 * l + u, 0:32], 32, False, u == us[-1]) for k, u in enumerate(us)],
                ["idb", "idn"] + yk + ["xr%d.%d" % (l, u) for u in us], ["X"])
            act(T.xf[:, 64 * l + o:64 * l + o + n], T.X[:, 0:n], ["X"], ["xf%d.%d" % (l, u) for u in us], n)

    def send(p, l):
        ctx[0] = ("post", p, l, 0); w = T["win%d" % p]
        dst = T.cores[(rank - 1) % len(T.cores)]
        rid, pid, _ = topo.addr(dst)
        m = topo.mask(core, dst)
        def fn():
            G.remote_dma(w[:, WL * l + WL - 4:WL * l + WL], w[:, WL * l + WL - 8:WL * l + WL - 4], T.sem["arr%d_%d" % (p, l)], T.sem.snt, pid, rid, m)
        add("G", 0.6, fn, ["w%d.%d.%d" % (p, l, a) for a in range(4)], ["w%d.%d.4" % (p, l)], n=0, sem="arr%d_%d" % (p, l), val=len(topo.engines(core, dst)),
            lat=COST["REMOTE"] + (0.0 if p + l else COST["FIRST"]))

    stores = [0]
    def store(q, out, in_, r):
        stores[0] += 1; eng = SY if q == "SY" else S
        add(q, 0.1, lambda: eng.dma_start(out, in_), r, [], sem="st", val=None, lat=2.0)

    prep(1, 0)
    reps0("reps", 0, 2)
    reps0("reps1", 2, 2 * L)
    for k in range(2 * L):
        p, l = k % 2, k // 2; lv[0] = (p, l)
        if l: prep(p, l)
        for u in range(2): search(p, l, u)
        for us in [[0], [1]]: post(p, l, us)
        if l < L - 1: send(p, l)
        for us in ([[0, 1]] if p and l < L - 1 else [[0], [1]]): left(p, l, us)
        ctx[0] = ("late", p, l, 0)
        if l == L - 1:
            am = T.am[:, 24 * p:24 * p + 24]
            cp(am, T["wo%d" % p][:], ["wo%d.%d.%d" % (p, q, u) for q in range(L) for u in range(2)], ["am%d" % p], 24)
            store("SY", T.argm[:, 24 * p:24 * p + 24], am, ["am%d" % p])
        if p == 1 and l in (3, 4, 5):
            f = l if l > 3 else 0
            store("SY" if l < 5 else "S", T.xo[:, 64 * f:64 * l + 64], T.xf[:, 64 * f:64 * l + 64], ["xf%d.%d" % (q, u) for q in range(f, l + 1) for u in range(2)])
    return ops, stores


def due(tag):
    k, p, l, u = tag
    return 4 * l + 2 * p + u + PRI[k]


def plan_old(ops):
    n = len(ops); WAKE = COST["WAKE"]; LOOK = COST["LOOK"]
    succ = [[] for _ in range(n)]
    for i, o in enumerate(ops):
        for d in o["deps"]: succ[d].append(i)
    way = [0.0] * n
    for i in range(n - 1, -1, -1):
        o = ops[i]
        way[i] = o["dur"] + max([o["lat"] + WAKE + way[j] for j in succ[i]] + [o["lat"]])
    pri = [(-due(ops[i]["tag"]), way[i]) for i in range(n)]
    left = [len(o["deps"]) for o in ops]
    ready = [0.0] * n
    free = {"V": 0.0, "S": 0.0, "G": 0.0, "T": 0.0, "SY": 0.0}
    cand = {q: [] for q in free}
    for i in range(n):
        if left[i] == 0: cand[ops[i]["q"]].append(i)
    order = []
    while len(order) < n:
        t0, q = min((max(free[q], min(ready[i] for i in cand[q])), q) for q in cand if cand[q])
        i = max((i for i in cand[q] if ready[i] <= t0), key=lambda i: (pri[i], -i))
        soon = [j for j in cand[q] if t0 < ready[j] < t0 + ops[i]["dur"] - COST["TOL"] and pri[j][0] > pri[i][0] + COST["GAP"]]
        if soon:
            tr = min(ready[j] for j in soon)
            fit = [j for j in cand[q] if ready[j] <= t0 and t0 + ops[j]["dur"] <= tr + COST["TOL"]]
            if fit: i = max(fit, key=lambda i: (pri[i], -i))
            elif tr - t0 <= LOOK: i = max((j for j in soon if ready[j] == tr), key=lambda i: (pri[i], -i))
        o = ops[i]; t = max(t0, ready[i])
        cand[q].remove(i)
        fin = t + o["dur"]; free[q] = fin
        order.append(i)
        for j in succ[i]:
            same = ops[j]["q"] == q and q == "T"
            ready[j] = max(ready[j], t if same else fin + o["lat"] + WAKE + ops[j].get("slack", 0.0))
            left[j] -= 1
            if left[j] == 0: cand[ops[j]["q"]].append(j)
    return order


def place(ops, pred, succ, key, k, back):
    n = len(ops); wake = float(COST["WAKE"][k]); left = [len(p) for p in pred]; ready = [0.0] * n; start = [0.0] * n
    line = {q: [] for q in ("V", "S", "G", "T", "SY")}
    todo = sorted((key[i], i) for i in range(n) if left[i] == 0)
    while todo:
        i = todo.pop(0)[1]; o = ops[i]; d = o["d"][k]; t = ready[i]; ln = line[o["q"]]
        if back and not pred[i]: t = o["l"][k]
        j = len(ln)
        while j > 0 and ln[j - 1][1] > t: j -= 1
        while j < len(ln) and ln[j][0] < t + d - 1e-9: t = max(t, ln[j][1]); j += 1
        ln.insert(j, (t, t + d)); start[i] = t
        for j in succ[i]:
            gap = 0.0 if o["q"] == "T" and ops[j]["q"] == "T" else wake + ops[j if back else i]["l"][k]
            if t + d + gap > ready[j]: ready[j] = t + d + gap
            left[j] -= 1
            if left[j] == 0:
                e = (key[j], j); m = len(todo)
                while m > 0 and todo[m - 1] > e: m -= 1
                todo.insert(m, e)
    return start


def length(ops, order):
    out = []
    for k in range(len(COST["CY"])):
        wake = float(COST["WAKE"][k]); free = {"V": 0.0, "S": 0.0, "G": 0.0, "T": 0.0, "SY": 0.0}; seen = [0.0] * len(ops); end = 0.0
        for i in order:
            o = ops[i]; t = free[o["q"]]
            for d in o["far"]:
                if seen[d] > t: t = seen[d]
            t += o["d"][k]; free[o["q"]] = t; t += o["l"][k]; seen[i] = t + wake
            if t > end: end = t
        out.append(end)
    return out


def plan(ops):
    n = len(ops); one = np.ones(len(COST["CY"]))
    pred = [o["deps"] for o in ops]; succ = [[] for _ in range(n)]
    for i, o in enumerate(ops):
        o["d"] = [float(x) for x in o["dur"] * one]; o["l"] = [float(x) for x in o["lat"] * one]
        o["far"] = [d for d in o["deps"] if not (o["q"] == "T" and ops[d]["q"] == "T")]
        for d in o["deps"]: succ[d].append(i)
    above = []
    for o in ops:
        far = 0
        for d in o["far"]: far |= above[d]
        o["far"] = [d for d in o["far"] if not far >> d & 1]
        for d in o["deps"]: far |= above[d] | 1 << d
        above.append(far)
    rng = np.random.default_rng(OPT["seed"]); best = None
    key = [3.0 * due(o["tag"]) + 1e-4 * i for i, o in enumerate(ops)]
    for it in range(OPT["rounds"]):
        k = OPT["sets"][int(rng.integers(len(OPT["sets"])))]
        start = place(ops, pred, succ, key, k, False)
        if it % 2 == OPT["back"]:
            back = place(ops, succ, pred, [-start[i] - ops[i]["d"][k] for i in range(n)], k, True)
            start = place(ops, pred, succ, [-back[i] - ops[i]["d"][k] for i in range(n)], k, False)
        order = sorted(range(n), key=lambda i: (start[i] if i >= len(LOADS) else -1.0, i))
        score = sum(t / c for t, c in zip(length(ops, order), COST["CY"] * 30 + COST["GE"] * 25))
        if best is None or score < best[0]: best = (score, order, start)
        st = best[2]; mid = rng.random() * max(st); wide = 1.0 + 6.0 * rng.random(); size = OPT["noise"] * rng.random()
        key = [st[i] + (size * rng.standard_normal() if abs(st[i] - mid) < wide else 0.0) for i in range(n)]
    count = {}; kind = []
    for o in ops:
        lv = o["lv"]; count[lv] = count.get(lv, 0) + 1
        kind.append((lv[0], 3 if 1 <= lv[1] <= OPT["same"] else lv[1], count[lv]))
    st = best[2]; first = lambda l: min(st[i] for i in range(n) if ops[i]["lv"] == (0, l) and ops[i]["tag"][0] == "search" and ops[i]["q"] == "S")
    period = (first(4) - first(2)) / 2
    off = {kind[i]: st[i] - period * ops[i]["lv"][1] for i in range(n) if kind[i][1] == ops[i]["lv"][1]}
    kinds = sorted(off); cur = None
    for it in range(OPT["periodic"]):
        new = dict(off)
        if it:
            a = int(rng.integers(len(kinds))); d = 0.6 * rng.standard_normal()
            for m in kinds[a:a + int(rng.integers(1, 5))]: new[m] += d
        start = place(ops, pred, succ, [new[kind[i]] + period * ops[i]["lv"][1] for i in range(n)], OPT["sets"][0], False)
        order = sorted(range(n), key=lambda i: (start[i] if i >= len(LOADS) else -1.0, i))
        score = sum(t / c for t, c in zip(length(ops, order), COST["CY"] * 30 + COST["GE"] * 25))
        if cur is None or score <= cur: cur, off = score, new
        if score < best[0]: best = (score, order, start)
    return polish(ops, best[1], succ, rng)


def polish(ops, order, succ, rng):
    norm = list(COST["CY"] * 30 + COST["GE"] * 25); K = len(norm)
    def score(od): return sum(t / c for t, c in zip(length(ops, od), norm))
    cur = score(order); it = 0
    count = {}; name = []
    for o in ops:
        count[o["lv"]] = count.get(o["lv"], 0) + 1; name.append(o["lv"] + (count[o["lv"]],))
    twin = {nm: i for i, nm in enumerate(name) if nm[0] >= 0 and 1 <= nm[1] <= OPT["same"]}
    def move(od, i, j, hop, down):
        a, b = od.index(i), od.index(j); q = ops[i]["q"]
        if a > b: return None
        for _ in range(hop):
            c = b + 1 if down else a - 1
            while 0 <= c < len(od) and ops[od[c]]["q"] != q: c += 1 if down else -1
            if not len(LOADS) <= c < len(od): break
            if down: b = c
            else: a = c
        if a < len(LOADS): return None
        between = set(od[a:b + 1])
        if down: return None if any(d in between for d in succ[i]) else od[:a] + od[a + 1:b + 1] + [i] + od[b + 1:]
        return None if any(d in between for d in ops[j]["deps"]) else od[:a] + [j] + od[a:b] + od[b + 1:]
    while it < OPT["polish"]:
        k = int(rng.integers(K)); wake = float(COST["WAKE"][k])
        free = {}; prev = {}; seen = [0.0] * len(ops); why = [None] * len(ops); end = (0.0, 0)
        for i in order:
            o = ops[i]; t = free.get(o["q"], 0.0); w = (prev.get(o["q"]), True)
            for d in o["far"]:
                if seen[d] > t: t = seen[d]; w = (d, False)
            why[i] = w; t += o["d"][k]; free[o["q"]] = t; prev[o["q"]] = i; t += o["l"][k]; seen[i] = t + wake
            if t > end[0]: end = (t, i)
        pairs = []; i = end[1]
        while why[i][0] is not None:
            if why[i][1]: pairs.append((why[i][0], i))
            i = why[i][0]
        order = order[:len(LOADS)] + sorted(order[len(LOADS):], key=lambda i: seen[i] - ops[i]["l"][k] - ops[i]["d"][k])
        for m in rng.permutation(len(pairs))[:OPT["tries"]]:
            i, j = pairs[m]; it += 1
            hop, down, every = int(rng.integers(3)), rng.random() < 0.5, rng.random() < OPT["every"]
            new = order
            for s in (range(-L, L) if every else [0]):
                i2, j2 = (twin.get((name[i][0], name[i][1] + s, name[i][2])), twin.get((name[j][0], name[j][1] + s, name[j][2]))) if s else (i, j)
                if i2 is not None and j2 is not None: new = move(new, i2, j2, hop, down) or new
            if new is order: continue
            sc = score(new)
            if sc <= cur + 1e-9:
                order, cur = new, sc
                break
    return order


CACHE = {}


def rank_program(g, core, T, topo):
    rank = T.rank_of(core)
    if rank is None:
        for owner in T.cores:
            if FOLDS and helper(owner, T, topo) == core: hand_back(g, core, T, topo, owner)
        return
    ops, stores = build(g, core, T, topo, rank)
    if "order" not in CACHE: CACHE["order"] = plan(ops)
    order = CACHE["order"]
    eng = {"V": g.vector, "S": g.scalar, "G": g, "T": g.tensor, "SY": g.sync}
    csem = {"V": T.sem.cV, "S": T.sem.cS, "T": T.sem.cT, "G": T.sem.cG}
    count = {q: 0 for q in csem}
    done = {}
    seen = {q: {} for q in eng}
    first = {ops[i]["grp"]: i for i in order[::-1] if ops[i]["grp"]}
    last = {ops[i]["grp"]: i for i in order if ops[i]["grp"]}
    for i in order:
        o = ops[i]; q = o["q"]; need = {}
        for d in o["deps"]:
            if ops[d]["q"] == q and q == "T": continue
            if done[d][1] > need.get(done[d][0], (0, 0))[0]: need[done[d][0]] = done[d][1:]
        waits = sorted(nm for nm in need if seen[q].get(nm, 0) < need[nm][0])
        waits = [nm for nm in waits if not any(need[m][1].get(nm, 0) >= need[nm][0] for m in waits if m != nm)]
        for nm in waits:
            eng[q].wait_ge(T.sem[nm], need[nm][0]); seen[q][nm] = need[nm][0]
            for m, v in need[nm][1].items(): seen[q][m] = max(seen[q].get(m, 0), v)
        res = o["fn"](last[o["grp"]] == i, not OPT["magic"] and first[o["grp"]] == i) if o["grp"] else o["fn"]()
        if o["sem"] is not None:
            if q != "G": res.then_inc(T.sem[o["sem"]], 16)
            done[i] = (o["sem"], o["val"], {})
        else:
            for x in (res if q == "T" else [res]): x.then_inc(csem[q], 1)
            count[q] += o["n"]
            done[i] = ("c" + q, count[q], dict(seen[q]))
    g.sync.wait_ge(T.sem.st, 16 * stores[0])
    dst = T.cores[(rank - 1) % len(T.cores)]
    g.wait_ge(T.sem.snt, 2 * (L - 1) * len(topo.engines(core, dst)) + len(FOLDS) * len(topo.engines(core, helper(core, T, topo))))
    for q in ("V", "S", "T", "G"):
        g.sync.wait_ge(csem[q], count[q])
